import numpy as np, ml_dtypes
CORES = [8,9,10,11,12,13]
N = 6
BF = ml_dtypes.bfloat16
W, L, S, J, TB, D = 4096, 128, 32, 32, 2, 3
NE = (TB + 1) // 2 * L
def cands(u, k):
    return ((u * u >> 5)[..., None] + (2 * np.arange(J) + 1) * u[..., None] + k) & (W - 1)
def pairs(rng, n, pen):
    s = np.arange(W) % S
    kv = rng.random(W) + pen * ((s < TB) & (s % 2 == 0)); ky = rng.random(W) + pen * ((s < TB) & (s % 2 == 1))
    row = np.full(W, -1, np.int64); row[rng.permutation(np.argsort(kv)[:n])] = np.argsort(ky)[:n]
    return row
def filled(rng, lo, hi):
    return np.stack([np.stack([pairs(rng, int(W * (lo + (hi - lo) * rng.random())), 0.6) for g in range(8)]) for r in range(N)])
def pack(x, a, w):
    b = np.full((N, 8, W), -1, np.int64)
    for r in range(N):
        for g in range(8):
            v = np.flatnonzero(a[r, g] >= 0); b[(r + 1) % N, g, a[r, g, v]] = v
    return {"x": np.ascontiguousarray(x).reshape(N, 128, W).astype(np.float32).astype(BF), "pa": a.astype(np.int32), "pb": b.astype(np.int32), "wt": np.ascontiguousarray(w).reshape(N, 128, 1).astype(np.int32)}
def some(rng, m):
    us = np.flatnonzero(m)
    return int(us[int(rng.integers(0, us.size))]) if us.size else 0
def hashed(z, w, u):
    z = np.array(z); z[:2] = 0; rho = (u - int(np.sum(w * z))) & (W - 1); z[0] = rho & 255; z[1] = rho >> 8
    return z
def firststep(x, a, w, r):
    q = (r + 1) % N; v = S * np.arange(L); z = x[r][:, :, v]; u = np.sum(w[q][:, :, None] * z, axis=1) & (W - 1); c = cands(u, 0)
    col = np.take_along_axis(x[q], c.reshape(8, 1, L * J), 2).reshape(8, 16, L, J); key = np.sum(np.abs(col - z[..., None]), axis=1) * W + c
    y = np.take_along_axis(c, np.argmin(key, axis=2)[..., None], 2)[..., 0]; taken = np.zeros((8, W), bool)
    for g in range(8): taken[g, a[r, g][a[r, g] >= 0]] = True
    return y, (a[r][:, v] < 0) & ~np.take_along_axis(taken, y, 1), taken
def setup_inputs(rng):
    return pack(rng.integers(0, 256, (N, 8, 16, W)), filled(rng, 0.4, 0.85), rng.integers(1, 4096, (N, 8, 16)))
def setup_inputs_spread(rng):
    x = np.minimum(np.exp2(8 * rng.random((N, 8, 1, W))) * rng.random((N, 8, 16, W)) * 1.25, 255).astype(np.int64) * (rng.random((N, 8, 1, W)) > 0.0625)
    w = np.minimum(np.maximum(np.exp2(12 * rng.random((N, 8, 16))).astype(np.int64), 1), 4095)
    return pack(x, filled(rng, 0.05, 0.95), w)
def setup_inputs_ties(rng):
    recs = rng.integers(0, 256, (1, 8, 16, 12)); recs[..., 0] = 0; recs[..., 1] = 0; recs[:, :, 0, 1] = 1
    pick = rng.integers(0, 12, (N, 8, W)); w = rng.integers(1, 4096, (N, 8, 16)); w[:, :, 0] = 2048
    x = np.take_along_axis(np.ascontiguousarray(np.broadcast_to(recs, (N, 8, 16, 12))), pick[:, :, None, :], 3)
    return pack(x, filled(rng, 0.3, 0.9), w)
def setup_inputs_corners(rng):
    x = rng.integers(0, 256, (N, 8, 16, W)); col = rng.random((N, 8, 1, W)); x = np.where(col < 0.06, 0, np.where(col > 0.94, 255, x))
    w = rng.integers(1, 4096, (N, 8, 16)); k = rng.integers(0, 4, (N, 8, 1)); w = np.where(k == 0, 1, np.where(k == 1, 4095, w))
    off = int(rng.integers(0, 8)); a = np.full((N, 8, W), -1, np.int64); s = np.arange(W)
    for r in range(N):
        for g in range(8):
            m = (r + g + off) % 8
            if m == 1: a[r, g] = rng.permutation(W)
            elif m == 2: a[r, g] = pairs(rng, W - NE, 2.0)
            elif m == 3: a[r, g, np.delete(s, W - S)] = rng.permutation(W - 1)
            elif m == 4 or m == 5:
                v = np.flatnonzero(pairs(rng, W // 2 if m == 4 else 3 * W // 4, 0.6) >= 0); a[r, g, v] = v if m == 4 else W - 1 - v
            elif m == 6:
                a[r, g] = pairs(rng, 3 * W // 4, 2.0); rec = rng.integers(0, 256, (16, 1))
                for t in range(0, TB, 2): x[r, g][:, t::S] = rec
    tab = cands(np.arange(W), 0); starter = (s % S < TB) & (s % S % 2 == 0)
    for r in range(N):
        g = (7 - r - off) % 8; q = (r + 1) % N; w[q, g, 0] = 1; w[q, g, 1] = 256
        lanes = np.concatenate([np.arange(0, 32, 2 - r % 2), np.arange(32, 96)]); pl = np.where(lanes < 32, 97 + lanes, 128 + lanes)
        held = a[r - 1, g]; held = held[held >= 0]; held = held[held % S >= TB]; h = rng.permutation(held)[:lanes.size]
        row = np.full(W, -1, np.int64); row[h] = pl[:h.size]; fv = ~starter; fv[h] = False; fy = np.ones(W, bool); fy[96:129] = False; fy[160:224] = False
        row[rng.permutation(np.flatnonzero(fv))[:W // 2]] = rng.permutation(np.flatnonzero(fy))[:W // 2]; a[r, g] = row
        for e in range(h.size):
            k = int(lanes[e]); P = int(pl[e]); z = hashed(rng.integers(0, 256, 16), w[q, g], some(rng, np.any(tab == P, axis=1)))
            if k < 32: there = z; back = np.zeros(16, np.int64)
            else:
                kk = (k - 32) >> 1 if r % 2 == 1 else 2 * ((k - 32) >> 2)
                hit = ((tab + 97 + kk) & (W - 1)) == P; there = hashed(z, w[q, g], some(rng, np.any(hit, axis=1) & ~np.all(hit, axis=1))); back = there
            x[r, g][:, S * k] = z; x[q, g][:, P] = there; x[r, g][:, int(h[e])] = back
    for r in range(0, N, 2):
        g = (7 - r - off) % 8; y, go, taken = firststep(x, a, w, r); n = 0
        for b in range(8): n = n + int(np.unique(y[b][go[b]]).size)
        if n % 2 == 1:
            cnt = np.bincount(y[g][go[g]], minlength=W); one = np.flatnonzero(go[g] & (cnt[y[g]] == 1) & (np.arange(L) >= 96))
            fr = ~taken[g]; fr[y[g]] = False; fr[96:129] = False; fr[160:224] = False; fr = np.flatnonzero(fr)
            if one.size and fr.size: a[r, g, S * int(one[int(rng.integers(0, one.size))])] = int(fr[int(rng.integers(0, fr.size))])
    return pack(x, a, w)
def setup_inputs_ends(rng):
    kind = (7 - np.arange(8)[None, :] + N - 1 - np.arange(N)[:, None]) % 4
    w = np.where(rng.random((N, 8, 16)) < 0.5, 1, 4095); w[kind == 0] = 4095; w[kind == 3] = 1
    x = 255 * (rng.random((N, 8, 16, W)) < rng.choice(np.array([0.0, 0.25, 0.5, 0.75, 1.0]), (N, 8, 1, W))).astype(np.int64)
    pick = rng.random((N, 8, L)) < 0.25; pick[:, :, L - 1] = True; x[:, :, :, ::S] = np.where(pick[:, :, None, :], 255, x[:, :, :, ::S])
    tab = cands(np.arange(W), 0); top = np.max(tab, axis=1); pool = np.flatnonzero(top == np.max(top))
    a = np.full((N, 8, W), -1, np.int64); n = 3 * W // 8
    for r in range(N):
        for g in range(8):
            if kind[r, g] == 1:
                need = int(pool[int(rng.integers(0, pool.size))]) * 3839; i = int(rng.integers(0, 16)); o = (i + 1) % 16; w[r, g, i] = 0
                if (need - int(np.sum(w[r, g]))) & (W - 1) == 0: w[r, g, o] = 4096 - w[r, g, o]
                w[r, g, i] = (need - int(np.sum(w[r, g]))) & (W - 1)
            c = cands(np.array([255 * int(np.sum(w[r, g])) & (W - 1)]), 0)[0]; c = c[c % S != 0]
            if c.size:
                x[r, g][:, c] = 0
                if kind[r, g] == 2: x[r, g][:, int(np.max(c))] = 255
            v = rng.permutation(W); v = v[(v != 0) & (v != W - 1) & (v != W - S)][:n]; y = rng.permutation(W); y = y[(y != 0) & (y != W - 1)][:n]
            a[r, g, v] = y
            if g % 2 == 0: a[r, g, 0] = W - 1; a[r, g, W - 1] = 0
    return pack(x, a, w)
def setup_inputs_paths(rng):
    x = rng.integers(0, 256, (N, 8, 16, W)); w = rng.integers(1, 4096, (N, 8, 16)); w[:, :, 0] = 1; w[:, :, 1] = 256
    tab = cands(np.arange(W), 0); s = np.arange(W); gs = rng.permutation(8); lanes = np.argsort(rng.random((N, 8, L)), axis=-1); cnt = np.zeros((N, 8), np.int64)
    use = np.zeros((N, 8, W), bool); use[:, :, s % S < TB] = True; use[:, :, 1850:1920] = True; use[:, :, 3770:3840] = True
    for o in range(0, W, 1024): use[:, :, o + 96:o + 256] = True
    fv = [[[] for g in range(8)] for r in range(N)]; fy = [[[] for g in range(8)] for r in range(N)]; link = [[[] for g in range(8)] for r in range(N)]
    k0 = np.zeros(N, np.int64); k1 = np.zeros(N, np.int64)
    def start(r, g):
        v = S * int(lanes[r, g, cnt[r, g]]); cnt[r, g] += 1; fv[r][g].append(v)
        return v
    def spot(r, g):
        c = np.flatnonzero(~use[r, g]); p = int(c[int(rng.integers(0, c.size))]); use[r, g, p] = True
        return p
    def reach(r, g, k, v=None, u=0):
        z = rng.integers(0, 256, 16)
        for e in range(40):
            z = rng.integers(0, 256, 16)
            if v is not None: z = hashed(z, v, u)
            c = cands(np.array([int(np.sum(w[r, g] * z)) & (W - 1)]), k)[0]; c = c[~use[r, g, c]]
            if c.size:
                p = int(c[int(rng.integers(0, c.size))]); use[r, g, p] = True
                return z, p
        return z, -1
    def visit(r, g, P, rec, b):
        q = (r + 1) % N; m = np.any(tab == P, axis=1)
        if not np.any(m): return None
        z = hashed(rng.integers(0, 256, 16), w[q, g], some(rng, m)); v = start(r, g)
        if b < 0: b = spot(r, g)
        x[r, g][:, v] = z; x[q, g][:, P] = z; x[r, g][:, b] = rec; link[r][g].append((b, P))
        return z
    for r in range(N):
        q = (r + 1) % N; g = int(gs[0])
        for i in range(L):
            z, p = reach(q, g, 0)
            if p >= 0: x[r, g][:, S * i] = z; x[q, g][:, p] = z; fv[r][g].append(S * i); fy[r][g].append(p); k0[q] += 1
        g = int(gs[1]); xq = x[q, g]
        z = hashed(rng.integers(200, 256, 16), w[q, g], 4095); x[r, g][:, start(r, g)] = z; c = cands(np.array([4095]), 0)[0]
        j = 2 * int(rng.integers(1, J // 2)); xq[:, c] = 0; xq[5, c[j]] = 8; xq[5, c[j - 1]] = 8; fy[r][g].append(int(c[j])); fy[r][g].append(int(c[j - 1]))
        z = hashed(rng.integers(200, 256, 16), w[q, g], 2047); x[r, g][:, start(r, g)] = z; c = cands(np.array([2047]), 0)[0]
        xq[:, c] = 0; xq[6, c] = (int(np.sum(z)) - 4) & 15; xq[5, c[0]] = 1; fy[r][g].append(int(c[0])); k0[q] += 2
    ka = [int(k) & 31 for k in k0]
    for r in range(N):
        q = (r + 1) % N; g = int(gs[2])
        if q % 2 == 1:
            w[q, g, 2] = 0; need = (1024 + 2048 * int(rng.integers(0, 2))) * 3839
            if (need - int(np.sum(w[q, g]))) & (W - 1) == 0: w[q, g, 3] += 1 if w[q, g, 3] < 4095 else -1
            w[q, g, 2] = (need - int(np.sum(w[q, g]))) & (W - 1)
            if visit(r, g, 1024 + 97 + ka[q], np.full(16, 255, np.int64), -1) is not None:
                x[q, g][:, 3072 + 97 + ka[q]] = 0; fy[r][g].append(3072 + 97 + ka[q]); k1[q] += 1
        g = int(gs[4])
        if r % 2 == 1:
            for o in (0, 2048):
                rb, b = reach(r, g, 97 + ka[r], w[q, g], o); z, p = reach(r, g, 0)
                if b >= 0 and p >= 0 and visit(r, g, o + 97 + ka[q], rb, b) is not None:
                    fy[r][g].append(o + 194); v = start(r - 1, g); e = spot(r - 1, g)
                    x[r - 1, g][:, v] = z; x[r, g][:, p] = z; x[r - 1, g][:, e] = rb; link[r - 1][g].append((e, p)); fy[r - 1][g].append(b); k1[r] += 1
    kb = [int(k) & 31 for k in k1]
    for r in range(N):
        q = (r + 1) % N; g = int(gs[3])
        for o in (0, 2048):
            if visit(r, g, o + 97 + ka[q], hashed(rng.integers(0, 256, 16), w[q, g], o), -1) is not None: fy[r][g].append(o + 194 + kb[q])
        g = int(gs[5]); z1, p = reach(q, g, 97 + ka[q])
        if p >= 0:
            z = visit(r, g, 1024 + 194 + kb[q], z1, -1)
            if z is not None:
                z = hashed(z, w[q, g], 1024); b = spot(r, g); x[q, g][:, p] = z1; x[r, g][:, b] = z; link[r][g].append((b, p))
                x[q, g][:, 3072 + 194 + kb[q]] = np.where(z < 128, 255, 0); fy[r][g].append(3072 + 194 + kb[q])
    a = np.full((N, 8, W), -1, np.int64)
    for r in range(N):
        for g in range(8):
            mv = np.ones(W, bool); my = np.ones(W, bool); mv[np.array(fv[r][g], np.int64)] = False; my[np.array(fy[r][g], np.int64)] = False
            for v, y in link[r][g]: mv[v] = False; my[y] = False; a[r, g, v] = y
            vs = np.flatnonzero(mv); vs = np.concatenate([vs[vs % S == 0], rng.permutation(vs[vs % S != 0])[:W // 2]])
            a[r, g, vs] = rng.permutation(np.flatnonzero(my))[:vs.size]
    return pack(x, a, w)
def check_inputs(d):
    bad = []; xx = np.asarray(d["x"]).astype(np.float32)
    if not (np.min(xx) >= 0 and np.max(xx) <= 255): bad.append("range of x")
    if np.any(xx != np.floor(xx)): bad.append("x not whole")
    for k, lo, hi in (("pa", -1, W - 1), ("pb", -1, W - 1), ("wt", 1, 4095)):
        if not (np.min(d[k]) >= lo and np.max(d[k]) <= hi): bad.append("range of " + k)
    own = np.arange(W)[None, :]; off = False
    for r in range(N):
        a = np.asarray(d["pa"])[r].astype(np.int64); b = np.asarray(d["pb"])[(r + 1) % N].astype(np.int64)
        for c, e in ((a, b), (b, a)):
            if np.any((c >= 0) & (np.take_along_axis(e, np.clip(c, 0, W - 1), 1) != own)): off = True
    if off: bad.append("pa and pb not mutual")
    return bad
def reference(x, pa, pb, wt):
    X = x.astype(np.float32).astype(np.int32).reshape(N, 8, 16, W); A = pa.astype(np.int64); B = pb.astype(np.int64); w = wt.astype(np.int64).reshape(N, 8, 16, 1)
    kap = np.zeros(N, np.int64); lane = np.arange(L)
    for t in range(TB):
        q = (np.arange(N) + (1 if t % 2 == 0 else -1)) % N
        near, far = (A, B) if t % 2 == 0 else (B, A)
        v = S * lane + t; x0 = X[:, :, :, v]; z = x0; live = near[:, :, v] < 0; last = np.full((N, 8, L), -1, np.int64)
        for d in range(D):
            u = np.sum(w[q] * z, axis=2) & (W - 1)
            c = cands(u, (97 * d + kap[q])[:, None, None, None])
            col = np.take_along_axis(X[q], c.reshape(N, 8, 1, L * J), 3).reshape(N, 8, 16, L, J)
            dist = np.sum(np.abs(col - z[..., None]), axis=2)
            key = np.where(c == last[..., None], 2 ** 24, dist.astype(np.int64) * W + c)
            y = np.take_along_axis(c, np.argmin(key, axis=3)[..., None], 3)[..., 0]
            go = live & (np.take_along_axis(far[q], y, 2) < 0)
            rr, gg, ii = np.nonzero(go); low = np.full((N, 8, W), L, np.int64); np.minimum.at(low, (rr, gg, y[go]), ii)
            win = go & (np.take_along_axis(low, y, 2) == lane)
            rr, gg, ii = np.nonzero(win); yy = y[win]; qq = q[rr]; vv = S * ii + t
            X[qq, gg, :, yy] = (X[qq, gg, :, yy] + x0[rr, gg, :, ii]) >> 1
            far[qq, gg, yy] = vv; near[rr, gg, vv] = yy
            live = live & ~win; kap = np.bincount(qq, minlength=N).astype(np.int64) & 31; last = y
            p = np.maximum(np.take_along_axis(far[q], y, 2), 0)
            z = np.where(live[:, :, None, :], np.take_along_axis(X, p[:, :, None, :], 3), z)
    return {"yx": X.reshape(N, 128, W).astype(np.float32).astype(BF), "ya": A.astype(np.float32), "yb": B.astype(np.float32)}

@@ -1,0 +1,561 @@
+from concourse.mybir import dt, AluOpType, AxisListType, ActivationFunctionType
+
+A = AluOpType
+AF = ActivationFunctionType
+W, L, TB, D = 4096, 128, 2, 3
+WX = W + L
+FULL = 16777216.0
+
+SCRATCH = {
+    "X": ("sbuf", [128, WX], "bfloat16"),
+    "XR0": ("sbuf", [128, WX], "bfloat16"),
+    "XR1": ("sbuf", [128, WX], "bfloat16"),
+    "FA": ("sbuf", [128, WX], "float32"),
+    "FB": ("sbuf", [128, WX], "float32"),
+    "P8": ("sbuf", [8, W], "int32"),
+    "PA2": ("sbuf", [128, 256], "int32"),
+    "PB2": ("sbuf", [128, 256], "int32"),
+    "PA2F": ("sbuf", [128, 256], "float32"),
+    "PB2F": ("sbuf", [128, 256], "float32"),
+    "da": ("dram", [8, W], "float32"),
+    "db": ("dram", [8, W], "float32"),
+    "WTI": ("sbuf", [128, 1], "int32"),
+    "WHI": ("sbuf", [128, 1], "int32"),
+    "WLI": ("sbuf", [128, 1], "int32"),
+    "WF": ("sbuf", [128, 2], "float32"),
+    "WH": ("sbuf", [128, 128], "bfloat16"),
+    "WL": ("sbuf", [128, 128], "bfloat16"),
+    "PI": ("sbuf", [128, 1], "int32"),
+    "PMI": ("sbuf", [128, 1], "int32"),
+    "PGI": ("sbuf", [128, 1], "int32"),
+    "PF": ("sbuf", [128, 3], "float32"),
+    "CI": ("sbuf", [128, 128], "int32"),
+    "CMI": ("sbuf", [128, 128], "int32"),
+    "CGI": ("sbuf", [128, 128], "int32"),
+    "M16": ("sbuf", [128, 128], "float32"),
+    "M16M": ("sbuf", [128, 128], "float32"),
+    "BOB": ("sbuf", [128, 128], "bfloat16"),
+    "BOF": ("sbuf", [128, 128], "float32"),
+    "IDF": ("sbuf", [128, 128], "float32"),
+    "NID": ("sbuf", [128, 128], "bfloat16"),
+    "ONF": ("sbuf", [128, 128], "float32"),
+    "SEL8": ("sbuf", [128, 8], "float32"),
+    "GM8": ("sbuf", [128, 8], "bfloat16"),
+    "GMF": ("sbuf", [128, 128], "float32"),
+    "GMX": ("sbuf", [128, 128], "bfloat16"),
+    "E8": ("sbuf", [8, 128], "bfloat16"),
+    "BJ": ("sbuf", [128, 2], "float32"),
+    "BJ2": ("sbuf", [128, 2], "float32"),
+    "KB": ("sbuf", [128, 2], "float32"),
+    "KC": ("sbuf", [128, 2], "float32"),
+    "ZD0": ("sbuf", [128, 128], "float32"),
+    "RS0": ("sbuf", [128, 128], "float32"),
+    "RS": ("sbuf", [128, 128], "float32"),
+    "HALF": ("sbuf", [128, 128], "float32"),
+    "ZERO": ("sbuf", [128, 128], "float32"),
+    "PW": ("sbuf", [128, 128], "float32"),
+    "PWM": ("sbuf", [128, 128], "float32"),
+    "PWS": ("sbuf", [128, 128], "float32"),
+    "DW0": ("sbuf", [128, 8], "float32"),
+    "DW": ("sbuf", [128, 8], "float32"),
+    "ST0": ("sbuf", [128, 128], "float32"),
+    "ST1": ("sbuf", [128, 128], "float32"),
+    "LV8": ("sbuf", [8, 128], "bfloat16"),
+    "LS0": ("sbuf", [128, 128], "float32"),
+    "LS1": ("sbuf", [128, 256], "float32"),
+    "LSF": ("sbuf", [128, 128], "float32"),
+    "LL0": ("sbuf", [128, 128], "float32"),
+    "LL1": ("sbuf", [128, 256], "float32"),
+    "LLF": ("sbuf", [128, 128], "float32"),
+    "SN0": ("sbuf", [128, 128], "bfloat16"),
+    "SN1": ("sbuf", [128, 128], "bfloat16"),
+    "SS0": ("sbuf", [128, 128], "bfloat16"),
+    "SS1": ("sbuf", [128, 128], "bfloat16"),
+    "RT": ("sbuf", [128, 128], "float32"),
+    "RSC": ("sbuf", [128, 128], "float32"),
+    "RW": ("sbuf", [128, 8], "float32"),
+    "RWT": ("sbuf", [128, 8], "float32"),
+    "Z": ("sbuf", [128, 128], "bfloat16"),
+    "ZR": ("sbuf", [128, 2048], "bfloat16"),
+    "UI": ("sbuf", [128, 128], "int32"),
+    "UM": ("sbuf", [128, 128], "int32"),
+    "UF": ("sbuf", [128, 128], "float32"),
+    "SQ": ("sbuf", [128, 256], "float32"),
+    "AI": ("sbuf", [128, 256], "int32"),
+    "CC": ("sbuf", [128, 256], "int32"),
+    "CU": ("sbuf", [128, 256], "uint16"),
+    "CF": ("sbuf", [128, 256], "float32"),
+    "NQ": ("sbuf", [128, 256], "bfloat16"),
+    "DD": ("sbuf", [128, W], "bfloat16"),
+    "R0": ("sbuf", [128, 128], "float32"),
+    "R1": ("sbuf", [128, 128], "float32"),
+    "IDB": ("sbuf", [128, 128], "bfloat16"),
+    "NIB": ("sbuf", [128, 128], "bfloat16"),
+    "GS": ("sbuf", [128, 1024], "bfloat16"),
+    "MI": ("sbuf", [128, 8], "int32"),
+    "ZS": ("sbuf", [128, 128], "int32"),
+    "YE": ("sbuf", [128, 128], "float32"),
+    "YM": ("sbuf", [128, 128], "float32"),
+    "YU": ("sbuf", [128, 8], "uint16"),
+    "YD": ("sbuf", [128, 8], "float32"),
+    "EL": ("sbuf", [128, 128], "float32"),
+    "TH": ("sbuf", [128, 128], "float32"),
+    "EQ": ("sbuf", [128, 1024], "bfloat16"),
+    "XG": ("sbuf", [128, 128], "float32"),
+    "NR": ("sbuf", [128, 128], "int32"),
+    "WM": ("sbuf", [128, 128], "float32"),
+    "WS": ("sbuf", [128, 128], "float32"),
+    "SF0": ("sbuf", [128, 8], "float32"),
+    "SF": ("sbuf", [128, 8], "float32"),
+    "Y1": ("sbuf", [128, 128], "float32"),
+    "YA": ("sbuf", [128, 128], "float32"),
+    "YN": ("sbuf", [128, 128], "float32"),
+    "CT": ("sbuf", [128, 1], "float32"),
+    "KI": ("sbuf", [128, 1], "int32"),
+    "KJ": ("sbuf", [128, 1], "int32"),
+    "KF": ("sbuf", [128, 1], "float32"),
+    "PG": ("sbuf", [128, 128], "float32"),
+    "PS": ("sbuf", [128, 128], "float32"),
+    "PU": ("sbuf", [128, 8], "uint16"),
+    "pU": ("psum", [128, 512], "float32"),
+    "pK0": ("psum", [128, 512], "float32"),
+    "pK1": ("psum", [128, 512], "float32"),
+    "pYR": ("psum", [128, 512], "float32"),
+    "pYW": ("psum", [128, 512], "float32"),
+    "pWS": ("psum", [128, 512], "float32"),
+    "pC": ("psum", [128, 512], "float32"),
+    "pM": ("psum", [128, 512], "float32"),
+}
+for _t in range(TB):
+    for _d in range(D):
+        SCRATCH["MU%d%d" % (_t, _d)] = ("sbuf", [128, 136], "uint16")
+        if _d < D - 1:
+            SCRATCH["UL%d%d" % (_t, _d)] = ("sbuf", [128, 136], "uint16")
+
+REMOTE = ["L0", "S0", "X0", "U00", "U01", "S1", "L1", "X1", "U10", "U11", "LF"]
+LOCAL = ["dW", "dP8", "dX", "dPB", "dPA", "dDB", "dDA", "dFB", "dFA", "oX", "oA", "oB"]
+SEMAPHORES = ["qV", "qS", "qT", "qG"] + ["a" + n for n in REMOTE] + ["l" + n for n in REMOTE] + LOCAL
+
+
+def machine(g, core, T, topo):
+    Q = {"V": g.vector, "S": g.scalar, "T": g.tensor, "G": g, "Y": g.sync}
+    sem = {"V": "qV", "S": "qS", "T": "qT", "G": "qG"}
+    cnt = {}
+    know = {q: {} for q in Q}
+    snap = {}
+    lastw = {}
+    readers = {}
+
+    def wait(q, toks):
+        todo = []
+        for t in toks:
+            if t not in todo and know[q].get(t[0], 0) < t[1]:
+                todo.append(t)
+        keep = []
+        for t in todo:
+            covered = False
+            for o in todo:
+                if o != t and snap.get(o, {}).get(t[0], 0) >= t[1]:
+                    covered = True
+            if not covered:
+                keep.append(t)
+        for s, v in keep:
+            if know[q].get(s, 0) >= v:
+                continue
+            Q[q].wait_ge(T.sem[s], v)
+            know[q][s] = max(know[q].get(s, 0), v)
+            for a, b in snap.get((s, v), {}).items():
+                know[q][a] = max(know[q].get(a, 0), b)
+
+    def deps(q, reads, writes):
+        toks = []
+        for r in reads:
+            if r in lastw:
+                toks.append(lastw[r][0])
+        for w in writes:
+            if w in lastw and not (q == "T" and lastw[w][1] == "T"):
+                toks.append(lastw[w][0])
+            toks.extend(readers.get(w, []))
+        wait(q, toks)
+
+    def book(q, tok, reads, writes):
+        for r in reads:
+            old = [t for t in readers.get(r, []) if t[0] != tok[0]]
+            readers[r] = old + [tok]
+        for w in writes:
+            lastw[w] = (tok, q)
+            readers[w] = []
+
+    def op(q, reads, writes, *fns):
+        deps(q, reads, writes)
+        ins = None
+        for f in fns:
+            ins = f()
+        cnt[sem[q]] = cnt.get(sem[q], 0) + 1
+        ins.then_inc(T.sem[sem[q]], 1)
+        tok = (sem[q], cnt[sem[q]])
+        know_now = dict(know[q])
+        know_now[sem[q]] = tok[1]
+        snap[tok] = know_now
+        book(q, tok, reads, writes)
+
+    def dma(q, name, pairs, reads, writes):
+        deps(q, reads, writes)
+        for o, i in pairs:
+            Q[q].dma_start(o, i).then_inc(T.sem[name], 16)
+        cnt[name] = 16 * len(pairs)
+        tok = (name, cnt[name])
+        snap[tok] = dict(know[q])
+        book(q, tok, reads, writes)
+
+    def send(name, dst, out, src, reads, lands):
+        deps("G", reads, [])
+        rid, pid = topo.addr(dst)[0], topo.addr(dst)[1]
+        g.remote_dma(out_ap=out, in_ap=src, remote_sem=T.sem["a" + name], local_sem=T.sem["l" + name],
+                     pid=pid, routing_id=rid, dma_engine_mask=topo.mask(core, dst))
+        n = len(topo.engines(core, dst))
+        cnt["l" + name] = n
+        cnt["a" + name] = n
+        book("G", ("l" + name, n), reads, [])
+        lastw[lands] = (("a" + name, n), "R")
+        readers[lands] = []
+
+    def finish():
+        wait("G", [(s, n) for s, n in cnt.items()])
+
+    return op, dma, send, finish
+
+
+def rank_program(g, core, T, topo):
+    rank = T.rank_of(core)
+    if rank is None:
+        return
+    N = len(T.cores)
+    nxt, prv = T.cores[(rank + 1) % N], T.cores[(rank - 1) % N]
+    op, dma, send, finish = machine(g, core, T, topo)
+    V, S, TE = g.vector, g.scalar, g.tensor
+
+    def ts(reads, writes, out, in0, s1, o0, s2=None, o1=None):
+        if o1 is None:
+            op("V", reads, writes, lambda: V.tensor_scalar(out, in0, s1, None, o0))
+        else:
+            op("V", reads, writes, lambda: V.tensor_scalar(out, in0, s1, s2, o0, o1))
+
+    def tt(reads, writes, out, in0, in1, o):
+        op("V", reads, writes, lambda: V.tensor_tensor(out, in0, in1, o))
+
+    def cp(reads, writes, out, in_):
+        op("V", reads, writes, lambda: V.tensor_copy(out, in_))
+
+    def scan(reads, writes, out, d0, d1, init, o0, o1):
+        op("V", reads, writes, lambda: V.tensor_tensor_scan(out, d0, d1, init, o0, o1))
+
+    def act(reads, writes, out, in_, **kw):
+        op("S", reads, writes, lambda: S.activation(out, in_, AF.Copy, **kw))
+
+    def fill(writes, ap, c):
+        op("V", [], writes, lambda: V.memset(ap, c))
+
+    def mm(out, lhsT, rhs, start=True, stop=True):
+        return lambda: TE.matmul(out, lhsT, rhs, start, stop)
+
+    dma("Y", "dP8", [(T.P8[:], T.pa[:])], [], ["P8"])
+    dma("Y", "dX", [(T.X[:, 0:W], T.x[:])], [], ["X"])
+    dma("Y", "dW", [(T.WTI[:], T.wt[:])], [], ["WTI"])
+    dma("Y", "dPB", [(T.PB2[:], T.pb[:])], [], ["PB2"])
+    dma("Y", "dPA", [(T.PA2[:], T.pa[:])], [], ["PA2"])
+
+    op("G", [], ["PI"], lambda: g.iota(T.PI[:], [[0, 1]], 0, 1))
+    op("G", [], ["CI"], lambda: g.iota(T.CI[:], [[1, 128]], 0, 0))
+    for b in range(TB):
+        op("G", [], ["ST%d" % b], lambda: g.iota(T["ST%d" % b][:], [[32, 128]], b, 0,
+                                                 allow_small_or_imprecise_dtypes=True))
+    fill(["ONF"], T.ONF[:], 1.0)
+    fill(["HALF"], T.HALF[:], 0.5)
+    fill(["ZERO"], T.ZERO[:], 0.0)
+    fill(["ZSc"], T.ZS[:], 0)
+    for n in ("X", "XR0", "XR1", "FA", "FB"):
+        fill([n + "spare"], T[n][:, W:WX], 0.0)
+    ts(["PI"], ["PMI"], T.PMI[:], T.PI[:], 15, A.bitwise_and)
+    ts(["PI"], ["PGI"], T.PGI[:], T.PI[:], 4, A.logical_shift_right)
+    ts(["CI"], ["CMI"], T.CMI[:], T.CI[:], 15, A.bitwise_and)
+    ts(["CI"], ["CGI"], T.CGI[:], T.CI[:], 4, A.logical_shift_right)
+    cp(["PI"], ["PFp"], T.PF[:, 0:1], T.PI[:])
+    cp(["PMI"], ["PFm"], T.PF[:, 1:2], T.PMI[:])
+    cp(["PGI"], ["PFg"], T.PF[:, 2:3], T.PGI[:])
+    P_, PM, PGc = T.PF[:, 0:1], T.PF[:, 1:2], T.PF[:, 2:3]
+    ts(["CGI", "PFp"], ["E8"], T.E8[:], T.CGI[0:8, :], T.PF[0:8, 0:1], A.is_equal)
+    ts(["CMI", "PFm"], ["M16"], T.M16[:], T.CMI[:], PM, A.is_equal)
+    ts(["P8"], ["LV8"], T.LV8[:], T.P8[:, 0:W:32], 0.0, A.is_lt)
+    op("T", ["E8", "LV8"], ["pM"], mm(T.pM[:, 0:128], T.E8[:], T.LV8[:]))
+    ts(["CGI", "PFg"], ["BOB"], T.BOB[:], T.CGI[:], PGc, A.is_equal)
+    act(["BOB"], ["BOF"], T.BOF[:], T.BOB[:])
+    tt(["pM", "M16"], ["LS0"], T.LS0[:], T.pM[:, 0:128], T.M16[:], A.mult)
+    send("L0", nxt, T.LL0[:], T.LS0[:], ["LS0"], "LL0")
+    ts(["WTI"], ["WHI"], T.WHI[:], T.WTI[:], 4032, A.bitwise_and)
+    ts(["WTI"], ["WLI"], T.WLI[:], T.WTI[:], 63, A.bitwise_and)
+    cp(["WHI"], ["WFh"], T.WF[:, 0:1], T.WHI[:])
+    cp(["WLI"], ["WFl"], T.WF[:, 1:2], T.WLI[:])
+    act(["BOB", "WFh"], ["WH"], T.WH[:], T.BOB[:], scale=T.WF[:, 0:1])
+    act(["BOB", "WFl"], ["WL"], T.WL[:], T.BOB[:], scale=T.WF[:, 1:2])
+    ts(["PFm"], ["BJa"], T.BJ[:, 0:1], PM, 32.0, A.mult, 16.0, A.add)
+    ts(["PFm"], ["BJb"], T.BJ[:, 1:2], PM, 32.0, A.mult, 528.0, A.add)
+    tt(["BJa", "BJb"], ["BJ2"], T.BJ2[:], T.BJ[:], T.BJ[:], A.mult)
+    ts(["BJ2"], ["KB"], T.KB[:], T.BJ2[:], -1.0 / 32, A.mult, -0.4375, A.add)
+    cp(["X"], ["SN0"], T.SN0[:], T.X[:, 0:W:32])
+    send("S0", nxt, T.SS0[:], T.SN0[:], ["SN0"], "SS0")
+    send("X0", nxt, T.XR0[:, 0:W], T.X[:, 0:W], ["X"], "XR0")
+    cp(["PB2"], ["PB2F"], T.PB2F[:], T.PB2[:])
+    cp(["PA2"], ["PA2F"], T.PA2F[:], T.PA2[:])
+    dma("Y", "dDB", [(T.db[:], T.PB2F[:])], ["PB2F"], ["db"])
+    dma("Y", "dFB", [(T.FB[f:128:16, 0:W], T.db[:]) for f in range(16)], ["db"], ["FB"])
+    dma("Y", "dDA", [(T.da[:], T.PA2F[:])], ["PA2F"], ["da"])
+    dma("Y", "dFA", [(T.FA[f:128:16, 0:W], T.da[:]) for f in range(16)], ["da"], ["FA"])
+    ts(["CI", "PFp"], ["IDF"], T.IDF[:], T.CI[:], P_, A.is_equal)
+    act(["IDF"], ["IDB"], T.IDB[:], T.IDF[:])
+    act(["IDF"], ["NIB"], T.NIB[:], T.IDF[:], scale=-1.0)
+    act(["IDF"], ["NID"], T.NID[:], T.IDF[:], scale=-FULL)
+    ts(["CI", "PFg"], ["SEL8"], T.SEL8[:], T.CI[:, 0:8], PGc, A.is_equal)
+    ts(["CI", "PFg"], ["GM8"], T.GM8[:], T.CI[:, 0:8], PGc, A.is_equal, 4096.0, A.mult)
+    ts(["CMI"], ["GMF"], T.GMF[:], T.CMI[:], 15.0, A.is_equal, 4096.0, A.mult)
+    tt(["GMF", "BOF"], ["GMX"], T.GMX[:], T.GMF[:], T.BOF[:], A.mult)
+    act(["M16"], ["M16M"], T.M16M[:], T.M16[:], bias=-1.0)
+    ts(["CMI"], ["ZD0"], T.ZD0[:], T.CMI[:], 0.0, A.is_gt)
+    ts(["CMI"], ["RS0"], T.RS0[:], T.CMI[:], 0.0, A.is_equal, 1.0e8, A.mult)
+    act(["RS0"], ["RS"], T.RS[:], T.RS0[:], bias=-5.0e7)
+    scan(["HALF", "ZERO"], ["PW"], T.PW[:], T.HALF[:], T.ZERO[:], 2.0 ** 64, A.mult, A.add)
+    act(["M16"], ["pC"], T.pC[:, 0:128], T.M16[:])
+    act(["PW"], ["pC"], T.pC[:, 128:256], T.PW[:], scale=2.5)
+    tt(["PW", "M16"], ["PWM"], T.PWM[:], T.PW[:], T.M16[:], A.mult)
+    scan(["PWM", "ZD0"], ["PWS"], T.PWS[:], T.ZD0[:], T.PWM[:], 0.0, A.mult, A.add)
+    ts(["CI", "PFm"], ["DW0"], T.DW0[:], T.CI[:, 0:8], 16.0, A.mult, PM, A.add)
+    ts(["DW0"], ["DW"], T.DW[:], T.DW0[:], float(W), A.add)
+
+    M16P, THRP = T.pC[:, 0:128], T.pC[:, 128:256]
+
+    later, counted, scaled = [], [], []
+    for t in range(TB):
+        far = "FB" if t == 0 else "FA"
+        F = T[far]
+        xr = "XR%d" % t
+        XR = T[xr]
+        ss = "SS%d" % t
+        SS = T[ss]
+        ll = "LL%d" % t
+        LL = T[ll]
+        ST = T["ST%d" % t]
+        to = nxt if t == 0 else prv
+        home = prv if t == 0 else nxt
+        for d in range(D):
+            zn = ss if d == 0 else "Z"
+            Z = T[zn]
+            op("T", ["WH", "WL", zn], ["pU"], mm(T.pU[:, 0:128], T.WH[:], Z[:], True, False),
+               mm(T.pU[:, 0:128], T.WL[:], Z[:], False, True))
+
+            def rep_v(m):
+                cp([zn], ["ZR%d" % m], T.ZR[:, m:2048:16], Z[:])
+
+            for m in range(8, 16):
+                op("S", [zn], ["ZR%d" % m],
+                   lambda: S.activation(T.ZR[:, m:2048:16], Z[:], AF.Copy))
+            for m in range(0, 4):
+                rep_v(m)
+            while counted:
+                counted.pop(0)()
+            cp(["pU"], ["UI"], T.UI[:], T.pU[:, 0:128])
+            ts(["UI"], ["UM"], T.UM[:], T.UI[:], W - 1, A.bitwise_and)
+            cp(["UM"], ["UF"], T.UF[:], T.UM[:])
+            for b in range(2):
+                op("S", ["UF", "BJa", "BJb"], ["SQ%d" % b],
+                   lambda: S.activation(T.SQ[:, 128 * b:128 * b + 128], T.UF[:], AF.Square, bias=T.BJ[:, b:b + 1]))
+            for m in range(4, 8):
+                rep_v(m)
+            while scaled:
+                scaled.pop(0)()
+            first = t == 0 and d == 0
+            KN = "KB" if first else "KC"
+
+            def lists(b):
+                c = slice(128 * b, 128 * b + 128)
+                ts(["SQ%d" % b, KN], ["AI%d" % b], T.AI[:, c], T.SQ[:, c], 1.0 / 32, A.mult, T[KN][:, b:b + 1], A.add)
+                ts(["AI%d" % b], ["CC%d" % b], T.CC[:, c], T.AI[:, c], W - 1, A.bitwise_and)
+                cp(["CC%d" % b], ["CU%d" % b], T.CU[:, c], T.CC[:, c])
+
+            def places(b):
+                c = slice(128 * b, 128 * b + 128)
+                cp(["CC%d" % b], ["CF%d" % b], T.CF[:, c], T.CC[:, c])
+                if d > 0:
+                    tt(["CC%d" % b, "pYR"], ["NQ%d" % b], T.NQ[:, c], T.CC[:, c], T.pYR[:, 0:128], A.not_equal)
+                pk = T["pK%d" % b]
+                op("T", ["CF%d" % b, "IDF"], ["pK%d" % b], mm(pk[:, 0:128], T.CF[:, c], T.IDF[:], True, False))
+                if d > 0:
+                    op("T", ["NQ%d" % b, "NID"], ["pK%d" % b], mm(pk[:, 0:128], T.NQ[:, c], T.NID[:], False, False))
+
+            zr_all = ["ZR%d" % m for m in range(16)]
+
+            def gather(b, lo, hi):
+                o, e = 2048 * b + 16 * lo, 2048 * b + 16 * hi
+                rg = "DD%d_%d" % (b, lo)
+                tt(["X", "CU%d" % b] + zr_all, [rg], T.DD[:, o:e],
+                   T.X[:, 0:W].indirect(T.CU[:, 128 * b + lo:128 * b + hi]), T.ZR[:, 16 * lo:16 * hi], A.subtract)
+                op("S", [rg], [rg], lambda: S.activation(T.DD[:, o:e], T.DD[:, o:e], AF.Abs))
+                return rg
+
+            def dist(b, c, rgs, close=False):
+                pn = "pK%d" % b
+                op("T", rgs + ["GM8"], [pn], *[
+                    mm(T[pn][32 * c:32 * c + 32, m:128:16], T.DD[:, 2048 * b + 512 * c + m:2048 * b + 512 * c + 512:16],
+                       T.GM8[:], False, False) for m in range(15)])
+                if close:
+                    op("T", rgs + ["GMX"], [pn],
+                       mm(T[pn][:, 0:128], T.DD[:, 2048 * b + 15:2048 * b + 2048:16], T.GMX[:], False, True))
+
+            def gather_s(b):
+                o, e = 2048 * b + 1536, 2048 * b + 2048
+                gs = T.GS[:, 512 * b:512 * b + 512]
+                pn = "pU" if b == 0 else "pWS"
+                op("S", ["X", "CU%d" % b], ["GS%d" % b], lambda: S.activation(
+                    gs, T.X[:, 0:W].indirect(T.CU[:, 128 * b + 96:128 * b + 128]), AF.Copy))
+                rg = "DD%d_96" % b
+                return (rg, lambda: op("T", ["GS%d" % b, "IDB"], [pn], mm(T[pn][:, 0:512], T.IDB[:], gs, False, True)),
+                        lambda: op("S", [pn], [rg], lambda: S.activation(T.DD[:, o:e], T[pn][:, 0:512], AF.Abs)))
+
+            for pn in ("pU", "pWS"):
+                op("T", ["NIB"] + zr_all, [pn], mm(T[pn][:, 0:512], T.NIB[:], T.ZR[:, 1536:2048], True, False))
+            lists(0)
+            places(0)
+            rs0, sub0, abs0 = gather_s(0)
+            sub0()
+            dist(0, 0, [gather(0, 0, 32)])
+            lists(1)
+            rs1, sub1, abs1 = gather_s(1)
+            places(1)
+            sub1()
+            abs0()
+            dist(0, 3, [rs0])
+            if t == 1 and d == 0:
+                op("T", [ll, "BOF"], ["pM"], mm(T.pM[:, 0:128], T.BOF[:], LL[:, 128:256]))
+            dist(0, 1, [gather(0, 32, 64)])
+            dist(0, 2, [gather(0, 64, 96)], True)
+            abs1()
+            dist(1, 3, [rs1])
+            dist(1, 0, [gather(1, 0, 32)])
+            dist(1, 1, [gather(1, 32, 64)])
+            dist(1, 2, [gather(1, 64, 80), gather(1, 80, 96)], True)
+            if d == 0:
+                lv = LL[:, 0:128]
+                ts([ll], ["RT"], T.RT[:], lv, -1.0, A.add)
+                scan([ll, "ZD0"], ["RSC"], T.RSC[:], T.ZD0[:], lv, 0.0, A.mult, A.add)
+                tt(["RSC", "PWS"], ["RW"], T.RW[:], T.RSC[:, 15:128:16], T.PWS[:, 15:128:16], A.mult)
+                if t == 1:
+                    tt(["FA", "pM"], ["FA"], T.FA[:, 0:W:32], T.FA[:, 0:W:32], T.pM[:, 0:128], A.add)
+            while later:
+                later.pop()()
+            scan(["pK0", "RS"], ["R0"], T.R0[:], T.RS[:], T.pK0[:, 0:128], 0.0, A.max, A.min)
+            scan(["pK1", "RS"], ["R1"], T.R1[:], T.RS[:], T.pK1[:, 0:128], 0.0, A.max, A.min)
+            tt(["R0", "R1"], ["MI"], T.MI[:], T.R0[:, 15:128:16], T.R1[:, 15:128:16], A.min)
+            ts(["MI", "ZSc"], ["ZS"], T.ZS[:, 0:128:16], T.MI[:], W - 1, A.bitwise_and)
+            scan(["ZS", "ZSc", "ZD0"], ["YE"], T.YE[:], T.ZD0[:], T.ZS[:], 0.0, A.mult, A.add)
+            tt(["YE", "pC"], ["YM"], T.YM[:], T.YE[:], M16P, A.mult)
+            op("T", ["YM", "SEL8"], ["pYW"], mm(T.pYW[:, 0:8], T.YM[:], T.SEL8[:]))
+            op("T", ["YE", "IDF"], ["pYR"], mm(T.pYR[:, 0:128], T.YE[:], T.IDF[:]))
+            cp(["pYW"], ["YU"], T.YU[:], T.pYW[:, 0:8])
+            tt([far, "YU", "RT"], ["EL"], T.EL[:], F[:, 0:W].indirect(T.YU[:]), T.RT[:], A.is_lt)
+            tt(["pYW", "DW"], ["YD"], T.YD[:], T.pYW[:, 0:8], T.DW[:], A.subtract)
+            tt(["EL", "pC"], ["TH"], T.TH[:], T.EL[:], THRP, A.mult)
+            for h in (0, 7, 6, 5, 4, 3, 2, 1):
+                lo = 16 * h if h > 1 else 0
+                a, e = 128 * h + lo, 128 * h + 128
+                ts(["pYR", "pYW", "RW"], ["EQ%d" % h], T.EQ[:, a:e], T.pYR[:, lo:128], T.pYW[:, h:h + 1],
+                   A.is_equal, T.RW[:, h:h + 1], A.mult)
+                op("T", ["EQ%d" % h, "BOB"], ["pWS"], mm(T.pWS[:, lo:128], T.BOB[:], T.EQ[:, a:e], h == 0, h == 1))
+            tt(["X", "YU", ss], ["XG"], T.XG[:], T.X[:, 0:W].indirect(T.YU[:]), SS[:], A.add)
+            ts(["XG"], ["NR"], T.NR[:], T.XG[:], 0.5, A.mult, -0.25, A.add)
+            mu = "MU%d%d" % (t, d)
+            MU = T[mu]
+            if d < D - 1:
+                cp(["NR"], [mu + "r"], MU[:, 0:128], T.NR[:])
+            else:
+                ts(["pYR"], ["Y1"], T.Y1[:], T.pYR[:, 0:128], 1.0, A.add)
+            tt(["pWS", "TH"], ["WM"], T.WM[:], T.pWS[:, 0:128], T.TH[:], A.is_lt)
+            scan(["WM", "ZD0"], ["WS"], T.WS[:], T.ZD0[:], T.WM[:], 0.0, A.mult, A.add)
+            won = T.WS[:, 15:128:16]
+            tt(["WS", "YD"], ["SF0"], T.SF0[:], won, T.YD[:], A.mult)
+            tt(["SF0", "DW"], ["SF"], T.SF[:], T.SF0[:], T.DW[:], A.add)
+            cp(["SF"], [mu], MU[:, 128:136], T.SF[:])
+            sl = MU[:, 128:136]
+
+            def far_write():
+                cp([mu, "ST%d" % t, far + "spare"], [far], F[:, 0:WX].indirect(sl), ST[:])
+
+            def rec_write():
+                cp([mu, "NR", "Xspare"], ["X"], T.X[:, 0:WX].indirect(sl), T.NR[:])
+
+            def pairs(d=d, t=t):
+                if d < D - 1:
+                    ts(["pYR"], ["Y1"], T.Y1[:], T.pYR[:, 0:128], 1.0, A.add)
+                if d == 0:
+                    tt(["WM", "Y1"], ["YN"], T.YN[:], T.WM[:], T.Y1[:], A.mult)
+                    return
+                tt(["WM", "Y1"], ["YA"], T.YA[:], T.WM[:], T.Y1[:], A.mult)
+                if d < D - 1:
+                    tt(["YN", "YA"], ["YN"], T.YN[:], T.YN[:], T.YA[:], A.add)
+                elif t == 0:
+                    tt(["YN", "YA"], ["LS1n"], T.LS1[:, 128:256], T.YN[:], T.YA[:], A.add)
+                else:
+                    tt(["YN", "YA"], ["LSF"], T.LSF[:], T.YN[:], T.YA[:], A.add)
+
+            def after(d=d, won=won, pairs=pairs):
+                tt(["RT", "WM"], ["RT"], T.RT[:], T.RT[:], T.WM[:], A.subtract)
+                tt(["RW", "WS"], ["RWT"], T.RWT[:], T.RW[:], won, A.mult)
+                tt(["RW", "RWT"], ["RW"], T.RW[:], T.RW[:], T.RWT[:], A.subtract)
+                pairs()
+
+            def kappa():
+                op("V", ["WS"], ["CT"], lambda: V.tensor_reduce(T.CT[:], won, AxisListType.X, A.add))
+                op("T", ["CT", "ONF"], ["pM"], mm(T.pM[:, 0:1], T.ONF[:], T.CT[:]))
+
+            def kappa2():
+                step = 97.0 * ((d + 1) % D)
+                counted.append(lambda: cp(["pM"], ["KI"], T.KI[:], T.pM[:, 0:1]))
+                counted.append(lambda: ts(["KI"], ["KJ"], T.KJ[:], T.KI[:], 31, A.bitwise_and))
+                scaled.append(lambda: cp(["KJ"], ["KF"], T.KF[:], T.KJ[:]))
+                scaled.append(lambda: ts(["KB", "KF"], ["KC"], T.KC[:], T.KB[:], T.KF[:], A.add, step, A.add))
+
+            if d < D - 1:
+                un = "U%d%d" % (t, d)
+                ul = "UL%d%d" % (t, d)
+                send(un, to, T[ul][:], MU[:], [mu, mu + "r"], ul)
+                far_write()
+                kappa()
+                tt([far, "YU", "M16"], ["PG"], T.PG[:], F[:, 0:W].indirect(T.YU[:]), T.M16[:], A.mult)
+                scan(["PG", "ZD0"], ["PS"], T.PS[:], T.ZD0[:], T.PG[:], 0.0, A.mult, A.add)
+                kappa2()
+                cp(["PS"], ["PU"], T.PU[:], T.PS[:, 15:128:16])
+                rec_write()
+                later.append(after)
+                cp([ul, xr + "spare"], [xr], XR[:, 0:WX].indirect(T[ul][:, 128:136]), T[ul][:, 0:128])
+                cp([xr, "PU"], ["Z"], T.Z[:], XR[:, 0:W].indirect(T.PU[:]))
+            elif t == 0:
+                rec_write()
+                cp(["X"], ["SN1"], T.SN1[:], T.X[:, 1:W:32])
+                send("S1", prv, T.SS1[:], T.SN1[:], ["SN1"], "SS1")
+                kappa()
+                far_write()
+                tt(["FB", "M16M"], ["LS1l"], T.LS1[:, 0:128], T.FB[:, 1:W:32], T.M16M[:], A.is_lt)
+                kappa2()
+                pairs()
+                send("X1", prv, T.XR1[:, 0:W], T.X[:, 0:W], ["X"], "XR1")
+                send("L1", prv, T.LL1[:], T.LS1[:], ["LS1l", "LS1n"], "LL1")
+            else:
+                pairs()
+                send("LF", home, T.LLF[:], T.LSF[:], ["LSF"], "LLF")
+                rec_write()
+                dma("Y", "oX", [(T.yx[:], T.X[:, 0:W])], ["X"], ["yx"])
+                far_write()
+                dma("Y", "oA", [(T.ya[:], T.FA[0:128:16, 0:W])], ["FA"], ["ya"])
+
+    op("T", ["LLF", "BOF"], ["pM"], mm(T.pM[:, 0:128], T.BOF[:], T.LLF[:]))
+    tt(["FB", "pM"], ["FB"], T.FB[:, 1:W:32], T.FB[:, 1:W:32], T.pM[:, 0:128], A.add)
+    dma("Y", "oB", [(T.yb[:], T.FB[0:128:16, 0:W])], ["FB"], ["yb"])
+    finish()

@@ -5,135 +5,41 @@ AF = ActivationFunctionType
 W, L, TB, D = 4096, 128, 2, 3
 WX = W + L
 FULL = 16777216.0
+BIG = 8192.0
+MAGIC = 12582912.0
 
-SCRATCH = {
-    "X": ("sbuf", [128, WX], "bfloat16"),
-    "XR0": ("sbuf", [128, WX], "bfloat16"),
-    "XR1": ("sbuf", [128, WX], "bfloat16"),
-    "FA": ("sbuf", [128, WX], "float32"),
-    "FB": ("sbuf", [128, WX], "float32"),
-    "P8": ("sbuf", [8, W], "int32"),
-    "PA2": ("sbuf", [128, 256], "int32"),
-    "PB2": ("sbuf", [128, 256], "int32"),
-    "PA2F": ("sbuf", [128, 256], "float32"),
-    "PB2F": ("sbuf", [128, 256], "float32"),
-    "da": ("dram", [8, W], "float32"),
-    "db": ("dram", [8, W], "float32"),
-    "WTI": ("sbuf", [128, 1], "int32"),
-    "WHI": ("sbuf", [128, 1], "int32"),
-    "WLI": ("sbuf", [128, 1], "int32"),
-    "WF": ("sbuf", [128, 2], "float32"),
-    "WH": ("sbuf", [128, 128], "bfloat16"),
-    "WL": ("sbuf", [128, 128], "bfloat16"),
-    "PI": ("sbuf", [128, 1], "int32"),
-    "PMI": ("sbuf", [128, 1], "int32"),
-    "PGI": ("sbuf", [128, 1], "int32"),
-    "PF": ("sbuf", [128, 3], "float32"),
-    "CI": ("sbuf", [128, 128], "int32"),
-    "CMI": ("sbuf", [128, 128], "int32"),
-    "CGI": ("sbuf", [128, 128], "int32"),
-    "M16": ("sbuf", [128, 128], "float32"),
-    "M16M": ("sbuf", [128, 128], "float32"),
-    "BOB": ("sbuf", [128, 128], "bfloat16"),
-    "BOF": ("sbuf", [128, 128], "float32"),
-    "IDF": ("sbuf", [128, 128], "float32"),
-    "NID": ("sbuf", [128, 128], "bfloat16"),
-    "ONF": ("sbuf", [128, 128], "float32"),
-    "SEL8": ("sbuf", [128, 8], "float32"),
-    "GM8": ("sbuf", [128, 8], "bfloat16"),
-    "GMF": ("sbuf", [128, 128], "float32"),
-    "GMX": ("sbuf", [128, 128], "bfloat16"),
-    "E8": ("sbuf", [8, 128], "bfloat16"),
-    "BJ": ("sbuf", [128, 2], "float32"),
-    "BJ2": ("sbuf", [128, 2], "float32"),
-    "KB": ("sbuf", [128, 2], "float32"),
-    "KC": ("sbuf", [128, 2], "float32"),
-    "ZD0": ("sbuf", [128, 128], "float32"),
-    "RS0": ("sbuf", [128, 128], "float32"),
-    "RS": ("sbuf", [128, 128], "float32"),
-    "HALF": ("sbuf", [128, 128], "float32"),
-    "ZERO": ("sbuf", [128, 128], "float32"),
-    "PW": ("sbuf", [128, 128], "float32"),
-    "PWM": ("sbuf", [128, 128], "float32"),
-    "PWS": ("sbuf", [128, 128], "float32"),
-    "DW0": ("sbuf", [128, 8], "float32"),
-    "DW": ("sbuf", [128, 8], "float32"),
-    "ST0": ("sbuf", [128, 128], "float32"),
-    "ST1": ("sbuf", [128, 128], "float32"),
-    "LV8": ("sbuf", [8, 128], "bfloat16"),
-    "LS0": ("sbuf", [128, 128], "float32"),
-    "LS1": ("sbuf", [128, 256], "float32"),
-    "LSF": ("sbuf", [128, 128], "float32"),
-    "LL0": ("sbuf", [128, 128], "float32"),
-    "LL1": ("sbuf", [128, 256], "float32"),
-    "LLF": ("sbuf", [128, 128], "float32"),
-    "SN0": ("sbuf", [128, 128], "bfloat16"),
-    "SN1": ("sbuf", [128, 128], "bfloat16"),
-    "SS0": ("sbuf", [128, 128], "bfloat16"),
-    "SS1": ("sbuf", [128, 128], "bfloat16"),
-    "RT": ("sbuf", [128, 128], "float32"),
-    "RSC": ("sbuf", [128, 128], "float32"),
-    "RW": ("sbuf", [128, 8], "float32"),
-    "RWT": ("sbuf", [128, 8], "float32"),
-    "Z": ("sbuf", [128, 128], "bfloat16"),
-    "ZR": ("sbuf", [128, 2048], "bfloat16"),
-    "UI": ("sbuf", [128, 128], "int32"),
-    "UM": ("sbuf", [128, 128], "int32"),
-    "UF": ("sbuf", [128, 128], "float32"),
-    "SQ": ("sbuf", [128, 256], "float32"),
-    "AI": ("sbuf", [128, 256], "int32"),
-    "CC": ("sbuf", [128, 256], "int32"),
-    "CU": ("sbuf", [128, 256], "uint16"),
-    "CF": ("sbuf", [128, 256], "float32"),
-    "NQ": ("sbuf", [128, 256], "bfloat16"),
-    "DD": ("sbuf", [128, W], "bfloat16"),
-    "R0": ("sbuf", [128, 128], "float32"),
-    "R1": ("sbuf", [128, 128], "float32"),
-    "IDB": ("sbuf", [128, 128], "bfloat16"),
-    "NIB": ("sbuf", [128, 128], "bfloat16"),
-    "GS": ("sbuf", [128, 1024], "bfloat16"),
-    "MI": ("sbuf", [128, 8], "int32"),
-    "ZS": ("sbuf", [128, 128], "int32"),
-    "YE": ("sbuf", [128, 128], "float32"),
-    "YM": ("sbuf", [128, 128], "float32"),
-    "YU": ("sbuf", [128, 8], "uint16"),
-    "YD": ("sbuf", [128, 8], "float32"),
-    "EL": ("sbuf", [128, 128], "float32"),
-    "TH": ("sbuf", [128, 128], "float32"),
-    "EQ": ("sbuf", [128, 1024], "bfloat16"),
-    "XG": ("sbuf", [128, 128], "float32"),
-    "NR": ("sbuf", [128, 128], "int32"),
-    "WM": ("sbuf", [128, 128], "float32"),
-    "WS": ("sbuf", [128, 128], "float32"),
-    "SF0": ("sbuf", [128, 8], "float32"),
-    "SF": ("sbuf", [128, 8], "float32"),
-    "Y1": ("sbuf", [128, 128], "float32"),
-    "YA": ("sbuf", [128, 128], "float32"),
-    "YN": ("sbuf", [128, 128], "float32"),
-    "CT": ("sbuf", [128, 1], "float32"),
-    "KI": ("sbuf", [128, 1], "int32"),
-    "KJ": ("sbuf", [128, 1], "int32"),
-    "KF": ("sbuf", [128, 1], "float32"),
-    "PG": ("sbuf", [128, 128], "float32"),
-    "PS": ("sbuf", [128, 128], "float32"),
-    "PU": ("sbuf", [128, 8], "uint16"),
-    "pU": ("psum", [128, 512], "float32"),
-    "pK0": ("psum", [128, 512], "float32"),
-    "pK1": ("psum", [128, 512], "float32"),
-    "pYR": ("psum", [128, 512], "float32"),
-    "pYW": ("psum", [128, 512], "float32"),
-    "pWS": ("psum", [128, 512], "float32"),
-    "pC": ("psum", [128, 512], "float32"),
-    "pM": ("psum", [128, 512], "float32"),
-}
-for _t in range(TB):
-    for _d in range(D):
-        SCRATCH["MU%d%d" % (_t, _d)] = ("sbuf", [128, 136], "uint16")
-        if _d < D - 1:
-            SCRATCH["UL%d%d" % (_t, _d)] = ("sbuf", [128, 136], "uint16")
+F32, BF, F16, I32, U16 = "float32", "bfloat16", "float16", "int32", "uint16"
+SCRATCH = {}
+for _names, _cols, _dt in (
+        ("X XR0 XR1", WX, BF), ("FA FB", WX, F32),
+        ("PA2 PB2", 256, I32), ("PA2H PB2H", 256, F16), ("FT", 2048, F16),
+        ("WTI", 1, I32), ("WI", 2, I32), ("WF", 2, F32), ("WM", 512, BF),
+        ("PI", 2, I32), ("PX", 6, I32), ("PF", 6, F32), ("PG", 8, F32),
+        ("CI CMI CGI CI8 ZS", 128, I32), ("SLI", 64, I32),
+        ("M16 IDF BOF ONF DM ND3 CEX ST0 ST1", 128, F32), ("IL CP", 256, F32),
+        ("BOB IB NIB HI BIGI D4K DQ1 KQ", 128, BF), ("K2K ZB", 192, BF), ("GM", 16, BF), ("SEL8", 8, F32),
+        ("BO16", 128, F16), ("I16", 256, F16), ("RC", 272, F16), ("C0", 272, BF), ("RN", 144, BF),
+        ("SL", 128, F16), ("NS", 128, BF),
+        ("RSA RSA0 RA", 192, F32), ("RSB RSB0 RB", 64, F32), ("BJ0 BJ BJ2 KC", 4, F32), ("KB", 12, F32),
+        ("SN0 SN1 SS0 SS1 NH0 NH1 NL0 NL1 LT Z", 128, BF), ("NN0 NN1 NM0 NM1", 128, F32),
+        ("ZR", 1024, BF), ("KI", 64, I32), ("FR", 64, F32), ("SQ", 256, F32), ("AI CC", 256, I32), ("CU", 256, U16),
+        ("CFE", 528, F16), ("NQE", 528, BF), ("DD GS", 2048, BF), ("AB", W, BF),
+        ("MI", 8, I32), ("YE YM", 128, F16), ("YU PU", 8, U16), ("EQ", 1024, BF),
+        ("TK XG NR", 128, BF), ("NRF YRS PGR PS", 128, F32),
+        ("YP0 YP1 YP2", 128, F32), ("WX0 WX1 WX2", 128, BF), ("WD", 128, BF),
+        ("CT KF", 1, F32), ("KJ", 2, I32),
+        ("MP", 8 * TB * D, U16), ("UP", 8 * TB * D, U16), ("UR", 128 * TB * (D - 1), BF)):
+    for _n in _names.split():
+        SCRATCH[_n] = ("sbuf", [128, _cols], _dt)
+SCRATCH["P8"] = ("sbuf", [8, W], I32)
+SCRATCH["LV8"] = ("sbuf", [8, 128], BF)
+SCRATCH["E8"] = ("sbuf", [8, 128], BF)
+for _n in ("p1", "p2", "p3", "p4", "p5", "p6", "p7", "pC"):
+    SCRATCH[_n] = ("psum", [128, 512], F32)
 
-REMOTE = ["L0", "S0", "X0", "U00", "U01", "S1", "L1", "X1", "U10", "U11", "LF"]
-LOCAL = ["dW", "dP8", "dX", "dPB", "dPA", "dDB", "dDA", "dFB", "dFA", "oX", "oA", "oB"]
+REMOTE = ["S0", "X0", "L0", "S1", "X1", "L1", "N0", "N1"] + [k + "%d%d" % (t, d) for k in "RP" for t in range(TB)
+                                                             for d in range(D - 1)]
+LOCAL = ["dW", "dP8", "dX", "dPB", "dPA", "oX", "oA", "oB"]
 SEMAPHORES = ["qV", "qS", "qT", "qG"] + ["a" + n for n in REMOTE] + ["l" + n for n in REMOTE] + LOCAL
 
 
@@ -172,6 +78,8 @@ def machine(g, core, T, topo):
         for r in reads:
             if r in lastw:
                 toks.append(lastw[r][0])
+            if r[0] == "p":
+                toks.extend([t for t in readers.get(r, []) if t[0] != sem.get(q)])
         for w in writes:
             if w in lastw and not (q == "T" and lastw[w][1] == "T"):
                 toks.append(lastw[w][0])
@@ -250,312 +158,433 @@ def rank_program(g, core, T, topo):
     def scan(reads, writes, out, d0, d1, init, o0, o1):
         op("V", reads, writes, lambda: V.tensor_tensor_scan(out, d0, d1, init, o0, o1))
 
-    def act(reads, writes, out, in_, **kw):
-        op("S", reads, writes, lambda: S.activation(out, in_, AF.Copy, **kw))
+    def act(reads, writes, out, in_, func=AF.Copy, **kw):
+        op("S", reads, writes, lambda: S.activation(out, in_, func, **kw))
 
     def fill(writes, ap, c):
         op("V", [], writes, lambda: V.memset(ap, c))
 
-    def mm(out, lhsT, rhs, start=True, stop=True):
+    def iota(name, pattern, base, cm, floats=False):
+        if floats:
+            op("G", [], [name], lambda: g.iota(T[name][:], pattern, base, cm, allow_small_or_imprecise_dtypes=True))
+        else:
+            op("G", [], [name], lambda: g.iota(T[name][:], pattern, base, cm))
+
+    def mm(out, lhsT, rhs, start=False, stop=False):
         return lambda: TE.matmul(out, lhsT, rhs, start, stop)
 
-    dma("Y", "dP8", [(T.P8[:], T.pa[:])], [], ["P8"])
-    dma("Y", "dX", [(T.X[:, 0:W], T.x[:])], [], ["X"])
+    def te(reads, bank, *fns):
+        op("T", reads, [bank], *fns)
+
     dma("Y", "dW", [(T.WTI[:], T.wt[:])], [], ["WTI"])
     dma("Y", "dPB", [(T.PB2[:], T.pb[:])], [], ["PB2"])
+    dma("Y", "dX", [(T.X[:, 0:W], T.x[:])], [], ["X"])
+    dma("Y", "dP8", [(T.P8[:], T.pa[:])], [], ["P8"])
     dma("Y", "dPA", [(T.PA2[:], T.pa[:])], [], ["PA2"])
 
-    op("G", [], ["PI"], lambda: g.iota(T.PI[:], [[0, 1]], 0, 1))
-    op("G", [], ["CI"], lambda: g.iota(T.CI[:], [[1, 128]], 0, 0))
-    for b in range(TB):
-        op("G", [], ["ST%d" % b], lambda: g.iota(T["ST%d" % b][:], [[32, 128]], b, 0,
-                                                 allow_small_or_imprecise_dtypes=True))
-    fill(["ONF"], T.ONF[:], 1.0)
-    fill(["HALF"], T.HALF[:], 0.5)
-    fill(["ZERO"], T.ZERO[:], 0.0)
+    iota("PI", [[1, 2]], 0, 1)
+    iota("CI", [[1, 128]], 0, 0)
+    iota("BJ0", [[256, 4]], 16, 0, True)
+    iota("SLI", [[-16, 8], [-1, 8]], 0, 1)
+    iota("RSA0", [[0, 8], [1, 24]], 0, 0, True)
+    iota("RSB0", [[0, 8], [1, 8]], 0, 0, True)
+    iota("ST0", [[32, 128]], 0, 0, True)
+    iota("ST1", [[32, 128]], 1, 0, True)
+    fill(["EQ%d" % h for h in range(8)], T.EQ[:], 0.0)
+    fill(["NQE"], T.NQE[:], 0.0)
     fill(["ZSc"], T.ZS[:], 0)
-    for n in ("X", "XR0", "XR1", "FA", "FB"):
-        fill([n + "spare"], T[n][:, W:WX], 0.0)
-    ts(["PI"], ["PMI"], T.PMI[:], T.PI[:], 15, A.bitwise_and)
-    ts(["PI"], ["PGI"], T.PGI[:], T.PI[:], 4, A.logical_shift_right)
+    p = T.PI[:, 0:1]
+    cp(["PI"], ["PX0"], T.PX[:, 0:1], p)
+    ts(["PI"], ["PX1"], T.PX[:, 1:2], p, 15, A.bitwise_and)
+    ts(["PI"], ["PX2"], T.PX[:, 2:3], p, 4, A.logical_shift_right)
+    ts(["PI"], ["PX3"], T.PX[:, 3:4], p, 7, A.bitwise_and)
+    ts(["PI"], ["PX4"], T.PX[:, 4:5], p, 3, A.logical_shift_right, 1, A.bitwise_and)
+    ts(["PI"], ["PX5"], T.PX[:, 5:6], T.PI[:, 1:2], 15, A.bitwise_and)
     ts(["CI"], ["CMI"], T.CMI[:], T.CI[:], 15, A.bitwise_and)
+    cp(["PX%d" % k for k in range(6)], ["PF"], T.PF[:], T.PX[:])
     ts(["CI"], ["CGI"], T.CGI[:], T.CI[:], 4, A.logical_shift_right)
-    cp(["PI"], ["PFp"], T.PF[:, 0:1], T.PI[:])
-    cp(["PMI"], ["PFm"], T.PF[:, 1:2], T.PMI[:])
-    cp(["PGI"], ["PFg"], T.PF[:, 2:3], T.PGI[:])
-    P_, PM, PGc = T.PF[:, 0:1], T.PF[:, 1:2], T.PF[:, 2:3]
-    ts(["CGI", "PFp"], ["E8"], T.E8[:], T.CGI[0:8, :], T.PF[0:8, 0:1], A.is_equal)
-    ts(["CMI", "PFm"], ["M16"], T.M16[:], T.CMI[:], PM, A.is_equal)
-    ts(["P8"], ["LV8"], T.LV8[:], T.P8[:, 0:W:32], 0.0, A.is_lt)
-    op("T", ["E8", "LV8"], ["pM"], mm(T.pM[:, 0:128], T.E8[:], T.LV8[:]))
-    ts(["CGI", "PFg"], ["BOB"], T.BOB[:], T.CGI[:], PGc, A.is_equal)
-    act(["BOB"], ["BOF"], T.BOF[:], T.BOB[:])
-    tt(["pM", "M16"], ["LS0"], T.LS0[:], T.pM[:, 0:128], T.M16[:], A.mult)
-    send("L0", nxt, T.LL0[:], T.LS0[:], ["LS0"], "LL0")
-    ts(["WTI"], ["WHI"], T.WHI[:], T.WTI[:], 4032, A.bitwise_and)
-    ts(["WTI"], ["WLI"], T.WLI[:], T.WTI[:], 63, A.bitwise_and)
-    cp(["WHI"], ["WFh"], T.WF[:, 0:1], T.WHI[:])
-    cp(["WLI"], ["WFl"], T.WF[:, 1:2], T.WLI[:])
-    act(["BOB", "WFh"], ["WH"], T.WH[:], T.BOB[:], scale=T.WF[:, 0:1])
-    act(["BOB", "WFl"], ["WL"], T.WL[:], T.BOB[:], scale=T.WF[:, 1:2])
-    ts(["PFm"], ["BJa"], T.BJ[:, 0:1], PM, 32.0, A.mult, 16.0, A.add)
-    ts(["PFm"], ["BJb"], T.BJ[:, 1:2], PM, 32.0, A.mult, 528.0, A.add)
-    tt(["BJa", "BJb"], ["BJ2"], T.BJ2[:], T.BJ[:], T.BJ[:], A.mult)
-    ts(["BJ2"], ["KB"], T.KB[:], T.BJ2[:], -1.0 / 32, A.mult, -0.4375, A.add)
+    ts(["CI"], ["CI8"], T.CI8[:], T.CI[:], 3, A.logical_shift_right)
+    P_, PM, PGc, PJ, PL, PM1 = [T.PF[:, k:k + 1] for k in range(6)]
+    ts(["CMI", "PF"], ["M16"], T.M16[:], T.CMI[:], PM, A.is_equal)
+    ts(["CGI", "PF"], ["BO16"], T.BO16[:], T.CGI[:], PGc, A.is_equal)
+    ts(["CI", "PF"], ["IDF"], T.IDF[:], T.CI[:], P_, A.is_equal)
+    ts(["PB2"], ["PB2H"], T.PB2H[:], T.PB2[:], -2047.0, A.add)
+    for k in range(16):
+        ts(["BO16", "M16"], ["FT%d" % k], T.FT[:, 128 * k:128 * k + 128], T.BO16[:], T.M16[:, k:k + 1], A.mult)
+
+    def table(name, c, bank, on):
+        src = T["P" + name[1] + "2H"]
+        te(["P" + name[1] + "2H", "FT%d" % (2 * c), "FT%d" % (2 * c + 1)], bank, *[
+            mm(T[bank][:, 256 * e:256 * e + 256], T.FT[:, 128 * (2 * c + e):128 * (2 * c + e + 1)], src[:], True, True)
+            for e in range(2)])
+        out = T[name][:, 512 * c:512 * c + 512]
+        if on == "S":
+            act([bank], [name + str(c)], out, T[bank][:, 0:512], bias=2047.0)
+        else:
+            ts([bank], [name + str(c)], out, T[bank][:, 0:512], 2047.0, A.add)
+
+    def whole(name):
+        return [name + str(c) for c in range(8)]
+
+    for c in range(8):
+        table("FB", c, ("p2", "p3", "p4", "p5")[c % 4], "S")
+    for k, (src, a, b) in enumerate(((PGc, 2.0, 0.0), (PGc, 2.0, 1.0), (PJ, 32.0, 0.0), (P_, 1.0, float(W)),
+                                     (P_, -3.0, -3.0 * W), (P_, 1.0, 1.0), (PL, -1.0, 1.0))):
+        ts(["PF"], ["PG%d" % k], T.PG[:, k:k + 1], src, a, A.mult, b, A.add)
+    ts(["PF"], ["PG7"], T.PG[:, 7:8], PM, 15.0, A.is_lt, BIG, A.mult)
+    ts(["WTI"], ["WI0"], T.WI[:, 0:1], T.WTI[:], 4032, A.bitwise_and)
+    ts(["WTI"], ["WI1"], T.WI[:, 1:2], T.WTI[:], 63, A.bitwise_and)
+    ts(["BJ0", "PG2"], ["BJ"], T.BJ[:], T.BJ0[:], T.PG[:, 2:3], A.add)
+    ts(["WI0", "WI1"], ["WF"], T.WF[:], T.WI[:], 1.0 / W, A.mult)
+    tt(["BJ"], ["BJ2"], T.BJ2[:], T.BJ[:], T.BJ[:], A.mult)
+    for k in range(4):
+        ts(["CI8", "PG%d" % (k // 2), "WF"], ["WM%d" % k], T.WM[:, 128 * k:128 * k + 128], T.CI8[:],
+           T.PG[:, k // 2:k // 2 + 1], A.is_equal, T.WF[:, k % 2:k % 2 + 1], A.mult)
+    for d in range(D):
+        ts(["BJ2"], ["KB%d" % d], T.KB[:, 4 * d:4 * d + 4], T.BJ2[:], -1.0 / 32, A.mult, 97.0 * d - 0.4375, A.add)
     cp(["X"], ["SN0"], T.SN0[:], T.X[:, 0:W:32])
     send("S0", nxt, T.SS0[:], T.SN0[:], ["SN0"], "SS0")
     send("X0", nxt, T.XR0[:, 0:W], T.X[:, 0:W], ["X"], "XR0")
-    cp(["PB2"], ["PB2F"], T.PB2F[:], T.PB2[:])
-    cp(["PA2"], ["PA2F"], T.PA2F[:], T.PA2[:])
-    dma("Y", "dDB", [(T.db[:], T.PB2F[:])], ["PB2F"], ["db"])
-    dma("Y", "dFB", [(T.FB[f:128:16, 0:W], T.db[:]) for f in range(16)], ["db"], ["FB"])
-    dma("Y", "dDA", [(T.da[:], T.PA2F[:])], ["PA2F"], ["da"])
-    dma("Y", "dFA", [(T.FA[f:128:16, 0:W], T.da[:]) for f in range(16)], ["da"], ["FA"])
-    ts(["CI", "PFp"], ["IDF"], T.IDF[:], T.CI[:], P_, A.is_equal)
-    act(["IDF"], ["IDB"], T.IDB[:], T.IDF[:])
-    act(["IDF"], ["NIB"], T.NIB[:], T.IDF[:], scale=-1.0)
-    act(["IDF"], ["NID"], T.NID[:], T.IDF[:], scale=-FULL)
-    ts(["CI", "PFg"], ["SEL8"], T.SEL8[:], T.CI[:, 0:8], PGc, A.is_equal)
-    ts(["CI", "PFg"], ["GM8"], T.GM8[:], T.CI[:, 0:8], PGc, A.is_equal, 4096.0, A.mult)
-    ts(["CMI"], ["GMF"], T.GMF[:], T.CMI[:], 15.0, A.is_equal, 4096.0, A.mult)
-    tt(["GMF", "BOF"], ["GMX"], T.GMX[:], T.GMF[:], T.BOF[:], A.mult)
-    act(["M16"], ["M16M"], T.M16M[:], T.M16[:], bias=-1.0)
-    ts(["CMI"], ["ZD0"], T.ZD0[:], T.CMI[:], 0.0, A.is_gt)
-    ts(["CMI"], ["RS0"], T.RS0[:], T.CMI[:], 0.0, A.is_equal, 1.0e8, A.mult)
-    act(["RS0"], ["RS"], T.RS[:], T.RS0[:], bias=-5.0e7)
-    scan(["HALF", "ZERO"], ["PW"], T.PW[:], T.HALF[:], T.ZERO[:], 2.0 ** 64, A.mult, A.add)
-    act(["M16"], ["pC"], T.pC[:, 0:128], T.M16[:])
-    act(["PW"], ["pC"], T.pC[:, 128:256], T.PW[:], scale=2.5)
-    tt(["PW", "M16"], ["PWM"], T.PWM[:], T.PW[:], T.M16[:], A.mult)
-    scan(["PWM", "ZD0"], ["PWS"], T.PWS[:], T.ZD0[:], T.PWM[:], 0.0, A.mult, A.add)
-    ts(["CI", "PFm"], ["DW0"], T.DW0[:], T.CI[:, 0:8], 16.0, A.mult, PM, A.add)
-    ts(["DW0"], ["DW"], T.DW[:], T.DW0[:], float(W), A.add)
+    for name, scale in (("IB", 1.0), ("NIB", -1.0), ("HI", 0.5), ("BIGI", BIG), ("D4K", float(W))):
+        act(["IDF"], [name], T[name][:], T.IDF[:], scale=scale)
+    fill(["K2K"], T.K2K[:], 2048.0)
+    fill(["ZB"], T.ZB[:], 0.0)
+    fill(["KQ"], T.KQ[:], -0.25)
+    fill(["ONF"], T.ONF[:], 1.0)
+    fill(["C0z"], T.C0[:], 0.0)
+    fill(["RNz"], T.RN[:, 128:136], 0.0)
+    for n in ("X", "XR0", "XR1", "FA", "FB"):
+        fill([n + "spare"], T[n][:, W:WX], 0.0)
+    cp(["EQ0"], ["CFE"], T.CFE[:], T.EQ[:, 0:528])
+    ts(["CI", "PF"], ["SEL8"], T.SEL8[:], T.CI[:, 0:8], PGc, A.is_equal)
+    ts(["CI", "PF"], ["GMa"], T.GM[:, 0:8], T.CI[:, 0:8], PGc, A.is_equal, float(W), A.mult)
+    ts(["CI", "PF"], ["GMb"], T.GM[:, 8:16], T.CI[:, 0:8], PGc, A.is_equal, -float(W), A.mult)
+    for e in range(2):
+        ts(["SLI"], ["SL%d" % e], T.SL[:, 64 * e:64 * e + 64], T.SLI[:], 8.0 * e, A.is_equal)
+        ts(["SLI"], ["NS%d" % e], T.NS[:, 64 * e:64 * e + 64], T.SLI[:], 8.0 * e, A.is_equal, -FULL, A.mult)
+    ts(["CGI", "PF"], ["BOB"], T.BOB[:], T.CGI[:], PGc, A.is_equal)
+    ts(["CGI", "PF"], ["E8"], T.E8[:], T.CGI[0:8, :], T.PF[0:8, 0:1], A.is_equal)
+    ts(["P8"], ["LV8"], T.LV8[:], T.P8[:, 0:W:32], 0.0, A.is_ge)
+    te(["E8", "LV8"], "p7", mm(T.p7[:, 0:128], T.LV8[:], T.E8[:], True, True))
+    for e in range(2):
+        cp(["IDF"], ["I16%d" % e], T.I16[:, 128 * e:128 * e + 128], T.IDF[:])
+    cp(["EQ0"], ["RCa"], T.RC[:, 0:128], T.EQ[:, 0:128])
+    ts(["BO16"], ["RCb"], T.RC[:, 128:256], T.BO16[:], -1.0, A.mult)
+    tt(["p7", "M16"], ["NH0"], T.NH0[:], T.p7[:, 0:128], T.M16[:], A.mult)
+    send("L0", nxt, T.NL0[:], T.NH0[:], ["NH0"], "NL0")
+    cp(["SEL8"], ["RCc"], T.RC[:, 256:264], T.SEL8[:])
+    cp(["SEL8"], ["RCd"], T.RC[:, 264:272], T.SEL8[:])
+    ts(["CMI", "PF", "C0z"], ["C0"], T.C0[:, 128:256], T.CMI[:], PM, A.is_le, BIG, A.mult)
+    ts(["CMI", "PF"], ["CPA"], T.CP[:, 0:128], T.CMI[:], PM, A.is_equal, 4 * BIG, A.mult)
+    ts(["CMI", "PF"], ["CPB"], T.CP[:, 128:256], T.CMI[:], PM1, A.is_equal, -BIG, A.mult)
+    ts(["CMI"], ["CEX"], T.CEX[:], T.CMI[:], 1.0e6, A.mult, -2048.0, A.add)
+    ts(["PA2"], ["PA2H"], T.PA2H[:], T.PA2[:], -2047.0, A.add)
+    tt(["CPA", "CPB"], ["pC"], T.pC[:, 256:384], T.CP[:, 0:128], T.CP[:, 128:256], A.add)
+    M16P, TWON, CPK, TFREE = [T.pC[:, 128 * k:128 * k + 128] for k in range(4)]
 
-    M16P, THRP = T.pC[:, 0:128], T.pC[:, 128:256]
+    def late_constants():
+        act(["RSA0"], ["RSA"], T.RSA[:], T.RSA0[:], scale=-1.0e8, bias=5.0e7)
+        act(["RSB0"], ["RSB"], T.RSB[:], T.RSB0[:], scale=-1.0e8, bias=5.0e7)
+        act(["M16"], ["pC"], M16P, T.M16[:])
+        act(["M16"], ["pC"], TWON, T.M16[:], scale=W + 1.0, bias=-1.0)
+        act(["M16"], ["pC"], TFREE, T.M16[:], scale=-BIG - 0.5, bias=BIG)
+        act(["BOB"], ["RNa"], T.RN[:, 0:128], T.BOB[:], scale=BIG)
+        act(["SEL8"], ["RNb"], T.RN[:, 136:144], T.SEL8[:], scale=BIG)
+        act(["M16", "PG3"], ["DM"], T.DM[:], T.M16[:], scale=T.PG[:, 3:4])
+        act(["M16", "PG4"], ["ND3"], T.ND3[:], T.M16[:], scale=T.PG[:, 4:5])
+        act(["IDF", "PG5"], ["DQ1"], T.DQ1[:], T.IDF[:], scale=T.PG[:, 5:6])
+        act(["IDF", "PG6"], ["IL0"], T.IL[:, 0:128], T.IDF[:], scale=T.PG[:, 6:7])
+        act(["IDF", "PF"], ["IL1"], T.IL[:, 128:256], T.IDF[:], scale=PL)
+        act(["BOB"], ["BOF"], T.BOF[:], T.BOB[:])
 
-    later, counted, scaled = [], [], []
+    late_constants()
+    RC_ALL = ["RCa", "RCb", "RCc", "RCd"]
+    RN_ALL = ["RNa", "RNz", "RNb"]
+    zr_all = ["ZR%d" % m for m in range(8)]
+    fa_left = list(range(8))
+
+    def fa_piece(bank):
+        if fa_left:
+            table("FA", fa_left.pop(0), bank, "S")
+
     for t in range(TB):
         far = "FB" if t == 0 else "FA"
         F = T[far]
-        xr = "XR%d" % t
+        xr, ss, nl, st = "XR%d" % t, "SS%d" % t, "NL%d" % t, "ST%d" % t
         XR = T[xr]
-        ss = "SS%d" % t
-        SS = T[ss]
-        ll = "LL%d" % t
-        LL = T[ll]
-        ST = T["ST%d" % t]
         to = nxt if t == 0 else prv
         home = prv if t == 0 else nxt
         for d in range(D):
             zn = ss if d == 0 else "Z"
             Z = T[zn]
-            op("T", ["WH", "WL", zn], ["pU"], mm(T.pU[:, 0:128], T.WH[:], Z[:], True, False),
-               mm(T.pU[:, 0:128], T.WL[:], Z[:], False, True))
-
-            def rep_v(m):
-                cp([zn], ["ZR%d" % m], T.ZR[:, m:2048:16], Z[:])
-
-            for m in range(8, 16):
-                op("S", [zn], ["ZR%d" % m],
-                   lambda: S.activation(T.ZR[:, m:2048:16], Z[:], AF.Copy))
-            for m in range(0, 4):
-                rep_v(m)
-            while counted:
-                counted.pop(0)()
-            cp(["pU"], ["UI"], T.UI[:], T.pU[:, 0:128])
-            ts(["UI"], ["UM"], T.UM[:], T.UI[:], W - 1, A.bitwise_and)
-            cp(["UM"], ["UF"], T.UF[:], T.UM[:])
-            for b in range(2):
-                op("S", ["UF", "BJa", "BJb"], ["SQ%d" % b],
-                   lambda: S.activation(T.SQ[:, 128 * b:128 * b + 128], T.UF[:], AF.Square, bias=T.BJ[:, b:b + 1]))
-            for m in range(4, 8):
-                rep_v(m)
-            while scaled:
-                scaled.pop(0)()
             first = t == 0 and d == 0
-            KN = "KB" if first else "KC"
+            kn, KN = ("KB0", T.KB) if first else ("KC", T.KC)
+            stopped = [nl] + ["WX%d" % e for e in range(d)]
 
-            def lists(b):
-                c = slice(128 * b, 128 * b + 128)
-                ts(["SQ%d" % b, KN], ["AI%d" % b], T.AI[:, c], T.SQ[:, c], 1.0 / 32, A.mult, T[KN][:, b:b + 1], A.add)
-                ts(["AI%d" % b], ["CC%d" % b], T.CC[:, c], T.AI[:, c], W - 1, A.bitwise_and)
-                cp(["CC%d" % b], ["CU%d" % b], T.CU[:, c], T.CC[:, c])
+            te(["WM%d" % k for k in range(4)] + [zn], "p1", *[
+                mm(T.p1[:, 0:64], T.WM[:, 128 * k:128 * k + 128], Z[:, k // 2:128:2], k == 0, k == 3) for k in range(4)])
 
-            def places(b):
-                c = slice(128 * b, 128 * b + 128)
-                cp(["CC%d" % b], ["CF%d" % b], T.CF[:, c], T.CC[:, c])
-                if d > 0:
-                    tt(["CC%d" % b, "pYR"], ["NQ%d" % b], T.NQ[:, c], T.CC[:, c], T.pYR[:, 0:128], A.not_equal)
-                pk = T["pK%d" % b]
-                op("T", ["CF%d" % b, "IDF"], ["pK%d" % b], mm(pk[:, 0:128], T.CF[:, c], T.IDF[:], True, False))
-                if d > 0:
-                    op("T", ["NQ%d" % b, "NID"], ["pK%d" % b], mm(pk[:, 0:128], T.NQ[:, c], T.NID[:], False, False))
+            def rep(m):
+                cp([zn], ["ZR%d" % m], T.ZR[:, m:1024:8], Z[:])
 
-            zr_all = ["ZR%d" % m for m in range(16)]
+            for m in range(0, 3):
+                rep(m)
+            ts(["p1"], ["KI"], T.KI[:], T.p1[:, 0:64], -0.5, A.add)
+            rep(3)
+            tt(["p1", "KI"], ["FR"], T.FR[:], T.p1[:, 0:64], T.KI[:], A.subtract)
+            for b in range(4):
+                act(["FR", "BJ"], ["SQ%d" % b], T.SQ[:, 64 * b:64 * b + 64], T.FR[:], AF.Square, scale=float(W),
+                    bias=T.BJ[:, b:b + 1])
+            for m in range(4, 8):
+                rep(m)
 
-            def gather(b, lo, hi):
-                o, e = 2048 * b + 16 * lo, 2048 * b + 16 * hi
-                rg = "DD%d_%d" % (b, lo)
-                tt(["X", "CU%d" % b] + zr_all, [rg], T.DD[:, o:e],
-                   T.X[:, 0:W].indirect(T.CU[:, 128 * b + lo:128 * b + hi]), T.ZR[:, 16 * lo:16 * hi], A.subtract)
-                op("S", [rg], [rg], lambda: S.activation(T.DD[:, o:e], T.DD[:, o:e], AF.Abs))
-                return rg
+            def whole_part(b):
+                c = slice(64 * b, 64 * b + 64)
+                ts(["SQ%d" % b, kn], ["AI%d" % b], T.AI[:, c], T.SQ[:, c], 1.0 / 32, A.mult, KN[:, b:b + 1], A.add)
 
-            def dist(b, c, rgs, close=False):
-                pn = "pK%d" % b
-                op("T", rgs + ["GM8"], [pn], *[
-                    mm(T[pn][32 * c:32 * c + 32, m:128:16], T.DD[:, 2048 * b + 512 * c + m:2048 * b + 512 * c + 512:16],
-                       T.GM8[:], False, False) for m in range(15)])
-                if close:
-                    op("T", rgs + ["GMX"], [pn],
-                       mm(T[pn][:, 0:128], T.DD[:, 2048 * b + 15:2048 * b + 2048:16], T.GMX[:], False, True))
+            def modulo(lo, hi):
+                ts(["AI%d" % b for b in range(lo, hi)], ["CC%d" % b for b in range(lo, hi)], T.CC[:, 64 * lo:64 * hi],
+                   T.AI[:, 64 * lo:64 * hi], W - 1, A.bitwise_and)
+
+            def offsets(lo, hi):
+                cp(["CC%d" % b for b in range(lo, hi)], ["CU%d" % b for b in range(lo, hi)], T.CU[:, 64 * lo:64 * hi],
+                   T.CC[:, 64 * lo:64 * hi])
+
+            def keys(b, lo, hi, j):
+                if b < 3:
+                    return T.p4[lo:hi, 3 * j + b:192:24]
+                return T.p5[lo:hi, j:64:8]
+
+            def kbank(b):
+                return "p4" if b < 3 else "p5"
+
+            def sbank(b):
+                return "p2" if b % 2 == 0 else "p3"
+
+            def gather_v(b, lo, hi):
+                tt(["X", "CU%d" % b] + zr_all, ["DD%d_%d" % (b, lo)], T.DD[:, 512 * b + 8 * lo:512 * b + 8 * hi],
+                   T.X[:, 0:W].indirect(T.CU[:, 64 * b + lo // 2:64 * b + hi // 2]), T.ZR[:, 8 * lo:8 * hi], A.subtract)
+
+            def relu_v(b, lo, hi):
+                ts(["DD%d_%d" % (b, lo)], ["AB%d_%d" % (b, lo)], T.AB[:, 1024 * b + 8 * lo:1024 * b + 8 * hi],
+                   T.DD[:, 512 * b + 8 * lo:512 * b + 8 * hi], 0.0, A.max, 2.0, A.mult)
+
+            def minus_d(b, lo, hi):
+                te(["DD%d_%d" % (b, lo), "GMb"], kbank(b), *[
+                    mm(keys(b, lo, hi, j), T.DD[:, 512 * b + 8 * lo + j:512 * b + 8 * hi:8], T.GM[:, 8:16])
+                    for j in range(8)])
+
+            def plus_abs(b, lo, hi, parts):
+                te(["AB%d_%d" % (b, e) for e in parts] + ["GMa"], kbank(b), *[
+                    mm(keys(b, lo, hi, j), T.AB[:, 1024 * b + 8 * lo + j:1024 * b + 8 * hi:8], T.GM[:, 0:8])
+                    for j in range(8)])
+
+            def minus_z(b):
+                te(["NIB"] + zr_all, sbank(b), mm(T[sbank(b)][:, 0:512], T.NIB[:], T.ZR[:, 512:1024], True, False))
 
             def gather_s(b):
-                o, e = 2048 * b + 1536, 2048 * b + 2048
-                gs = T.GS[:, 512 * b:512 * b + 512]
-                pn = "pU" if b == 0 else "pWS"
-                op("S", ["X", "CU%d" % b], ["GS%d" % b], lambda: S.activation(
-                    gs, T.X[:, 0:W].indirect(T.CU[:, 128 * b + 96:128 * b + 128]), AF.Copy))
-                rg = "DD%d_96" % b
-                return (rg, lambda: op("T", ["GS%d" % b, "IDB"], [pn], mm(T[pn][:, 0:512], T.IDB[:], gs, False, True)),
-                        lambda: op("S", [pn], [rg], lambda: S.activation(T.DD[:, o:e], T[pn][:, 0:512], AF.Abs)))
+                act(["X", "CU%d" % b], ["GS%d" % b], T.GS[:, 512 * b:512 * b + 512],
+                    T.X[:, 0:W].indirect(T.CU[:, 64 * b + 32:64 * b + 64]))
 
-            for pn in ("pU", "pWS"):
-                op("T", ["NIB"] + zr_all, [pn], mm(T[pn][:, 0:512], T.NIB[:], T.ZR[:, 1536:2048], True, False))
-            lists(0)
-            places(0)
-            rs0, sub0, abs0 = gather_s(0)
-            sub0()
-            dist(0, 0, [gather(0, 0, 32)])
-            lists(1)
-            rs1, sub1, abs1 = gather_s(1)
-            places(1)
-            sub1()
-            abs0()
-            dist(0, 3, [rs0])
+            def plus_x(b):
+                te(["GS%d" % b, "IB"], sbank(b),
+                   mm(T[sbank(b)][:, 0:512], T.IB[:], T.GS[:, 512 * b:512 * b + 512], False, True))
+
+            def abs_s(b, lo, hi):
+                act([sbank(b)], ["AB%d_%d" % (b, lo)], T.AB[:, 1024 * b + 8 * lo:1024 * b + 8 * hi],
+                    T[sbank(b)][:, 8 * (lo - 64):8 * (hi - 64)], AF.Abs)
+
+            def spread(src, sel, names, b, stop=False):
+                out = T.p4[:, b:192:3] if b < 3 else T.p5[:, 0:64]
+                te(names, kbank(b), *[
+                    mm(out, src[:, 2 - e + 128 * b:130 - e + 128 * b], sel[:, 64 * e:64 * e + 64], False, stop and e == 1)
+                    for e in range(2)])
+
+            def barred(b):
+                tt(["CC%d" % b, "p6"], ["NQE%d" % b], T.NQE[:, 2 + 128 * b:130 + 128 * b:2], T.CC[:, 64 * b:64 * b + 64],
+                   T.p6[:, 0:64], A.not_equal)
+                spread(T.NQE, T.NS, ["NQE", "NQE%d" % b, "NS0", "NS1"], b)
+
+            te(["IB", "K2K"], "p4", mm(T.p4[:, 0:192], T.IB[:], T.K2K[:], True, False))
+            te(["IB", "K2K"], "p5", mm(T.p5[:, 0:64], T.IB[:], T.K2K[:, 0:64], True, False))
+            minus_z(0)
+            minus_z(1)
+            whole_part(0)
+            whole_part(1)
+            modulo(0, 1)
+            whole_part(2)
+            offsets(0, 1)
+            gather_s(0)
+            whole_part(3)
+            modulo(1, 4)
+            plus_x(0)
+            if d > 0:
+                barred(0)
+            offsets(1, 4)
+            gather_s(1)
+            gather_v(0, 0, 64)
+            abs_s(0, 64, 128)
+            minus_d(0, 0, 64)
+            plus_x(1)
+            minus_z(2)
+            gather_s(2)
+            gather_v(1, 0, 64)
+            relu_v(0, 0, 64)
+            abs_s(1, 64, 128)
+            minus_d(1, 0, 64)
+            plus_abs(0, 0, 128, [0, 64])
+            plus_x(2)
+            minus_z(3)
+            gather_s(3)
+            ts(["CU%d" % b for b in range(4)], ["CFE"], T.CFE[:, 2:514:2], T.CU[:], -2048.0, A.add)
+            gather_v(2, 0, 64)
+            relu_v(1, 0, 64)
+            abs_s(2, 64, 128)
+            minus_d(2, 0, 64)
+            plus_abs(1, 0, 128, [0, 64])
+            plus_x(3)
+            if d > 0:
+                for b in range(1, 4):
+                    barred(b)
+            gather_v(3, 0, 32)
+            relu_v(2, 0, 64)
+            abs_s(3, 64, 96)
+            abs_s(3, 96, 128)
+            minus_d(3, 0, 32)
+            plus_abs(2, 0, 128, [0, 64])
+            for b in range(3):
+                spread(T.CFE, T.SL, ["CFE", "SL0", "SL1"], b)
+            te(["ZB"], "p4", mm(T.p4[:, 0:192], T.ZB[:, 0:128], T.ZB[:], False, True))
+            gather_v(3, 32, 64)
+            relu_v(3, 0, 32)
+            plus_abs(3, 64, 96, [64])
+            minus_d(3, 32, 64)
+            relu_v(3, 32, 64)
+            plus_abs(3, 0, 32, [0])
+            plus_abs(3, 96, 128, [96])
+            plus_abs(3, 32, 64, [32])
+            spread(T.CFE, T.SL, ["CFE", "SL0", "SL1"], 3, True)
+            scan(["p4", "RSA"], ["RA"], T.RA[:], T.RSA[:], T.p4[:, 0:192], 0.0, A.max, A.min)
             if t == 1 and d == 0:
-                op("T", [ll, "BOF"], ["pM"], mm(T.pM[:, 0:128], T.BOF[:], LL[:, 128:256]))
-            dist(0, 1, [gather(0, 32, 64)])
-            dist(0, 2, [gather(0, 64, 96)], True)
-            abs1()
-            dist(1, 3, [rs1])
-            dist(1, 0, [gather(1, 0, 32)])
-            dist(1, 1, [gather(1, 32, 64)])
-            dist(1, 2, [gather(1, 64, 80), gather(1, 80, 96)], True)
-            if d == 0:
-                lv = LL[:, 0:128]
-                ts([ll], ["RT"], T.RT[:], lv, -1.0, A.add)
-                scan([ll, "ZD0"], ["RSC"], T.RSC[:], T.ZD0[:], lv, 0.0, A.mult, A.add)
-                tt(["RSC", "PWS"], ["RW"], T.RW[:], T.RSC[:, 15:128:16], T.PWS[:, 15:128:16], A.mult)
-                if t == 1:
-                    tt(["FA", "pM"], ["FA"], T.FA[:, 0:W:32], T.FA[:, 0:W:32], T.pM[:, 0:128], A.add)
-            while later:
-                later.pop()()
-            scan(["pK0", "RS"], ["R0"], T.R0[:], T.RS[:], T.pK0[:, 0:128], 0.0, A.max, A.min)
-            scan(["pK1", "RS"], ["R1"], T.R1[:], T.RS[:], T.pK1[:, 0:128], 0.0, A.max, A.min)
-            tt(["R0", "R1"], ["MI"], T.MI[:], T.R0[:, 15:128:16], T.R1[:, 15:128:16], A.min)
+                te(["NM0", "BOF"], "p7", mm(T.p7[:, 0:128], T.BOF[:], T.NM0[:], True, True))
+                tt(whole("FA") + ["p7"], whole("FA"), T.FA[:, 0:W:32], T.FA[:, 0:W:32], T.p7[:, 0:128], A.add)
+            te(["IB", "C0", "C0z"], "p6", mm(T.p6[:, 0:272], T.IB[:], T.C0[:], True, False))
+            te(stopped + RN_ALL, "p6", *[mm(T.p6[:, 128:272], T[n][:], T.RN[:]) for n in stopped])
+            te(["IB", "K2K"], "p4", mm(T.p4[:, 0:128], T.IB[:], T.K2K[:, 0:128], True, False))
+            te(stopped + ["BIGI"], "p4", *[mm(T.p4[:, 0:128], T.BIGI[:], T[n][:]) for n in stopped])
+            te(["IB", "KQ", "HI", ss], "p2", mm(T.p2[:, 0:128], T.IB[:], T.KQ[:], True, False),
+               mm(T.p2[:, 0:128], T.HI[:], T[ss][:]))
+            if t == 0:
+                fa_piece("p7")
+                fa_piece("p3")
+
+            scan(["p5", "RSB"], ["RB"], T.RB[:], T.RSB[:], T.p5[:, 0:64], 0.0, A.max, A.min)
+            tt(["RA", "RB"], ["MI"], T.MI[:], T.RA[:, 23:192:24], T.RB[:, 7:64:8], A.min)
             ts(["MI", "ZSc"], ["ZS"], T.ZS[:, 0:128:16], T.MI[:], W - 1, A.bitwise_and)
-            scan(["ZS", "ZSc", "ZD0"], ["YE"], T.YE[:], T.ZD0[:], T.ZS[:], 0.0, A.mult, A.add)
+            scan(["ZS", "ZSc", "CEX"], ["YE"], T.YE[:], T.CEX[:], T.ZS[:], 0.0, A.min, A.add)
+            te(["YE", "I160", "I161"], "p6", mm(T.p6[:, 0:256], T.YE[:], T.I16[:]))
             tt(["YE", "pC"], ["YM"], T.YM[:], T.YE[:], M16P, A.mult)
-            op("T", ["YM", "SEL8"], ["pYW"], mm(T.pYW[:, 0:8], T.YM[:], T.SEL8[:]))
-            op("T", ["YE", "IDF"], ["pYR"], mm(T.pYR[:, 0:128], T.YE[:], T.IDF[:]))
-            cp(["pYW"], ["YU"], T.YU[:], T.pYW[:, 0:8])
-            tt([far, "YU", "RT"], ["EL"], T.EL[:], F[:, 0:W].indirect(T.YU[:]), T.RT[:], A.is_lt)
-            tt(["pYW", "DW"], ["YD"], T.YD[:], T.pYW[:, 0:8], T.DW[:], A.subtract)
-            tt(["EL", "pC"], ["TH"], T.TH[:], T.EL[:], THRP, A.mult)
-            for h in (0, 7, 6, 5, 4, 3, 2, 1):
-                lo = 16 * h if h > 1 else 0
-                a, e = 128 * h + lo, 128 * h + 128
-                ts(["pYR", "pYW", "RW"], ["EQ%d" % h], T.EQ[:, a:e], T.pYR[:, lo:128], T.pYW[:, h:h + 1],
-                   A.is_equal, T.RW[:, h:h + 1], A.mult)
-                op("T", ["EQ%d" % h, "BOB"], ["pWS"], mm(T.pWS[:, lo:128], T.BOB[:], T.EQ[:, a:e], h == 0, h == 1))
-            tt(["X", "YU", ss], ["XG"], T.XG[:], T.X[:, 0:W].indirect(T.YU[:]), SS[:], A.add)
-            ts(["XG"], ["NR"], T.NR[:], T.XG[:], 0.5, A.mult, -0.25, A.add)
-            mu = "MU%d%d" % (t, d)
-            MU = T[mu]
-            if d < D - 1:
-                cp(["NR"], [mu + "r"], MU[:, 0:128], T.NR[:])
-            else:
-                ts(["pYR"], ["Y1"], T.Y1[:], T.pYR[:, 0:128], 1.0, A.add)
-            tt(["pWS", "TH"], ["WM"], T.WM[:], T.pWS[:, 0:128], T.TH[:], A.is_lt)
-            scan(["WM", "ZD0"], ["WS"], T.WS[:], T.ZD0[:], T.WM[:], 0.0, A.mult, A.add)
-            won = T.WS[:, 15:128:16]
-            tt(["WS", "YD"], ["SF0"], T.SF0[:], won, T.YD[:], A.mult)
-            tt(["SF0", "DW"], ["SF"], T.SF[:], T.SF0[:], T.DW[:], A.add)
-            cp(["SF"], [mu], MU[:, 128:136], T.SF[:])
-            sl = MU[:, 128:136]
+            te(["YM"] + RC_ALL, "p6", mm(T.p6[:, 0:272], T.YM[:], T.RC[:], False, True))
+            te(["YE", "I160"], "p4", mm(T.p4[:, 0:128], T.I16[:, 0:128], T.YE[:]))
+            ts(["p6"], ["YU"], T.YU[:], T.p6[:, 256:264], 2048.0, A.add)
+            act(whole(far) + ["YU"], ["TK"], T.TK[:], F[:, 0:W].indirect(T.YU[:]), AF.Relu, bias=1.0)
+            act(["X", "YU"], ["XG"], T.XG[:], T.X[:, 0:W].indirect(T.YU[:]))
+            ts(["p6"], ["EQ7"], T.EQ[:, 896:1024], T.p6[:, 128:256], 0.0, A.is_equal)
+            te(["EQ7", "RNa"], "p4", mm(T.p4[:, 0:128], T.EQ[:, 896:1024], T.RN[:, 0:128]))
+            for h in range(7):
+                lo = 16 * h + 16
+                ts(["p6"], ["EQ%d" % h], T.EQ[:, 128 * h + lo:128 * h + 128], T.p6[:, lo:128], T.p6[:, 264 + h:265 + h],
+                   A.is_equal)
+                if h == 3:
+                    te(["TK", "RNa"], "p4", mm(T.p4[:, 0:128], T.TK[:], T.RN[:, 0:128]))
+                te(["EQ%d" % h, "RNa"], "p4",
+                   mm(T.p4[:, 0:128], T.EQ[:, 128 * h:128 * h + 128], T.RN[:, 0:128], False, h == 6))
+            te(["XG", "HI"], "p2", mm(T.p2[:, 0:128], T.HI[:], T.XG[:], False, True))
+            act(["p2"], ["NRF"], T.NRF[:], T.p2[:, 0:128], bias=MAGIC)
+            act(["NRF"], ["NR"], T.NR[:], T.NRF[:], bias=-MAGIC)
+            yp, wx = "YP%d" % d, "WX%d" % d
+            tt(["p4", "DM"], [yp], T[yp][:], T.p4[:, 0:128], T.DM[:], A.min)
+            te([yp, "SEL8"], "p1", mm(T.p1[:, 0:8], T[yp][:], T.SEL8[:], True, True))
+            tt([yp, "pC"], [wx], T[wx][:], T[yp][:], TWON, A.is_lt)
+            k = D * t + d
+            mp = "MP%d" % k
+            sl = T.MP[:, 8 * k:8 * k + 8]
+            cp(["p1"], [mp], sl, T.p1[:, 0:8])
 
             def far_write():
-                cp([mu, "ST%d" % t, far + "spare"], [far], F[:, 0:WX].indirect(sl), ST[:])
+                cp([mp, st, far + "spare"], whole(far), F[:, 0:WX].indirect(sl), T[st][:])
 
             def rec_write():
-                cp([mu, "NR", "Xspare"], ["X"], T.X[:, 0:WX].indirect(sl), T.NR[:])
+                cp([mp, "NR", "Xspare"], ["X"], T.X[:, 0:WX].indirect(sl), T.NR[:])
 
-            def pairs(d=d, t=t):
-                if d < D - 1:
-                    ts(["pYR"], ["Y1"], T.Y1[:], T.pYR[:, 0:128], 1.0, A.add)
-                if d == 0:
-                    tt(["WM", "Y1"], ["YN"], T.YN[:], T.WM[:], T.Y1[:], A.mult)
-                    return
-                tt(["WM", "Y1"], ["YA"], T.YA[:], T.WM[:], T.Y1[:], A.mult)
-                if d < D - 1:
-                    tt(["YN", "YA"], ["YN"], T.YN[:], T.YN[:], T.YA[:], A.add)
-                elif t == 0:
-                    tt(["YN", "YA"], ["LS1n"], T.LS1[:, 128:256], T.YN[:], T.YA[:], A.add)
+            def count():
+                act([wx], ["CT", "WD"], T.WD[:], T[wx][:], accum_out=T.CT[:])
+                te(["CT", "ONF"], "p1", mm(T.p1[:, 0:1], T.ONF[:], T.CT[:], True, True))
+
+            def kappa(step):
+                if step == 0:
+                    cp(["p1"], ["KJ0"], T.KJ[:, 0:1], T.p1[:, 0:1])
+                elif step == 1:
+                    ts(["KJ0"], ["KJ1"], T.KJ[:, 1:2], T.KJ[:, 0:1], 31, A.bitwise_and)
                 else:
-                    tt(["YN", "YA"], ["LSF"], T.LSF[:], T.YN[:], T.YA[:], A.add)
+                    cp(["KJ1"], ["KF"], T.KF[:], T.KJ[:, 1:2])
+                    e = (d + 1) % D
+                    act(["KF", "KB%d" % e], ["KC"], T.KC[:], T.KB[:, 4 * e:4 * e + 4], AF.Identity, bias=T.KF[:])
 
-            def after(d=d, won=won, pairs=pairs):
-                tt(["RT", "WM"], ["RT"], T.RT[:], T.RT[:], T.WM[:], A.subtract)
-                tt(["RW", "WS"], ["RWT"], T.RWT[:], T.RW[:], won, A.mult)
-                tt(["RW", "RWT"], ["RW"], T.RW[:], T.RW[:], T.RWT[:], A.subtract)
-                pairs()
-
-            def kappa():
-                op("V", ["WS"], ["CT"], lambda: V.tensor_reduce(T.CT[:], won, AxisListType.X, A.add))
-                op("T", ["CT", "ONF"], ["pM"], mm(T.pM[:, 0:1], T.ONF[:], T.CT[:]))
-
-            def kappa2():
-                step = 97.0 * ((d + 1) % D)
-                counted.append(lambda: cp(["pM"], ["KI"], T.KI[:], T.pM[:, 0:1]))
-                counted.append(lambda: ts(["KI"], ["KJ"], T.KJ[:], T.KI[:], 31, A.bitwise_and))
-                scaled.append(lambda: cp(["KJ"], ["KF"], T.KF[:], T.KJ[:]))
-                scaled.append(lambda: ts(["KB", "KF"], ["KC"], T.KC[:], T.KB[:], T.KF[:], A.add, step, A.add))
+            def pairings():
+                te(["ND3", "IDF"], "p7", mm(T.p7[:, 0:128], T.ND3[:], T.IDF[:], True, False))
+                for e in range(D):
+                    te(["WX%d" % e, "YP%d" % e, "D4K", "DQ1", "IDF"], "p7",
+                       mm(T.p7[:, 0:128], T["WX%d" % e][:], T.D4K[:]), mm(T.p7[:, 0:128], T["WX%d" % e][:], T.DQ1[:]),
+                       mm(T.p7[:, 0:128], T["YP%d" % e][:], T.IDF[:], False, e == D - 1))
+                act(["p7"], ["NN%d" % t], T["NN%d" % t][:], T.p7[:, 0:128])
+                send("N%d" % t, home, T["NM%d" % t][:], T["NN%d" % t][:], ["NN%d" % t], "NM%d" % t)
 
             if d < D - 1:
-                un = "U%d%d" % (t, d)
-                ul = "UL%d%d" % (t, d)
-                send(un, to, T[ul][:], MU[:], [mu, mu + "r"], ul)
+                kk = (D - 1) * t + d
+                ur, up = T.UR[:, 128 * kk:128 * kk + 128], T.UP[:, 8 * k:8 * k + 8]
+                send("R%d%d" % (t, d), to, ur, T.NR[:], ["NR"], "UR%d" % kk)
+                send("P%d%d" % (t, d), to, up, sl, [mp], "UP%d" % k)
+                count()
                 far_write()
-                kappa()
-                tt([far, "YU", "M16"], ["PG"], T.PG[:], F[:, 0:W].indirect(T.YU[:]), T.M16[:], A.mult)
-                scan(["PG", "ZD0"], ["PS"], T.PS[:], T.ZD0[:], T.PG[:], 0.0, A.mult, A.add)
-                kappa2()
-                cp(["PS"], ["PU"], T.PU[:], T.PS[:, 15:128:16])
+                act(["p6"], ["YRS"], T.YRS[:], T.p6[:, 0:128], bias=2048.0)
+                act(whole(far) + ["YU"], ["PGR"], T.PGR[:], F[:, 0:W].indirect(T.YU[:]))
+                te(["YRS", "IL0", "IL1"], "p6", *[
+                    mm(T.p6[:, 0:64], T.IL[:, 128 * e:128 * e + 128], T.YRS[:, e:128:2], e == 0, e == 1) for e in range(2)])
+                kappa(0)
                 rec_write()
-                later.append(after)
-                cp([ul, xr + "spare"], [xr], XR[:, 0:WX].indirect(T[ul][:, 128:136]), T[ul][:, 0:128])
+                kappa(1)
+                scan(["PGR", "pC"], ["PS"], T.PS[:], CPK, T.PGR[:], -BIG, A.add, A.min)
+                kappa(2)
+                ts(["PS", "PG7"], ["PU"], T.PU[:], T.PS[:, 15:128:16], T.PG[:, 7:8], A.add)
+                if t == 0:
+                    fa_piece("p7")
+                    fa_piece("p3")
+                cp(["UR%d" % kk, "UP%d" % k, xr + "spare"], [xr], XR[:, 0:WX].indirect(up), ur)
                 cp([xr, "PU"], ["Z"], T.Z[:], XR[:, 0:W].indirect(T.PU[:]))
             elif t == 0:
                 rec_write()
                 cp(["X"], ["SN1"], T.SN1[:], T.X[:, 1:W:32])
                 send("S1", prv, T.SS1[:], T.SN1[:], ["SN1"], "SS1")
-                kappa()
+                count()
                 far_write()
-                tt(["FB", "M16M"], ["LS1l"], T.LS1[:, 0:128], T.FB[:, 1:W:32], T.M16M[:], A.is_lt)
-                kappa2()
-                pairs()
+                kappa(0)
+                tt(whole("FB") + ["pC"], ["LT"], T.LT[:], T.FB[:, 1:W:32], TFREE, A.is_gt)
+                kappa(1)
+                te(["LT", "IB"], "p3", mm(T.p3[:, 0:128], T.LT[:], T.IB[:], True, True))
+                kappa(2)
+                act(["p3"], ["NH1"], T.NH1[:], T.p3[:, 0:128])
+                send("L1", prv, T.NL1[:], T.NH1[:], ["NH1"], "NL1")
+                pairings()
                 send("X1", prv, T.XR1[:, 0:W], T.X[:, 0:W], ["X"], "XR1")
-                send("L1", prv, T.LL1[:], T.LS1[:], ["LS1l", "LS1n"], "LL1")
             else:
-                pairs()
-                send("LF", home, T.LLF[:], T.LSF[:], ["LSF"], "LLF")
                 rec_write()
                 dma("Y", "oX", [(T.yx[:], T.X[:, 0:W])], ["X"], ["yx"])
+                pairings()
                 far_write()
-                dma("Y", "oA", [(T.ya[:], T.FA[0:128:16, 0:W])], ["FA"], ["ya"])
+                dma("Y", "oA", [(T.ya[:], T.FA[0:128:16, 0:W])], whole("FA"), ["ya"])
 
-    op("T", ["LLF", "BOF"], ["pM"], mm(T.pM[:, 0:128], T.BOF[:], T.LLF[:]))
-    tt(["FB", "pM"], ["FB"], T.FB[:, 1:W:32], T.FB[:, 1:W:32], T.pM[:, 0:128], A.add)
-    dma("Y", "oB", [(T.yb[:], T.FB[0:128:16, 0:W])], ["FB"], ["yb"])
+    te(["NM1", "BOF"], "p7", mm(T.p7[:, 0:128], T.BOF[:], T.NM1[:], True, True))
+    tt(whole("FB") + ["p7"], whole("FB"), T.FB[:, 1:W:32], T.FB[:, 1:W:32], T.p7[:, 0:128], A.add)
+    dma("Y", "oB", [(T.yb[:], T.FB[0:128:16, 0:W])], whole("FB"), ["yb"])
     finish()

@@ -6,6 +6,8 @@ W, L, TB, D = 4096, 128, 2, 3
 WX = W + L
 FULL = 16777216.0
 BIG = 8192.0
+LOW = 1.0e6
+SPLIT = (72, 72, 64)
 MAGIC = 12582912.0
 
 F32, BF, F16, I32, U16 = "float32", "bfloat16", "float16", "int32", "uint16"
@@ -13,20 +15,18 @@ SCRATCH = {}
 for _names, _cols, _dt in (
         ("X XR0 XR1", WX, BF), ("FA FB", WX, F32),
         ("PA2 PB2", 256, I32), ("PA2H PB2H", 256, F16), ("FT", 2048, F16),
-        ("WTI", 1, I32), ("WI", 2, I32), ("WF", 2, F32), ("WM", 512, BF),
+        ("WTI", 1, I32), ("WI", 2, I32), ("WF", 2, F32), ("WM", 1024, BF),
         ("PI", 2, I32), ("PX", 6, I32), ("PF", 6, F32), ("PG", 8, F32),
         ("CI CMI CGI CI8 ZS", 128, I32), ("SLI", 64, I32),
-        ("M16 IDF BOF ONF DM ND3 CEX ST0 ST1", 128, F32), ("IL CP", 256, F32),
-        ("BOB IB NIB HI BIGI D4K DQ1 KQ", 128, BF), ("K2K ZB", 192, BF), ("GM", 16, BF), ("SEL8", 8, F32),
-        ("BO16", 128, F16), ("I16", 256, F16), ("RC", 272, F16), ("C0", 272, BF), ("RN", 144, BF),
-        ("SL", 128, F16), ("NS", 128, BF),
+        ("M16 IDF NBO ONF CEX CY CIW CPL CPK TFREE ST0 ST1", 128, F32), ("IL CP", 256, F32),
+        ("BOB BO4K BOBIG IB NIB HI BIGI KM", 128, BF), ("K2K KQ", 192, BF), ("GM", 16, BF),
+        ("BO16 I16", 128, F16), ("C0", 256, BF), ("SL", 128, F16), ("NS", 128, BF),
         ("RSA RSA0 RA", 192, F32), ("RSB RSB0 RB", 64, F32), ("BJ0 BJ BJ2 KC", 4, F32), ("KB", 12, F32),
-        ("SN0 SN1 SS0 SS1 NH0 NH1 NL0 NL1 LT Z", 128, BF), ("NN0 NN1 NM0 NM1", 128, F32),
-        ("ZR", 1024, BF), ("KI", 64, I32), ("FR", 64, F32), ("SQ", 256, F32), ("AI CC", 256, I32), ("CU", 256, U16),
-        ("CFE", 528, F16), ("NQE", 528, BF), ("DD GS", 2048, BF), ("AB", W, BF),
-        ("MI", 8, I32), ("YE YM", 128, F16), ("YU PU", 8, U16), ("EQ", 1024, BF),
-        ("TK XG NR", 128, BF), ("NRF YRS PGR PS", 128, F32),
-        ("YP0 YP1 YP2", 128, F32), ("WX0 WX1 WX2", 128, BF), ("WD", 128, BF),
+        ("SN0 SN1 SS0 SS1 NH0 NH1 NL0 NL1 Z", 128, BF), ("NN0 NN1 NM0 NM1", 128, F32),
+        ("ZR", 1024, BF), ("SQ", 256, F32), ("AI CC", 256, I32), ("CU", 256, U16),
+        ("CFE", 528, F16), ("NQE", 528, BF), ("DD GS AB", W, BF),
+        ("MI", 8, I32), ("YE", 128, F16), ("PY", 136, F32), ("YU PU", 8, U16), ("EQ", 1024, BF),
+        ("TK XG NR", 128, BF), ("YRS PGR PS PP WV", 128, F32), ("SG0 SG1 SG2", 128, BF),
         ("CT KF", 1, F32), ("KJ", 2, I32),
         ("MP", 8 * TB * D, U16), ("UP", 8 * TB * D, U16), ("UR", 128 * TB * (D - 1), BF)):
     for _n in _names.split():
@@ -34,8 +34,8 @@ for _names, _cols, _dt in (
 SCRATCH["P8"] = ("sbuf", [8, W], I32)
 SCRATCH["LV8"] = ("sbuf", [8, 128], BF)
 SCRATCH["E8"] = ("sbuf", [8, 128], BF)
-for _n in ("p1", "p2", "p3", "p4", "p5", "p6", "p7", "pC"):
-    SCRATCH[_n] = ("psum", [128, 512], F32)
+for _n in range(1, 9):
+    SCRATCH["p%d" % _n] = ("psum", [128, 512], F32)
 
 REMOTE = ["S0", "X0", "L0", "S1", "X1", "L1", "N0", "N1"] + [k + "%d%d" % (t, d) for k in "RP" for t in range(TB)
                                                              for d in range(D - 1)]
@@ -176,23 +176,18 @@ def rank_program(g, core, T, topo):
     def te(reads, bank, *fns):
         op("T", reads, [bank], *fns)
 
-    dma("Y", "dW", [(T.WTI[:], T.wt[:])], [], ["WTI"])
-    dma("Y", "dPB", [(T.PB2[:], T.pb[:])], [], ["PB2"])
-    dma("Y", "dX", [(T.X[:, 0:W], T.x[:])], [], ["X"])
     dma("Y", "dP8", [(T.P8[:], T.pa[:])], [], ["P8"])
+    dma("Y", "dPB", [(T.PB2[:], T.pb[:])], [], ["PB2"])
+    dma("Y", "dW", [(T.WTI[:], T.wt[:])], [], ["WTI"])
+    dma("Y", "dX", [(T.X[:, 0:W], T.x[:])], [], ["X"])
     dma("Y", "dPA", [(T.PA2[:], T.pa[:])], [], ["PA2"])
 
     iota("PI", [[1, 2]], 0, 1)
+    iota("CMI", [[0, 8], [1, 16]], 0, 0)
+    iota("CGI", [[1, 8], [0, 16]], 0, 0)
     iota("CI", [[1, 128]], 0, 0)
-    iota("BJ0", [[256, 4]], 16, 0, True)
-    iota("SLI", [[-16, 8], [-1, 8]], 0, 1)
-    iota("RSA0", [[0, 8], [1, 24]], 0, 0, True)
-    iota("RSB0", [[0, 8], [1, 8]], 0, 0, True)
-    iota("ST0", [[32, 128]], 0, 0, True)
-    iota("ST1", [[32, 128]], 1, 0, True)
-    fill(["EQ%d" % h for h in range(8)], T.EQ[:], 0.0)
+    iota("CI8", [[1, 16], [0, 8]], 0, 0)
     fill(["NQE"], T.NQE[:], 0.0)
-    fill(["ZSc"], T.ZS[:], 0)
     p = T.PI[:, 0:1]
     cp(["PI"], ["PX0"], T.PX[:, 0:1], p)
     ts(["PI"], ["PX1"], T.PX[:, 1:2], p, 15, A.bitwise_and)
@@ -200,15 +195,42 @@ def rank_program(g, core, T, topo):
     ts(["PI"], ["PX3"], T.PX[:, 3:4], p, 7, A.bitwise_and)
     ts(["PI"], ["PX4"], T.PX[:, 4:5], p, 3, A.logical_shift_right, 1, A.bitwise_and)
     ts(["PI"], ["PX5"], T.PX[:, 5:6], T.PI[:, 1:2], 15, A.bitwise_and)
-    ts(["CI"], ["CMI"], T.CMI[:], T.CI[:], 15, A.bitwise_and)
+    fill(["K2K"], T.K2K[:], 2048.0)
     cp(["PX%d" % k for k in range(6)], ["PF"], T.PF[:], T.PX[:])
-    ts(["CI"], ["CGI"], T.CGI[:], T.CI[:], 4, A.logical_shift_right)
-    ts(["CI"], ["CI8"], T.CI8[:], T.CI[:], 3, A.logical_shift_right)
+    fill(["C0a"], T.C0[:, 0:128], 2048.0)
+    fill(["KQa"], T.KQ[:, 0:128], -0.25)
+    fill(["KQ"], T.KQ[:, 128:192], 0.5)
+    fill(["KM"], T.KM[:], MAGIC)
     P_, PM, PGc, PJ, PL, PM1 = [T.PF[:, k:k + 1] for k in range(6)]
     ts(["CMI", "PF"], ["M16"], T.M16[:], T.CMI[:], PM, A.is_equal)
     ts(["CGI", "PF"], ["BO16"], T.BO16[:], T.CGI[:], PGc, A.is_equal)
+    ts(["CGI", "PF"], ["E8"], T.E8[:], T.CGI[0:8, :], T.PF[0:8, 0:1], A.is_equal)
     ts(["CI", "PF"], ["IDF"], T.IDF[:], T.CI[:], P_, A.is_equal)
+    ts(["CGI", "PF"], ["BOB"], T.BOB[:], T.CGI[:], PGc, A.is_equal)
+    for k, (src, a, b) in enumerate(((PGc, 2.0, 0.0), (PGc, 2.0, 1.0), (PJ, 32.0, 0.0), (PL, -1.0, 1.0))):
+        ts(["PF"], ["PG%d" % k], T.PG[:, k:k + 1], src, a, A.mult, b, A.add)
+    ts(["PF"], ["PG4"], T.PG[:, 4:5], PM, 15.0, A.is_lt, BIG, A.mult)
+    ts(["P8"], ["LV8"], T.LV8[:], T.P8[:, 0:W:32], 0.0, A.is_ge)
+    te(["E8", "LV8"], "p7", mm(T.p7[:, 0:128], T.E8[:], T.LV8[:], True, True))
     ts(["PB2"], ["PB2H"], T.PB2H[:], T.PB2[:], -2047.0, A.add)
+    tt(["p7", "M16"], ["NH0"], T.NH0[:], T.p7[:, 0:128], T.M16[:], A.mult)
+    send("L0", nxt, T.NL0[:], T.NH0[:], ["NH0"], "NL0")
+    iota("BJ0", [[256, 4]], 16, 0, True)
+    iota("SLI", [[-16, 8], [-1, 8]], 0, 1)
+    iota("RSA0", [[0, 8], [1, 24]], 0, 0, True)
+    iota("RSB0", [[0, 8], [1, 8]], 0, 0, True)
+    iota("CEX", [[0, 8], [30000, 16]], -2048, 0, True)
+    iota("CIW", [[1, 128]], W, 0, True)
+    iota("ST0", [[32, 128]], 0, 0, True)
+    for name, scale in (("IB", 1.0), ("NIB", -1.0), ("HI", 0.5), ("BIGI", BIG)):
+        act(["IDF"], [name], T[name][:], T.IDF[:], scale=scale)
+    act(["M16"], ["C0b"], T.C0[:, 128:256], T.M16[:], scale=-4 * BIG, bias=4 * BIG + 2048)
+    act(["M16"], ["CY"], T.CY[:], T.M16[:], scale=LOW, bias=-LOW)
+    act(["M16"], ["TFREE"], T.TFREE[:], T.M16[:], scale=-BIG - 0.5, bias=BIG)
+    for name, scale in (("BOBIG", BIG), ("BO4K", float(W)), ("NBO", -1.0)):
+        act(["BOB"], [name], T[name][:], T.BOB[:], scale=scale)
+    act(["IDF", "PG3"], ["IL0"], T.IL[:, 0:128], T.IDF[:], scale=T.PG[:, 3:4])
+    act(["IDF", "PF"], ["IL1"], T.IL[:, 128:256], T.IDF[:], scale=PL)
     for k in range(16):
         ts(["BO16", "M16"], ["FT%d" % k], T.FT[:, 128 * k:128 * k + 128], T.BO16[:], T.M16[:, k:k + 1], A.mult)
 
@@ -226,12 +248,8 @@ def rank_program(g, core, T, topo):
     def whole(name):
         return [name + str(c) for c in range(8)]
 
-    for c in range(8):
+    for c in range(7):
         table("FB", c, ("p2", "p3", "p4", "p5")[c % 4], "S")
-    for k, (src, a, b) in enumerate(((PGc, 2.0, 0.0), (PGc, 2.0, 1.0), (PJ, 32.0, 0.0), (P_, 1.0, float(W)),
-                                     (P_, -3.0, -3.0 * W), (P_, 1.0, 1.0), (PL, -1.0, 1.0))):
-        ts(["PF"], ["PG%d" % k], T.PG[:, k:k + 1], src, a, A.mult, b, A.add)
-    ts(["PF"], ["PG7"], T.PG[:, 7:8], PM, 15.0, A.is_lt, BIG, A.mult)
     ts(["WTI"], ["WI0"], T.WI[:, 0:1], T.WTI[:], 4032, A.bitwise_and)
     ts(["WTI"], ["WI1"], T.WI[:, 1:2], T.WTI[:], 63, A.bitwise_and)
     ts(["BJ0", "PG2"], ["BJ"], T.BJ[:], T.BJ0[:], T.PG[:, 2:3], A.add)
@@ -242,64 +260,36 @@ def rank_program(g, core, T, topo):
            T.PG[:, k // 2:k // 2 + 1], A.is_equal, T.WF[:, k % 2:k % 2 + 1], A.mult)
     for d in range(D):
         ts(["BJ2"], ["KB%d" % d], T.KB[:, 4 * d:4 * d + 4], T.BJ2[:], -1.0 / 32, A.mult, 97.0 * d - 0.4375, A.add)
-    cp(["X"], ["SN0"], T.SN0[:], T.X[:, 0:W:32])
-    send("S0", nxt, T.SS0[:], T.SN0[:], ["SN0"], "SS0")
-    send("X0", nxt, T.XR0[:, 0:W], T.X[:, 0:W], ["X"], "XR0")
-    for name, scale in (("IB", 1.0), ("NIB", -1.0), ("HI", 0.5), ("BIGI", BIG), ("D4K", float(W))):
-        act(["IDF"], [name], T[name][:], T.IDF[:], scale=scale)
-    fill(["K2K"], T.K2K[:], 2048.0)
-    fill(["ZB"], T.ZB[:], 0.0)
-    fill(["KQ"], T.KQ[:], -0.25)
-    fill(["ONF"], T.ONF[:], 1.0)
-    fill(["C0z"], T.C0[:], 0.0)
-    fill(["RNz"], T.RN[:, 128:136], 0.0)
-    for n in ("X", "XR0", "XR1", "FA", "FB"):
-        fill([n + "spare"], T[n][:, W:WX], 0.0)
-    cp(["EQ0"], ["CFE"], T.CFE[:], T.EQ[:, 0:528])
-    ts(["CI", "PF"], ["SEL8"], T.SEL8[:], T.CI[:, 0:8], PGc, A.is_equal)
+    ts(["WM%d" % k for k in range(4)], ["WMn"], T.WM[:, 512:1024], T.WM[:, 0:512], -1.0, A.mult)
+    cp(["NQE"], ["CFE"], T.CFE[:], T.NQE[:])
     ts(["CI", "PF"], ["GMa"], T.GM[:, 0:8], T.CI[:, 0:8], PGc, A.is_equal, float(W), A.mult)
     ts(["CI", "PF"], ["GMb"], T.GM[:, 8:16], T.CI[:, 0:8], PGc, A.is_equal, -float(W), A.mult)
     for e in range(2):
         ts(["SLI"], ["SL%d" % e], T.SL[:, 64 * e:64 * e + 64], T.SLI[:], 8.0 * e, A.is_equal)
         ts(["SLI"], ["NS%d" % e], T.NS[:, 64 * e:64 * e + 64], T.SLI[:], 8.0 * e, A.is_equal, -FULL, A.mult)
-    ts(["CGI", "PF"], ["BOB"], T.BOB[:], T.CGI[:], PGc, A.is_equal)
-    ts(["CGI", "PF"], ["E8"], T.E8[:], T.CGI[0:8, :], T.PF[0:8, 0:1], A.is_equal)
-    ts(["P8"], ["LV8"], T.LV8[:], T.P8[:, 0:W:32], 0.0, A.is_ge)
-    te(["E8", "LV8"], "p7", mm(T.p7[:, 0:128], T.LV8[:], T.E8[:], True, True))
-    for e in range(2):
-        cp(["IDF"], ["I16%d" % e], T.I16[:, 128 * e:128 * e + 128], T.IDF[:])
-    cp(["EQ0"], ["RCa"], T.RC[:, 0:128], T.EQ[:, 0:128])
-    ts(["BO16"], ["RCb"], T.RC[:, 128:256], T.BO16[:], -1.0, A.mult)
-    tt(["p7", "M16"], ["NH0"], T.NH0[:], T.p7[:, 0:128], T.M16[:], A.mult)
-    send("L0", nxt, T.NL0[:], T.NH0[:], ["NH0"], "NL0")
-    cp(["SEL8"], ["RCc"], T.RC[:, 256:264], T.SEL8[:])
-    cp(["SEL8"], ["RCd"], T.RC[:, 264:272], T.SEL8[:])
-    ts(["CMI", "PF", "C0z"], ["C0"], T.C0[:, 128:256], T.CMI[:], PM, A.is_le, BIG, A.mult)
-    ts(["CMI", "PF"], ["CPA"], T.CP[:, 0:128], T.CMI[:], PM, A.is_equal, 4 * BIG, A.mult)
-    ts(["CMI", "PF"], ["CPB"], T.CP[:, 128:256], T.CMI[:], PM1, A.is_equal, -BIG, A.mult)
-    ts(["CMI"], ["CEX"], T.CEX[:], T.CMI[:], 1.0e6, A.mult, -2048.0, A.add)
-    ts(["PA2"], ["PA2H"], T.PA2H[:], T.PA2[:], -2047.0, A.add)
-    tt(["CPA", "CPB"], ["pC"], T.pC[:, 256:384], T.CP[:, 0:128], T.CP[:, 128:256], A.add)
-    M16P, TWON, CPK, TFREE = [T.pC[:, 128 * k:128 * k + 128] for k in range(4)]
+    cp(["X"], ["SN0"], T.SN0[:], T.X[:, 0:W:32])
+    send("S0", nxt, T.SS0[:], T.SN0[:], ["SN0"], "SS0")
+    send("X0", nxt, T.XR0[:, 0:W], T.X[:, 0:W], ["X"], "XR0")
+    iota("ST1", [[32, 128]], 1, 0, True)
+    act(["RSA0"], ["RSA"], T.RSA[:], T.RSA0[:], scale=-1.0e8, bias=5.0e7)
+    act(["RSB0"], ["RSB"], T.RSB[:], T.RSB0[:], scale=-1.0e8, bias=5.0e7)
+    table("FB", 7, "p5", "V")
+    fill(["ZSc"], T.ZS[:], 0)
+    fill(["PYc"], T.PY[:, 0:1], -1.0)
+    for n in ("X", "FB"):
+        fill([n + "spare"], T[n][:, W:WX], 0.0)
+    cp(["IDF"], ["I16"], T.I16[:], T.IDF[:])
+    tt(["CY", "CIW"], ["CPL"], T.CPL[:], T.CY[:], T.CIW[:], A.add)
 
     def late_constants():
-        act(["RSA0"], ["RSA"], T.RSA[:], T.RSA0[:], scale=-1.0e8, bias=5.0e7)
-        act(["RSB0"], ["RSB"], T.RSB[:], T.RSB0[:], scale=-1.0e8, bias=5.0e7)
-        act(["M16"], ["pC"], M16P, T.M16[:])
-        act(["M16"], ["pC"], TWON, T.M16[:], scale=W + 1.0, bias=-1.0)
-        act(["M16"], ["pC"], TFREE, T.M16[:], scale=-BIG - 0.5, bias=BIG)
-        act(["BOB"], ["RNa"], T.RN[:, 0:128], T.BOB[:], scale=BIG)
-        act(["SEL8"], ["RNb"], T.RN[:, 136:144], T.SEL8[:], scale=BIG)
-        act(["M16", "PG3"], ["DM"], T.DM[:], T.M16[:], scale=T.PG[:, 3:4])
-        act(["M16", "PG4"], ["ND3"], T.ND3[:], T.M16[:], scale=T.PG[:, 4:5])
-        act(["IDF", "PG5"], ["DQ1"], T.DQ1[:], T.IDF[:], scale=T.PG[:, 5:6])
-        act(["IDF", "PG6"], ["IL0"], T.IL[:, 0:128], T.IDF[:], scale=T.PG[:, 6:7])
-        act(["IDF", "PF"], ["IL1"], T.IL[:, 128:256], T.IDF[:], scale=PL)
-        act(["BOB"], ["BOF"], T.BOF[:], T.BOB[:])
+        for n in ("XR0", "XR1", "FA"):
+            fill([n + "spare"], T[n][:, W:WX], 0.0)
+        fill(["ONF"], T.ONF[:], 1.0)
+        ts(["CMI", "PF"], ["CPA"], T.CP[:, 0:128], T.CMI[:], PM, A.is_equal, 4 * BIG, A.mult)
+        ts(["CMI", "PF"], ["CPB"], T.CP[:, 128:256], T.CMI[:], PM1, A.is_equal, -BIG, A.mult)
+        ts(["PA2"], ["PA2H"], T.PA2H[:], T.PA2[:], -2047.0, A.add)
+        tt(["CPA", "CPB"], ["CPK"], T.CPK[:], T.CP[:, 0:128], T.CP[:, 128:256], A.add)
 
-    late_constants()
-    RC_ALL = ["RCa", "RCb", "RCc", "RCd"]
-    RN_ALL = ["RNa", "RNz", "RNb"]
     zr_all = ["ZR%d" % m for m in range(8)]
     fa_left = list(range(8))
 
@@ -319,24 +309,22 @@ def rank_program(g, core, T, topo):
             Z = T[zn]
             first = t == 0 and d == 0
             kn, KN = ("KB0", T.KB) if first else ("KC", T.KC)
-            stopped = [nl] + ["WX%d" % e for e in range(d)]
+            stopped = [nl] + ["SG%d" % e for e in range(d)]
 
-            te(["WM%d" % k for k in range(4)] + [zn], "p1", *[
-                mm(T.p1[:, 0:64], T.WM[:, 128 * k:128 * k + 128], Z[:, k // 2:128:2], k == 0, k == 3) for k in range(4)])
+            pu = T.p1[:, 0:64]
 
-            def rep(m):
+            def weighted(sign):
+                return [mm(pu, T.WM[:, 128 * (4 * sign + k):128 * (4 * sign + k + 1)], Z[:, k // 2:128:2], False,
+                           sign == 0 and k == 3) for k in range(4)]
+
+            te(["IB", "KQ"], "p1", mm(pu, T.IB[:], T.KQ[:, 128:192], True, False))
+            te(["WMn", "IB", "NIB", "KM", zn] + ["WM%d" % k for k in range(4)], "p1", *(
+                weighted(1) + [mm(pu, T.IB[:], T.KM[:, 0:64]), mm(pu, T.NIB[:], T.KM[:, 0:64])] + weighted(0)))
+            for m in range(8):
                 cp([zn], ["ZR%d" % m], T.ZR[:, m:1024:8], Z[:])
-
-            for m in range(0, 3):
-                rep(m)
-            ts(["p1"], ["KI"], T.KI[:], T.p1[:, 0:64], -0.5, A.add)
-            rep(3)
-            tt(["p1", "KI"], ["FR"], T.FR[:], T.p1[:, 0:64], T.KI[:], A.subtract)
             for b in range(4):
-                act(["FR", "BJ"], ["SQ%d" % b], T.SQ[:, 64 * b:64 * b + 64], T.FR[:], AF.Square, scale=float(W),
+                act(["p1", "BJ"], ["SQ%d" % b], T.SQ[:, 64 * b:64 * b + 64], pu, AF.Square, scale=float(W),
                     bias=T.BJ[:, b:b + 1])
-            for m in range(4, 8):
-                rep(m)
 
             def whole_part(b):
                 c = slice(64 * b, 64 * b + 64)
@@ -358,20 +346,17 @@ def rank_program(g, core, T, topo):
             def kbank(b):
                 return "p4" if b < 3 else "p5"
 
-            def sbank(b):
-                return "p2" if b % 2 == 0 else "p3"
-
             def gather_v(b, lo, hi):
-                tt(["X", "CU%d" % b] + zr_all, ["DD%d_%d" % (b, lo)], T.DD[:, 512 * b + 8 * lo:512 * b + 8 * hi],
+                tt(["X", "CU%d" % b] + zr_all, ["DD%d_%d" % (b, lo)], T.DD[:, 1024 * b + 8 * lo:1024 * b + 8 * hi],
                    T.X[:, 0:W].indirect(T.CU[:, 64 * b + lo // 2:64 * b + hi // 2]), T.ZR[:, 8 * lo:8 * hi], A.subtract)
 
             def relu_v(b, lo, hi):
                 ts(["DD%d_%d" % (b, lo)], ["AB%d_%d" % (b, lo)], T.AB[:, 1024 * b + 8 * lo:1024 * b + 8 * hi],
-                   T.DD[:, 512 * b + 8 * lo:512 * b + 8 * hi], 0.0, A.max, 2.0, A.mult)
+                   T.DD[:, 1024 * b + 8 * lo:1024 * b + 8 * hi], 0.0, A.max, 2.0, A.mult)
 
             def minus_d(b, lo, hi):
                 te(["DD%d_%d" % (b, lo), "GMb"], kbank(b), *[
-                    mm(keys(b, lo, hi, j), T.DD[:, 512 * b + 8 * lo + j:512 * b + 8 * hi:8], T.GM[:, 8:16])
+                    mm(keys(b, lo, hi, j), T.DD[:, 1024 * b + 8 * lo + j:1024 * b + 8 * hi:8], T.GM[:, 8:16])
                     for j in range(8)])
 
             def plus_abs(b, lo, hi, parts):
@@ -379,20 +364,22 @@ def rank_program(g, core, T, topo):
                     mm(keys(b, lo, hi, j), T.AB[:, 1024 * b + 8 * lo + j:1024 * b + 8 * hi:8], T.GM[:, 0:8])
                     for j in range(8)])
 
-            def minus_z(b):
-                te(["NIB"] + zr_all, sbank(b), mm(T[sbank(b)][:, 0:512], T.NIB[:], T.ZR[:, 512:1024], True, False))
+            def minus_z(bank, lo, hi):
+                te(["NIB"] + zr_all, bank, mm(T[bank][:, 0:8 * (hi - lo)], T.NIB[:], T.ZR[:, 8 * lo:8 * hi], True, False))
 
-            def gather_s(b):
-                act(["X", "CU%d" % b], ["GS%d" % b], T.GS[:, 512 * b:512 * b + 512],
-                    T.X[:, 0:W].indirect(T.CU[:, 64 * b + 32:64 * b + 64]))
+            def gs(b, lo, hi):
+                return T.GS[:, 1024 * b + 8 * lo:1024 * b + 8 * hi]
 
-            def plus_x(b):
-                te(["GS%d" % b, "IB"], sbank(b),
-                   mm(T[sbank(b)][:, 0:512], T.IB[:], T.GS[:, 512 * b:512 * b + 512], False, True))
+            def gather_s(b, lo, hi):
+                act(["X", "CU%d" % b], ["GS%d_%d" % (b, lo)], gs(b, lo, hi),
+                    T.X[:, 0:W].indirect(T.CU[:, 64 * b + lo // 2:64 * b + hi // 2]))
 
-            def abs_s(b, lo, hi):
-                act([sbank(b)], ["AB%d_%d" % (b, lo)], T.AB[:, 1024 * b + 8 * lo:1024 * b + 8 * hi],
-                    T[sbank(b)][:, 8 * (lo - 64):8 * (hi - 64)], AF.Abs)
+            def plus_x(bank, b, lo, hi):
+                te(["GS%d_%d" % (b, lo), "IB"], bank, mm(T[bank][:, 0:8 * (hi - lo)], T.IB[:], gs(b, lo, hi), False, True))
+
+            def abs_s(bank, b, lo, hi):
+                act([bank], ["AB%d_%d" % (b, lo)], T.AB[:, 1024 * b + 8 * lo:1024 * b + 8 * hi],
+                    T[bank][:, 0:8 * (hi - lo)], AF.Abs)
 
             def spread(src, sel, names, b, stop=False):
                 out = T.p4[:, b:192:3] if b < 3 else T.p5[:, 0:64]
@@ -401,115 +388,113 @@ def rank_program(g, core, T, topo):
                     for e in range(2)])
 
             def barred(b):
-                tt(["CC%d" % b, "p6"], ["NQE%d" % b], T.NQE[:, 2 + 128 * b:130 + 128 * b:2], T.CC[:, 64 * b:64 * b + 64],
-                   T.p6[:, 0:64], A.not_equal)
-                spread(T.NQE, T.NS, ["NQE", "NQE%d" % b, "NS0", "NS1"], b)
+                if d > 0:
+                    tt(["CC%d" % b, "p6"], ["NQE%d" % b], T.NQE[:, 2 + 128 * b:130 + 128 * b:2],
+                       T.CC[:, 64 * b:64 * b + 64], T.p6[:, 0:64], A.not_equal)
+                    spread(T.NQE, T.NS, ["NQE", "NQE%d" % b, "NS0", "NS1"], b)
+
+            def places(b, stop):
+                spread(T.CFE, T.SL, ["CFE", "SL0", "SL1"], b, stop)
 
             te(["IB", "K2K"], "p4", mm(T.p4[:, 0:192], T.IB[:], T.K2K[:], True, False))
             te(["IB", "K2K"], "p5", mm(T.p5[:, 0:64], T.IB[:], T.K2K[:, 0:64], True, False))
-            minus_z(0)
-            minus_z(1)
-            whole_part(0)
-            whole_part(1)
+            s0, s1, s2 = SPLIT
+            minus_z("p2", s0, 128)
+            minus_z("p3", s1, 128)
+            minus_z("p7", s2, 128)
+            for b in range(4):
+                whole_part(b)
             modulo(0, 1)
-            whole_part(2)
-            offsets(0, 1)
-            gather_s(0)
-            whole_part(3)
             modulo(1, 4)
-            plus_x(0)
-            if d > 0:
-                barred(0)
+            offsets(0, 1)
             offsets(1, 4)
-            gather_s(1)
-            gather_v(0, 0, 64)
-            abs_s(0, 64, 128)
-            minus_d(0, 0, 64)
-            plus_x(1)
-            minus_z(2)
-            gather_s(2)
-            gather_v(1, 0, 64)
-            relu_v(0, 0, 64)
-            abs_s(1, 64, 128)
-            minus_d(1, 0, 64)
-            plus_abs(0, 0, 128, [0, 64])
-            plus_x(2)
-            minus_z(3)
-            gather_s(3)
+            gather_s(0, s0, 128)
+            gather_v(0, 0, s0)
+            te(["IB", "C0b"], "p1", mm(T.p1[:, 0:128], T.IB[:], T.C0[:, 128:256], True, False))
+            plus_x("p2", 0, s0, 128)
+            gather_s(1, s1, 128)
+            abs_s("p2", 0, s0, 128)
+            minus_d(0, 0, s0)
+            for b in range(4):
+                barred(b)
+            relu_v(0, 0, s0)
+            gather_v(1, 0, s1)
+            plus_x("p3", 1, s1, 128)
+            gather_s(2, s2, 128)
+            te(["IB", "C0a"], "p6", mm(T.p6[:, 0:128], T.IB[:], T.C0[:, 0:128], True, False))
+            abs_s("p3", 1, s1, 128)
+            plus_abs(0, 0, 128, [0, s0])
+            minus_z("p2", 64, 96)
             ts(["CU%d" % b for b in range(4)], ["CFE"], T.CFE[:, 2:514:2], T.CU[:], -2048.0, A.add)
-            gather_v(2, 0, 64)
-            relu_v(1, 0, 64)
-            abs_s(2, 64, 128)
-            minus_d(2, 0, 64)
-            plus_abs(1, 0, 128, [0, 64])
-            plus_x(3)
-            if d > 0:
-                for b in range(1, 4):
-                    barred(b)
+            minus_d(1, 0, s1)
+            gather_v(2, 0, s2)
+            relu_v(1, 0, s1)
+            plus_x("p7", 2, s2, 128)
+            places(0, False)
+            gather_s(3, 64, 96)
+            minus_z("p3", 96, 128)
+            gather_s(3, 96, 128)
+            abs_s("p7", 2, s2, 128)
+            minus_d(2, 0, s2)
+            plus_abs(1, 0, 128, [0, s1])
+            places(1, False)
             gather_v(3, 0, 32)
-            relu_v(2, 0, 64)
-            abs_s(3, 64, 96)
-            abs_s(3, 96, 128)
+            relu_v(2, 0, s2)
+            plus_x("p2", 3, 64, 96)
+            abs_s("p2", 3, 64, 96)
             minus_d(3, 0, 32)
-            plus_abs(2, 0, 128, [0, 64])
-            for b in range(3):
-                spread(T.CFE, T.SL, ["CFE", "SL0", "SL1"], b)
-            te(["ZB"], "p4", mm(T.p4[:, 0:192], T.ZB[:, 0:128], T.ZB[:], False, True))
+            plus_x("p3", 3, 96, 128)
+            abs_s("p3", 3, 96, 128)
             gather_v(3, 32, 64)
             relu_v(3, 0, 32)
-            plus_abs(3, 64, 96, [64])
-            minus_d(3, 32, 64)
+            plus_abs(2, 0, 128, [0, s2])
+            places(2, True)
             relu_v(3, 32, 64)
+            minus_d(3, 32, 64)
             plus_abs(3, 0, 32, [0])
-            plus_abs(3, 96, 128, [96])
+            plus_abs(3, 64, 96, [64])
             plus_abs(3, 32, 64, [32])
-            spread(T.CFE, T.SL, ["CFE", "SL0", "SL1"], 3, True)
+            plus_abs(3, 96, 128, [96])
+            places(3, True)
             scan(["p4", "RSA"], ["RA"], T.RA[:], T.RSA[:], T.p4[:, 0:192], 0.0, A.max, A.min)
+            te(stopped + ["IB", "C0b", "BIGI"], "p7", mm(T.p7[:, 0:128], T.IB[:], T.C0[:, 128:256], True, False),
+               *[mm(T.p7[:, 0:128], T.BIGI[:], T[n][:]) for n in stopped])
+            te(stopped + ["BIGI"], "p1", *[mm(T.p1[:, 0:128], T.BIGI[:], T[n][:]) for n in stopped])
             if t == 1 and d == 0:
-                te(["NM0", "BOF"], "p7", mm(T.p7[:, 0:128], T.BOF[:], T.NM0[:], True, True))
-                tt(whole("FA") + ["p7"], whole("FA"), T.FA[:, 0:W:32], T.FA[:, 0:W:32], T.p7[:, 0:128], A.add)
-            te(["IB", "C0", "C0z"], "p6", mm(T.p6[:, 0:272], T.IB[:], T.C0[:], True, False))
-            te(stopped + RN_ALL, "p6", *[mm(T.p6[:, 128:272], T[n][:], T.RN[:]) for n in stopped])
-            te(["IB", "K2K"], "p4", mm(T.p4[:, 0:128], T.IB[:], T.K2K[:, 0:128], True, False))
-            te(stopped + ["BIGI"], "p4", *[mm(T.p4[:, 0:128], T.BIGI[:], T[n][:]) for n in stopped])
-            te(["IB", "KQ", "HI", ss], "p2", mm(T.p2[:, 0:128], T.IB[:], T.KQ[:], True, False),
-               mm(T.p2[:, 0:128], T.HI[:], T[ss][:]))
-            if t == 0:
-                fa_piece("p7")
-                fa_piece("p3")
+                tt(whole("FA") + ["NM0"], whole("FA"), T.FA[:, 0:W:32], T.FA[:, 0:W:32], T.NM0[:], A.add)
 
             scan(["p5", "RSB"], ["RB"], T.RB[:], T.RSB[:], T.p5[:, 0:64], 0.0, A.max, A.min)
             tt(["RA", "RB"], ["MI"], T.MI[:], T.RA[:, 23:192:24], T.RB[:, 7:64:8], A.min)
             ts(["MI", "ZSc"], ["ZS"], T.ZS[:, 0:128:16], T.MI[:], W - 1, A.bitwise_and)
             scan(["ZS", "ZSc", "CEX"], ["YE"], T.YE[:], T.CEX[:], T.ZS[:], 0.0, A.min, A.add)
-            te(["YE", "I160", "I161"], "p6", mm(T.p6[:, 0:256], T.YE[:], T.I16[:]))
-            tt(["YE", "pC"], ["YM"], T.YM[:], T.YE[:], M16P, A.mult)
-            te(["YM"] + RC_ALL, "p6", mm(T.p6[:, 0:272], T.YM[:], T.RC[:], False, True))
-            te(["YE", "I160"], "p4", mm(T.p4[:, 0:128], T.I16[:, 0:128], T.YE[:]))
-            ts(["p6"], ["YU"], T.YU[:], T.p6[:, 256:264], 2048.0, A.add)
+            for bank, stop in (("p7", True), ("p6", True), ("p1", False)):
+                te(["YE", "I16"], bank, mm(T[bank][:, 0:128], T.YE[:], T.I16[:], False, stop))
+            te(["IB", "KQa", "HI", ss], "p2", mm(T.p2[:, 0:128], T.IB[:], T.KQ[:, 0:128], True, False),
+               mm(T.p2[:, 0:128], T.HI[:], T[ss][:]))
+            te(["IB", "C0b"], "p4", mm(T.p4[:, 0:128], T.IB[:], T.C0[:, 128:256], True, False))
+            scan(["p7", "CPL", "PYc"], ["PY"], T.PY[:, 1:129], T.CPL[:], T.p7[:, 0:128], -1.0, A.max, A.min)
+            ts(["PY"], ["YU"], T.YU[:], T.PY[:, 16:129:16], W - 1.0, A.min)
             act(whole(far) + ["YU"], ["TK"], T.TK[:], F[:, 0:W].indirect(T.YU[:]), AF.Relu, bias=1.0)
             act(["X", "YU"], ["XG"], T.XG[:], T.X[:, 0:W].indirect(T.YU[:]))
-            ts(["p6"], ["EQ7"], T.EQ[:, 896:1024], T.p6[:, 128:256], 0.0, A.is_equal)
-            te(["EQ7", "RNa"], "p4", mm(T.p4[:, 0:128], T.EQ[:, 896:1024], T.RN[:, 0:128]))
+            tt(["p6", "PY", "PYc"], ["EQ7"], T.EQ[:, 896:1024], T.p6[:, 0:128], T.PY[:, 0:128], A.is_equal)
+            te(["EQ7", "BOBIG"], "p1", mm(T.p1[:, 0:128], T.BOBIG[:], T.EQ[:, 896:1024]))
             for h in range(7):
-                lo = 16 * h + 16
-                ts(["p6"], ["EQ%d" % h], T.EQ[:, 128 * h + lo:128 * h + 128], T.p6[:, lo:128], T.p6[:, 264 + h:265 + h],
-                   A.is_equal)
-                if h == 3:
-                    te(["TK", "RNa"], "p4", mm(T.p4[:, 0:128], T.TK[:], T.RN[:, 0:128]))
-                te(["EQ%d" % h, "RNa"], "p4",
-                   mm(T.p4[:, 0:128], T.EQ[:, 128 * h:128 * h + 128], T.RN[:, 0:128], False, h == 6))
-            te(["XG", "HI"], "p2", mm(T.p2[:, 0:128], T.HI[:], T.XG[:], False, True))
-            act(["p2"], ["NRF"], T.NRF[:], T.p2[:, 0:128], bias=MAGIC)
-            act(["NRF"], ["NR"], T.NR[:], T.NRF[:], bias=-MAGIC)
-            yp, wx = "YP%d" % d, "WX%d" % d
-            tt(["p4", "DM"], [yp], T[yp][:], T.p4[:, 0:128], T.DM[:], A.min)
-            te([yp, "SEL8"], "p1", mm(T.p1[:, 0:8], T[yp][:], T.SEL8[:], True, True))
-            tt([yp, "pC"], [wx], T[wx][:], T[yp][:], TWON, A.is_lt)
+                lo = 16 * h + 17
+                e = T.EQ[:, 128 * h + lo:128 * h + 128]
+                ts(["p6", "PY"], ["EQ%d" % h], e, T.p6[:, lo:128], T.PY[:, 16 * h + 16:16 * h + 17], A.is_equal)
+                if h == 5:
+                    te(["TK", "BIGI"], "p1", mm(T.p1[:, 0:128], T.BIGI[:], T.TK[:]))
+                te(["EQ%d" % h, "BOBIG"], "p1", mm(T.p1[:, lo:128], T.BOBIG[:], e, False, h == 6))
+            te(["XG", "HI", "IB", "KM"], "p2", mm(T.p2[:, 0:128], T.HI[:], T.XG[:]),
+               mm(T.p2[:, 0:128], T.IB[:], T.KM[:], False, True))
+            act(["p2"], ["NR"], T.NR[:], T.p2[:, 0:128], bias=-MAGIC)
+            if first:
+                late_constants()
+            scan(["p1", "CPL"], ["PP"], T.PP[:], T.CPL[:], T.p1[:, 0:128], -1.0, A.max, A.min)
             k = D * t + d
-            mp = "MP%d" % k
+            mp, sg = "MP%d" % k, "SG%d" % d
             sl = T.MP[:, 8 * k:8 * k + 8]
-            cp(["p1"], [mp], sl, T.p1[:, 0:8])
+            cp(["PP"], [mp], sl, T.PP[:, 15:128:16])
 
             def far_write():
                 cp([mp, st, far + "spare"], whole(far), F[:, 0:WX].indirect(sl), T[st][:])
@@ -517,13 +502,24 @@ def rank_program(g, core, T, topo):
             def rec_write():
                 cp([mp, "NR", "Xspare"], ["X"], T.X[:, 0:WX].indirect(sl), T.NR[:])
 
+            def winners():
+                te(["PP", "IDF"], "p4", mm(T.p4[:, 0:128], T.IDF[:], T.PP[:], False, True))
+                act(["p4"], ["WV"], T.WV[:], T.p4[:, 0:128], AF.Relu, scale=-1.0, bias=W + 2048.0)
+                act(["WV"], [sg, "CT"], T[sg][:], T.WV[:], AF.Sign, accum_out=T.CT[:])
+
             def count():
-                act([wx], ["CT", "WD"], T.WD[:], T[wx][:], accum_out=T.CT[:])
-                te(["CT", "ONF"], "p1", mm(T.p1[:, 0:1], T.ONF[:], T.CT[:], True, True))
+                te(["CT", "ONF"], "p5", mm(T.p5[:, 0:1], T.ONF[:], T.CT[:], True, True))
+
+            def pairings():
+                te([sg, "WV", "BO4K", "BOB", "NBO"], "p8", mm(T.p8[:, 0:128], T.NBO[:], T.WV[:], d == 0, False),
+                   mm(T.p8[:, 0:128], T.BO4K[:], T[sg][:]), mm(T.p8[:, 0:128], T.BOB[:], T[sg][:], False, d == D - 1))
+                if d == D - 1:
+                    act(["p8"], ["NN%d" % t], T["NN%d" % t][:], T.p8[:, 0:128])
+                    send("N%d" % t, home, T["NM%d" % t][:], T["NN%d" % t][:], ["NN%d" % t], "NM%d" % t)
 
             def kappa(step):
                 if step == 0:
-                    cp(["p1"], ["KJ0"], T.KJ[:, 0:1], T.p1[:, 0:1])
+                    cp(["p5"], ["KJ0"], T.KJ[:, 0:1], T.p5[:, 0:1])
                 elif step == 1:
                     ts(["KJ0"], ["KJ1"], T.KJ[:, 1:2], T.KJ[:, 0:1], 31, A.bitwise_and)
                 else:
@@ -531,60 +527,56 @@ def rank_program(g, core, T, topo):
                     e = (d + 1) % D
                     act(["KF", "KB%d" % e], ["KC"], T.KC[:], T.KB[:, 4 * e:4 * e + 4], AF.Identity, bias=T.KF[:])
 
-            def pairings():
-                te(["ND3", "IDF"], "p7", mm(T.p7[:, 0:128], T.ND3[:], T.IDF[:], True, False))
-                for e in range(D):
-                    te(["WX%d" % e, "YP%d" % e, "D4K", "DQ1", "IDF"], "p7",
-                       mm(T.p7[:, 0:128], T["WX%d" % e][:], T.D4K[:]), mm(T.p7[:, 0:128], T["WX%d" % e][:], T.DQ1[:]),
-                       mm(T.p7[:, 0:128], T["YP%d" % e][:], T.IDF[:], False, e == D - 1))
-                act(["p7"], ["NN%d" % t], T["NN%d" % t][:], T.p7[:, 0:128])
-                send("N%d" % t, home, T["NM%d" % t][:], T["NN%d" % t][:], ["NN%d" % t], "NM%d" % t)
-
             if d < D - 1:
                 kk = (D - 1) * t + d
                 ur, up = T.UR[:, 128 * kk:128 * kk + 128], T.UP[:, 8 * k:8 * k + 8]
                 send("R%d%d" % (t, d), to, ur, T.NR[:], ["NR"], "UR%d" % kk)
                 send("P%d%d" % (t, d), to, up, sl, [mp], "UP%d" % k)
+                act(["p6"], ["YRS"], T.YRS[:], T.p6[:, 0:128])
+                winners()
                 count()
                 far_write()
-                act(["p6"], ["YRS"], T.YRS[:], T.p6[:, 0:128], bias=2048.0)
                 act(whole(far) + ["YU"], ["PGR"], T.PGR[:], F[:, 0:W].indirect(T.YU[:]))
                 te(["YRS", "IL0", "IL1"], "p6", *[
                     mm(T.p6[:, 0:64], T.IL[:, 128 * e:128 * e + 128], T.YRS[:, e:128:2], e == 0, e == 1) for e in range(2)])
-                kappa(0)
+                pairings()
                 rec_write()
+                scan(["PGR", "CPK"], ["PS"], T.PS[:], T.CPK[:], T.PGR[:], -BIG, A.add, A.min)
+                kappa(0)
+                ts(["PS", "PG4"], ["PU"], T.PU[:], T.PS[:, 15:128:16], T.PG[:, 4:5], A.add)
                 kappa(1)
-                scan(["PGR", "pC"], ["PS"], T.PS[:], CPK, T.PGR[:], -BIG, A.add, A.min)
-                kappa(2)
-                ts(["PS", "PG7"], ["PU"], T.PU[:], T.PS[:, 15:128:16], T.PG[:, 7:8], A.add)
                 if t == 0:
                     fa_piece("p7")
                     fa_piece("p3")
                 cp(["UR%d" % kk, "UP%d" % k, xr + "spare"], [xr], XR[:, 0:WX].indirect(up), ur)
+                kappa(2)
                 cp([xr, "PU"], ["Z"], T.Z[:], XR[:, 0:W].indirect(T.PU[:]))
             elif t == 0:
                 rec_write()
                 cp(["X"], ["SN1"], T.SN1[:], T.X[:, 1:W:32])
                 send("S1", prv, T.SS1[:], T.SN1[:], ["SN1"], "SS1")
+                winners()
                 count()
                 far_write()
-                kappa(0)
-                tt(whole("FB") + ["pC"], ["LT"], T.LT[:], T.FB[:, 1:W:32], TFREE, A.is_gt)
-                kappa(1)
-                te(["LT", "IB"], "p3", mm(T.p3[:, 0:128], T.LT[:], T.IB[:], True, True))
-                kappa(2)
-                act(["p3"], ["NH1"], T.NH1[:], T.p3[:, 0:128])
-                send("L1", prv, T.NL1[:], T.NH1[:], ["NH1"], "NL1")
                 pairings()
+                kappa(0)
+                tt(whole("FB") + ["TFREE"], ["NH1"], T.NH1[:], T.FB[:, 1:W:32], T.TFREE[:], A.is_gt)
+                kappa(1)
+                send("L1", prv, T.NL1[:], T.NH1[:], ["NH1"], "NL1")
+                kappa(2)
                 send("X1", prv, T.XR1[:, 0:W], T.X[:, 0:W], ["X"], "XR1")
+                fa_piece("p7")
+                fa_piece("p3")
+                fa_piece("p2")
+                fa_piece("p7")
             else:
                 rec_write()
-                dma("Y", "oX", [(T.yx[:], T.X[:, 0:W])], ["X"], ["yx"])
+                winners()
                 pairings()
+                dma("Y", "oX", [(T.yx[:], T.X[:, 0:W])], ["X"], ["yx"])
                 far_write()
                 dma("Y", "oA", [(T.ya[:], T.FA[0:128:16, 0:W])], whole("FA"), ["ya"])
 
-    te(["NM1", "BOF"], "p7", mm(T.p7[:, 0:128], T.BOF[:], T.NM1[:], True, True))
-    tt(whole("FB") + ["p7"], whole("FB"), T.FB[:, 1:W:32], T.FB[:, 1:W:32], T.p7[:, 0:128], A.add)
+    tt(whole("FB") + ["NM1"], whole("FB"), T.FB[:, 1:W:32], T.FB[:, 1:W:32], T.NM1[:], A.add)
     dma("Y", "oB", [(T.yb[:], T.FB[0:128:16, 0:W])], whole("FB"), ["yb"])
     finish()

@@ -16,19 +16,19 @@ for _names, _cols, _dt in (
         ("X XR0 XR1", WX, BF), ("FA FB", WX, F32),
         ("PA2 PB2", 256, I32), ("PA2H PB2H", 256, F16), ("FT", 2048, F16),
         ("WTI", 1, I32), ("WI", 2, I32), ("WF", 2, F32), ("WM", 1024, BF),
-        ("PI", 2, I32), ("PX", 6, I32), ("PF", 6, F32), ("PG", 8, F32),
-        ("CI CMI CGI CI8 ZS", 128, I32), ("SLI", 64, I32),
-        ("M16 IDF NBO ONF CEX CY CIW CPL CPK TFREE ST0 ST1", 128, F32), ("IL CP", 256, F32),
-        ("BOB BO4K BOBIG IB NIB HI BIGI KM", 128, BF), ("K2K KQ", 192, BF), ("GM", 16, BF),
-        ("BO16 I16", 128, F16), ("C0", 256, BF), ("SL", 128, F16), ("NS", 128, BF),
-        ("RSA RSA0 RA", 192, F32), ("RSB RSB0 RB", 64, F32), ("BJ0 BJ BJ2 KC", 4, F32), ("KB", 12, F32),
-        ("SN0 SN1 SS0 SS1 NH0 NH1 NL0 NL1 Z", 128, BF), ("NN0 NN1 NM0 NM1", 128, F32),
+        ("PI", 2, I32), ("PX", 5, I32), ("PF", 5, F32), ("PG", 8, F32),
+        ("CI CGI CI8 ZS", 128, I32), ("SLI", 64, I32), ("SL9 RB", 72, I32), ("IOT", WX, F32), ("CMI", 144, I32),
+        ("IDF ONF CEX CY CIW CPL CPK ST0 ST1", 128, F32), ("IL", 256, F32), ("CP", 256, BF), ("M16", 144, F32),
+        ("BOB BOBIG IB NIB HI BIGI KM", 128, BF), ("K2K KQ", 192, BF), ("GM", 16, BF), ("K9", 72, BF),
+        ("BO16 I16", 128, F16), ("C0", 256, BF), ("SL", 272, F16), ("NS", 272, BF),
+        ("RSB", 72, F32), ("BJ0 BJ BJ2 KC", 4, F32), ("KB", 12, F32),
+        ("SN0 SN1 SS0 SS1 NH0 NH1 NL0 NL1 Z", 128, BF),
         ("ZR", 1024, BF), ("SQ", 256, F32), ("AI CC", 256, I32), ("CU", 256, U16),
         ("CFE", 528, F16), ("NQE", 528, BF), ("DD GS AB", W, BF),
-        ("MI", 8, I32), ("YE", 128, F16), ("PY", 136, F32), ("YU PU", 8, U16), ("EQ", 1024, BF),
-        ("TK XG NR", 128, BF), ("YRS PGR PS PP WV", 128, F32), ("SG0 SG1 SG2", 128, BF),
+        ("YE", 128, F16), ("PY", 136, F32), ("YU PU", 8, U16), ("EQ", 1024, BF),
+        ("TK XG", 128, BF), ("YRS PGR PS PP", 128, F32), ("SG0 SG1 SG2", 128, BF),
         ("CT KF", 1, F32), ("KJ", 2, I32),
-        ("MP", 8 * TB * D, U16), ("UP", 8 * TB * D, U16), ("UR", 128 * TB * (D - 1), BF)):
+        ("MP NM", 8 * TB * D, U16), ("MU", 136, U16), ("UL", 136 * TB * (D - 1), U16)):
     for _n in _names.split():
         SCRATCH[_n] = ("sbuf", [128, _cols], _dt)
 SCRATCH["P8"] = ("sbuf", [8, W], I32)
@@ -37,8 +37,8 @@ SCRATCH["E8"] = ("sbuf", [8, 128], BF)
 for _n in range(1, 9):
     SCRATCH["p%d" % _n] = ("psum", [128, 512], F32)
 
-REMOTE = ["S0", "X0", "L0", "S1", "X1", "L1", "N0", "N1"] + [k + "%d%d" % (t, d) for k in "RP" for t in range(TB)
-                                                             for d in range(D - 1)]
+REMOTE = ["S0", "X0", "L0", "S1", "X1", "L1", "N0", "N1", "N2"]
+REMOTE += ["U%d%d" % (t, d) for t in range(TB) for d in range(D - 1)]
 LOCAL = ["dW", "dP8", "dX", "dPB", "dPA", "oX", "oA", "oB"]
 SEMAPHORES = ["qV", "qS", "qT", "qG"] + ["a" + n for n in REMOTE] + ["l" + n for n in REMOTE] + LOCAL
 
@@ -177,13 +177,13 @@ def rank_program(g, core, T, topo):
         op("T", reads, [bank], *fns)
 
     dma("Y", "dP8", [(T.P8[:], T.pa[:])], [], ["P8"])
-    dma("Y", "dPB", [(T.PB2[:], T.pb[:])], [], ["PB2"])
     dma("Y", "dW", [(T.WTI[:], T.wt[:])], [], ["WTI"])
     dma("Y", "dX", [(T.X[:, 0:W], T.x[:])], [], ["X"])
+    dma("Y", "dPB", [(T.PB2[:], T.pb[:])], [], ["PB2"])
     dma("Y", "dPA", [(T.PA2[:], T.pa[:])], [], ["PA2"])
 
     iota("PI", [[1, 2]], 0, 1)
-    iota("CMI", [[0, 8], [1, 16]], 0, 0)
+    iota("CMI", [[0, 9], [1, 16]], 0, 0)
     iota("CGI", [[1, 8], [0, 16]], 0, 0)
     iota("CI", [[1, 128]], 0, 0)
     iota("CI8", [[1, 16], [0, 8]], 0, 0)
@@ -194,14 +194,12 @@ def rank_program(g, core, T, topo):
     ts(["PI"], ["PX2"], T.PX[:, 2:3], p, 4, A.logical_shift_right)
     ts(["PI"], ["PX3"], T.PX[:, 3:4], p, 7, A.bitwise_and)
     ts(["PI"], ["PX4"], T.PX[:, 4:5], p, 3, A.logical_shift_right, 1, A.bitwise_and)
-    ts(["PI"], ["PX5"], T.PX[:, 5:6], T.PI[:, 1:2], 15, A.bitwise_and)
     fill(["K2K"], T.K2K[:], 2048.0)
-    cp(["PX%d" % k for k in range(6)], ["PF"], T.PF[:], T.PX[:])
+    cp(["PX%d" % k for k in range(5)], ["PF"], T.PF[:], T.PX[:])
     fill(["C0a"], T.C0[:, 0:128], 2048.0)
-    fill(["KQa"], T.KQ[:, 0:128], -0.25)
     fill(["KQ"], T.KQ[:, 128:192], 0.5)
     fill(["KM"], T.KM[:], MAGIC)
-    P_, PM, PGc, PJ, PL, PM1 = [T.PF[:, k:k + 1] for k in range(6)]
+    P_, PM, PGc, PJ, PL = [T.PF[:, k:k + 1] for k in range(5)]
     ts(["CMI", "PF"], ["M16"], T.M16[:], T.CMI[:], PM, A.is_equal)
     ts(["CGI", "PF"], ["BO16"], T.BO16[:], T.CGI[:], PGc, A.is_equal)
     ts(["CGI", "PF"], ["E8"], T.E8[:], T.CGI[0:8, :], T.PF[0:8, 0:1], A.is_equal)
@@ -212,23 +210,19 @@ def rank_program(g, core, T, topo):
     ts(["PF"], ["PG4"], T.PG[:, 4:5], PM, 15.0, A.is_lt, BIG, A.mult)
     ts(["P8"], ["LV8"], T.LV8[:], T.P8[:, 0:W:32], 0.0, A.is_ge)
     te(["E8", "LV8"], "p7", mm(T.p7[:, 0:128], T.E8[:], T.LV8[:], True, True))
-    ts(["PB2"], ["PB2H"], T.PB2H[:], T.PB2[:], -2047.0, A.add)
-    tt(["p7", "M16"], ["NH0"], T.NH0[:], T.p7[:, 0:128], T.M16[:], A.mult)
+    cp(["p7"], ["NH0"], T.NH0[:], T.p7[:, 0:128])
     send("L0", nxt, T.NL0[:], T.NH0[:], ["NH0"], "NL0")
     iota("BJ0", [[256, 4]], 16, 0, True)
     iota("SLI", [[-16, 8], [-1, 8]], 0, 1)
-    iota("RSA0", [[0, 8], [1, 24]], 0, 0, True)
-    iota("RSB0", [[0, 8], [1, 8]], 0, 0, True)
+    iota("SL9", [[-16, 8], [-1, 9]], 1, 1)
     iota("CEX", [[0, 8], [30000, 16]], -2048, 0, True)
     iota("CIW", [[1, 128]], W, 0, True)
     iota("ST0", [[32, 128]], 0, 0, True)
     for name, scale in (("IB", 1.0), ("NIB", -1.0), ("HI", 0.5), ("BIGI", BIG)):
         act(["IDF"], [name], T[name][:], T.IDF[:], scale=scale)
-    act(["M16"], ["C0b"], T.C0[:, 128:256], T.M16[:], scale=-4 * BIG, bias=4 * BIG + 2048)
-    act(["M16"], ["CY"], T.CY[:], T.M16[:], scale=LOW, bias=-LOW)
-    act(["M16"], ["TFREE"], T.TFREE[:], T.M16[:], scale=-BIG - 0.5, bias=BIG)
-    for name, scale in (("BOBIG", BIG), ("BO4K", float(W)), ("NBO", -1.0)):
-        act(["BOB"], [name], T[name][:], T.BOB[:], scale=scale)
+    act(["M16"], ["C0b"], T.C0[:, 128:256], T.M16[:, 0:128], scale=-4 * BIG, bias=4 * BIG + 2048)
+    act(["M16"], ["CY"], T.CY[:], T.M16[:, 0:128], scale=LOW, bias=-LOW)
+    act(["BOB"], ["BOBIG"], T.BOBIG[:], T.BOB[:], scale=BIG)
     act(["IDF", "PG3"], ["IL0"], T.IL[:, 0:128], T.IDF[:], scale=T.PG[:, 3:4])
     act(["IDF", "PF"], ["IL1"], T.IL[:, 128:256], T.IDF[:], scale=PL)
     for k in range(16):
@@ -240,6 +234,8 @@ def rank_program(g, core, T, topo):
             mm(T[bank][:, 256 * e:256 * e + 256], T.FT[:, 128 * (2 * c + e):128 * (2 * c + e + 1)], src[:], True, True)
             for e in range(2)])
         out = T[name][:, 512 * c:512 * c + 512]
+        if on == "later":
+            return lambda: act([bank], [name + str(c)], out, T[bank][:, 0:512], bias=2047.0)
         if on == "S":
             act([bank], [name + str(c)], out, T[bank][:, 0:512], bias=2047.0)
         else:
@@ -248,8 +244,6 @@ def rank_program(g, core, T, topo):
     def whole(name):
         return [name + str(c) for c in range(8)]
 
-    for c in range(7):
-        table("FB", c, ("p2", "p3", "p4", "p5")[c % 4], "S")
     ts(["WTI"], ["WI0"], T.WI[:, 0:1], T.WTI[:], 4032, A.bitwise_and)
     ts(["WTI"], ["WI1"], T.WI[:, 1:2], T.WTI[:], 63, A.bitwise_and)
     ts(["BJ0", "PG2"], ["BJ"], T.BJ[:], T.BJ0[:], T.PG[:, 2:3], A.add)
@@ -264,38 +258,51 @@ def rank_program(g, core, T, topo):
     cp(["NQE"], ["CFE"], T.CFE[:], T.NQE[:])
     ts(["CI", "PF"], ["GMa"], T.GM[:, 0:8], T.CI[:, 0:8], PGc, A.is_equal, float(W), A.mult)
     ts(["CI", "PF"], ["GMb"], T.GM[:, 8:16], T.CI[:, 0:8], PGc, A.is_equal, -float(W), A.mult)
-    for e in range(2):
-        ts(["SLI"], ["SL%d" % e], T.SL[:, 64 * e:64 * e + 64], T.SLI[:], 8.0 * e, A.is_equal)
-        ts(["SLI"], ["NS%d" % e], T.NS[:, 64 * e:64 * e + 64], T.SLI[:], 8.0 * e, A.is_equal, -FULL, A.mult)
+    for e in range(4):
+        src, c = ("SLI", slice(64 * e, 64 * e + 64)) if e < 2 else ("SL9", slice(72 * e - 16, 72 * e + 56))
+        ts([src], ["SL%d" % e], T.SL[:, c], T[src][:], 8.0 * (e % 2), A.is_equal)
+        ts([src], ["NS%d" % e], T.NS[:, c], T[src][:], 8.0 * (e % 2), A.is_equal, -FULL, A.mult)
+
+    def const(writes, ap, c, reads=()):
+        act(["IDF"] + list(reads), writes, ap, T.IDF[:, 0:ap.shape[1]], scale=0.0, bias=c)
+
+    const(["K9a"], T.K9[:], 2048.0)
+    const(["KQa"], T.KQ[:, 0:128], -0.25)
+    const(["PYc"], T.PY[:, 0:1], -1.0)
+    const(["RSBc"], T.RSB[:], -5.0e7)
+    const(["ONF"], T.ONF[:], 1.0 / 16)
+    const(["K9"], T.K9[:, 0:72:9], -2 * FULL, ["K9a"])
+    for n in ("X", "FB", "XR0", "XR1", "FA", "IOT"):
+        const([n + "spare"], T[n][:, W:WX], 0.0)
+    act(["M16"], ["CPA"], T.CP[:, 0:128], T.M16[:, 0:128], scale=4 * BIG)
+    act(["M16"], ["CPB"], T.CP[:, 128:256], T.M16[:, 15:143], scale=-BIG)
+    te(["IB", "CPA", "CPB"], "p6", mm(T.p6[:, 0:128], T.IB[:], T.CP[:, 0:128], True, False),
+       mm(T.p6[:, 0:128], T.IB[:], T.CP[:, 128:256], False, True))
+    te(["IDF", "CY", "CIW"], "p1", mm(T.p1[:, 0:128], T.IDF[:], T.CY[:], True, False),
+       mm(T.p1[:, 0:128], T.IDF[:], T.CIW[:], False, True))
+    act(["p6"], ["CPK"], T.CPK[:], T.p6[:, 0:128])
+    act(["p1"], ["CPL"], T.CPL[:], T.p1[:, 0:128])
     cp(["X"], ["SN0"], T.SN0[:], T.X[:, 0:W:32])
     send("S0", nxt, T.SS0[:], T.SN0[:], ["SN0"], "SS0")
     send("X0", nxt, T.XR0[:, 0:W], T.X[:, 0:W], ["X"], "XR0")
     iota("ST1", [[32, 128]], 1, 0, True)
-    act(["RSA0"], ["RSA"], T.RSA[:], T.RSA0[:], scale=-1.0e8, bias=5.0e7)
-    act(["RSB0"], ["RSB"], T.RSB[:], T.RSB0[:], scale=-1.0e8, bias=5.0e7)
-    table("FB", 7, "p5", "V")
+    op("G", [], ["IOT"], lambda: g.iota(T.IOT[:, 0:W], [[1, W]], 1, 0, allow_small_or_imprecise_dtypes=True))
     fill(["ZSc"], T.ZS[:], 0)
-    fill(["PYc"], T.PY[:, 0:1], -1.0)
-    for n in ("X", "FB"):
-        fill([n + "spare"], T[n][:, W:WX], 0.0)
     cp(["IDF"], ["I16"], T.I16[:], T.IDF[:])
-    tt(["CY", "CIW"], ["CPL"], T.CPL[:], T.CY[:], T.CIW[:], A.add)
-
-    def late_constants():
-        for n in ("XR0", "XR1", "FA"):
-            fill([n + "spare"], T[n][:, W:WX], 0.0)
-        fill(["ONF"], T.ONF[:], 1.0)
-        ts(["CMI", "PF"], ["CPA"], T.CP[:, 0:128], T.CMI[:], PM, A.is_equal, 4 * BIG, A.mult)
-        ts(["CMI", "PF"], ["CPB"], T.CP[:, 128:256], T.CMI[:], PM1, A.is_equal, -BIG, A.mult)
-        ts(["PA2"], ["PA2H"], T.PA2H[:], T.PA2[:], -2047.0, A.add)
-        tt(["CPA", "CPB"], ["CPK"], T.CPK[:], T.CP[:, 0:128], T.CP[:, 128:256], A.add)
+    ts(["PB2"], ["PB2H"], T.PB2H[:], T.PB2[:], -2047.0, A.add)
+    for c in range(5):
+        table("FB", c, ("p2", "p3", "p4", "p5", "p7")[c], "V" if c in (1, 3) else "S")
 
     zr_all = ["ZR%d" % m for m in range(8)]
-    fa_left = list(range(8))
+    pieces = [("FB", c) for c in range(5, 8)] + [("FA", c) for c in range(8)]
 
-    def fa_piece(bank):
-        if fa_left:
-            table("FA", fa_left.pop(0), bank, "S")
+    def piece(bank):
+        if pieces:
+            table(*pieces.pop(0), bank, "S")
+
+    def near(name, k, msg):
+        c = T[name][:, k // D:W:32]
+        tt(whole(name) + ["IOT", "IOTspare", msg], whole(name), c, T.IOT[:].indirect(T.NM[:, 8 * k:8 * k + 8]), c, A.add)
 
     for t in range(TB):
         far = "FB" if t == 0 else "FA"
@@ -341,7 +348,7 @@ def rank_program(g, core, T, topo):
             def keys(b, lo, hi, j):
                 if b < 3:
                     return T.p4[lo:hi, 3 * j + b:192:24]
-                return T.p5[lo:hi, j:64:8]
+                return T.p5[lo:hi, j + 1:72:9]
 
             def kbank(b):
                 return "p4" if b < 3 else "p5"
@@ -382,22 +389,22 @@ def rank_program(g, core, T, topo):
                     T[bank][:, 0:8 * (hi - lo)], AF.Abs)
 
             def spread(src, sel, names, b, stop=False):
-                out = T.p4[:, b:192:3] if b < 3 else T.p5[:, 0:64]
+                out, o, n = (T.p4[:, b:192:3], 0, 64) if b < 3 else (T.p5[:, 0:72], 128, 72)
                 te(names, kbank(b), *[
-                    mm(out, src[:, 2 - e + 128 * b:130 - e + 128 * b], sel[:, 64 * e:64 * e + 64], False, stop and e == 1)
-                    for e in range(2)])
+                    mm(out, src[:, 2 - e + 128 * b:130 - e + 128 * b], sel[:, o + n * e:o + n * e + n], False,
+                       stop and e == 1) for e in range(2)])
 
             def barred(b):
                 if d > 0:
                     tt(["CC%d" % b, "p6"], ["NQE%d" % b], T.NQE[:, 2 + 128 * b:130 + 128 * b:2],
                        T.CC[:, 64 * b:64 * b + 64], T.p6[:, 0:64], A.not_equal)
-                    spread(T.NQE, T.NS, ["NQE", "NQE%d" % b, "NS0", "NS1"], b)
+                    spread(T.NQE, T.NS, ["NQE", "NQE%d" % b] + ["NS%d" % e for e in range(4)], b)
 
             def places(b, stop):
-                spread(T.CFE, T.SL, ["CFE", "SL0", "SL1"], b, stop)
+                spread(T.CFE, T.SL, ["CFE"] + ["SL%d" % e for e in range(4)], b, stop)
 
             te(["IB", "K2K"], "p4", mm(T.p4[:, 0:192], T.IB[:], T.K2K[:], True, False))
-            te(["IB", "K2K"], "p5", mm(T.p5[:, 0:64], T.IB[:], T.K2K[:, 0:64], True, False))
+            te(["IB", "K9"], "p5", mm(T.p5[:, 0:72], T.IB[:], T.K9[:], True, False))
             s0, s1, s2 = SPLIT
             minus_z("p2", s0, 128)
             minus_z("p3", s1, 128)
@@ -411,6 +418,7 @@ def rank_program(g, core, T, topo):
             gather_s(0, s0, 128)
             gather_v(0, 0, s0)
             te(["IB", "C0b"], "p1", mm(T.p1[:, 0:128], T.IB[:], T.C0[:, 128:256], True, False))
+            early = table(*pieces.pop(0), "p8", "later") if pieces else None
             plus_x("p2", 0, s0, 128)
             gather_s(1, s1, 128)
             abs_s("p2", 0, s0, 128)
@@ -445,34 +453,42 @@ def rank_program(g, core, T, topo):
             minus_d(3, 0, 32)
             plus_x("p3", 3, 96, 128)
             abs_s("p3", 3, 96, 128)
+            if early:
+                early()
             gather_v(3, 32, 64)
             relu_v(3, 0, 32)
             plus_abs(2, 0, 128, [0, s2])
             places(2, True)
             relu_v(3, 32, 64)
             minus_d(3, 32, 64)
-            plus_abs(3, 0, 32, [0])
-            plus_abs(3, 64, 96, [64])
-            plus_abs(3, 32, 64, [32])
-            plus_abs(3, 96, 128, [96])
+            plus_abs(3, 0, 128, [0, 32, 64, 96])
             places(3, True)
-            scan(["p4", "RSA"], ["RA"], T.RA[:], T.RSA[:], T.p4[:, 0:192], 0.0, A.max, A.min)
+            for e in range(8):
+                op("V", ["p4", "RSBc"], ["RSB%d" % e], lambda: V.tensor_reduce(
+                    T.RSB[:, 9 * e + 1:9 * e + 2], T.p4[:, 24 * e:24 * e + 24], AxisListType.X, A.min))
             te(stopped + ["IB", "C0b", "BIGI"], "p7", mm(T.p7[:, 0:128], T.IB[:], T.C0[:, 128:256], True, False),
                *[mm(T.p7[:, 0:128], T.BIGI[:], T[n][:]) for n in stopped])
             te(stopped + ["BIGI"], "p1", *[mm(T.p1[:, 0:128], T.BIGI[:], T[n][:]) for n in stopped])
-            if t == 1 and d == 0:
-                tt(whole("FA") + ["NM0"], whole("FA"), T.FA[:, 0:W:32], T.FA[:, 0:W:32], T.NM0[:], A.add)
+            piece("p3")
+            if first:
+                piece("p2")
+            late = {(1, 0): [("FA", e, "N0") for e in range(D)], (1, 2): [("FB", D + e, "N1") for e in range(D - 1)]}
+            late = late.get((t, d), [])
 
-            scan(["p5", "RSB"], ["RB"], T.RB[:], T.RSB[:], T.p5[:, 0:64], 0.0, A.max, A.min)
-            tt(["RA", "RB"], ["MI"], T.MI[:], T.RA[:, 23:192:24], T.RB[:, 7:64:8], A.min)
-            ts(["MI", "ZSc"], ["ZS"], T.ZS[:, 0:128:16], T.MI[:], W - 1, A.bitwise_and)
+            scan(["p5", "RSBc"] + ["RSB%d" % e for e in range(8)], ["RB"], T.RB[:], T.RSB[:], T.p5[:, 0:72], 0.0, A.max, A.min)
+            ts(["RB", "ZSc"], ["ZS"], T.ZS[:, 0:128:16], T.RB[:, 8:72:9], W - 1, A.bitwise_and)
             scan(["ZS", "ZSc", "CEX"], ["YE"], T.YE[:], T.CEX[:], T.ZS[:], 0.0, A.min, A.add)
+            if first:
+                ts(["PA2"], ["PA2H"], T.PA2H[:], T.PA2[:], -2047.0, A.add)
+            for e in late[:2]:
+                near(*e)
             for bank, stop in (("p7", True), ("p6", True), ("p1", False)):
                 te(["YE", "I16"], bank, mm(T[bank][:, 0:128], T.YE[:], T.I16[:], False, stop))
             te(["IB", "KQa", "HI", ss], "p2", mm(T.p2[:, 0:128], T.IB[:], T.KQ[:, 0:128], True, False),
                mm(T.p2[:, 0:128], T.HI[:], T[ss][:]))
-            te(["IB", "C0b"], "p4", mm(T.p4[:, 0:128], T.IB[:], T.C0[:, 128:256], True, False))
             scan(["p7", "CPL", "PYc"], ["PY"], T.PY[:, 1:129], T.CPL[:], T.p7[:, 0:128], -1.0, A.max, A.min)
+            for e in late[2:]:
+                near(*e)
             ts(["PY"], ["YU"], T.YU[:], T.PY[:, 16:129:16], W - 1.0, A.min)
             act(whole(far) + ["YU"], ["TK"], T.TK[:], F[:, 0:W].indirect(T.YU[:]), AF.Relu, bias=1.0)
             act(["X", "YU"], ["XG"], T.XG[:], T.X[:, 0:W].indirect(T.YU[:]))
@@ -487,35 +503,27 @@ def rank_program(g, core, T, topo):
                 te(["EQ%d" % h, "BOBIG"], "p1", mm(T.p1[:, lo:128], T.BOBIG[:], e, False, h == 6))
             te(["XG", "HI", "IB", "KM"], "p2", mm(T.p2[:, 0:128], T.HI[:], T.XG[:]),
                mm(T.p2[:, 0:128], T.IB[:], T.KM[:], False, True))
-            act(["p2"], ["NR"], T.NR[:], T.p2[:, 0:128], bias=-MAGIC)
-            if first:
-                late_constants()
             scan(["p1", "CPL"], ["PP"], T.PP[:], T.CPL[:], T.p1[:, 0:128], -1.0, A.max, A.min)
+            ts(["p2"], ["NR"], T.MU[:, 0:128], T.p2[:, 0:128], -MAGIC, A.add)
             k = D * t + d
-            mp, sg = "MP%d" % k, "SG%d" % d
-            sl = T.MP[:, 8 * k:8 * k + 8]
+            mp, sg = "ML", "SG%d" % d
+            sl = T.MU[:, 128:136]
             cp(["PP"], [mp], sl, T.PP[:, 15:128:16])
+            cp(["PP"], ["MP%d" % k], T.MP[:, 8 * k:8 * k + 8], T.PP[:, 15:128:16])
 
             def far_write():
                 cp([mp, st, far + "spare"], whole(far), F[:, 0:WX].indirect(sl), T[st][:])
 
             def rec_write():
-                cp([mp, "NR", "Xspare"], ["X"], T.X[:, 0:WX].indirect(sl), T.NR[:])
+                cp([mp, "NR", "Xspare"], ["X"], T.X[:, 0:WX].indirect(sl), T.MU[:, 0:128])
 
             def winners():
-                te(["PP", "IDF"], "p4", mm(T.p4[:, 0:128], T.IDF[:], T.PP[:], False, True))
-                act(["p4"], ["WV"], T.WV[:], T.p4[:, 0:128], AF.Relu, scale=-1.0, bias=W + 2048.0)
-                act(["WV"], [sg, "CT"], T[sg][:], T.WV[:], AF.Sign, accum_out=T.CT[:])
-
-            def count():
+                act(["IOT", "IOTspare", mp], [sg, "CT"], T[sg][:], T.IOT[:].indirect(sl), AF.Sign, accum_out=T.CT[:])
                 te(["CT", "ONF"], "p5", mm(T.p5[:, 0:1], T.ONF[:], T.CT[:], True, True))
 
-            def pairings():
-                te([sg, "WV", "BO4K", "BOB", "NBO"], "p8", mm(T.p8[:, 0:128], T.NBO[:], T.WV[:], d == 0, False),
-                   mm(T.p8[:, 0:128], T.BO4K[:], T[sg][:]), mm(T.p8[:, 0:128], T.BOB[:], T[sg][:], False, d == D - 1))
-                if d == D - 1:
-                    act(["p8"], ["NN%d" % t], T["NN%d" % t][:], T.p8[:, 0:128])
-                    send("N%d" % t, home, T["NM%d" % t][:], T["NN%d" % t][:], ["NN%d" % t], "NM%d" % t)
+            def pairings(lo, name):
+                c = slice(8 * lo, 8 * k + 8)
+                send(name, home, T.NM[:, c], T.MP[:, c], ["MP%d" % e for e in range(lo, k + 1)], name)
 
             def kappa(step):
                 if step == 0:
@@ -529,26 +537,24 @@ def rank_program(g, core, T, topo):
 
             if d < D - 1:
                 kk = (D - 1) * t + d
-                ur, up = T.UR[:, 128 * kk:128 * kk + 128], T.UP[:, 8 * k:8 * k + 8]
-                send("R%d%d" % (t, d), to, ur, T.NR[:], ["NR"], "UR%d" % kk)
-                send("P%d%d" % (t, d), to, up, sl, [mp], "UP%d" % k)
+                ur, up = T.UL[:, 136 * kk:136 * kk + 128], T.UL[:, 136 * kk + 128:136 * kk + 136]
+                send("U%d%d" % (t, d), to, T.UL[:, 136 * kk:136 * kk + 136], T.MU[:], ["NR", mp], "UL%d" % kk)
+                if t == 1 and d == 1:
+                    pairings(D, "N1")
                 act(["p6"], ["YRS"], T.YRS[:], T.p6[:, 0:128])
                 winners()
-                count()
                 far_write()
                 act(whole(far) + ["YU"], ["PGR"], T.PGR[:], F[:, 0:W].indirect(T.YU[:]))
                 te(["YRS", "IL0", "IL1"], "p6", *[
                     mm(T.p6[:, 0:64], T.IL[:, 128 * e:128 * e + 128], T.YRS[:, e:128:2], e == 0, e == 1) for e in range(2)])
-                pairings()
                 rec_write()
                 scan(["PGR", "CPK"], ["PS"], T.PS[:], T.CPK[:], T.PGR[:], -BIG, A.add, A.min)
                 kappa(0)
                 ts(["PS", "PG4"], ["PU"], T.PU[:], T.PS[:, 15:128:16], T.PG[:, 4:5], A.add)
                 kappa(1)
-                if t == 0:
-                    fa_piece("p7")
-                    fa_piece("p3")
-                cp(["UR%d" % kk, "UP%d" % k, xr + "spare"], [xr], XR[:, 0:WX].indirect(up), ur)
+                piece("p7")
+                piece("p3")
+                cp(["UL%d" % kk, xr + "spare"], [xr], XR[:, 0:WX].indirect(up), ur)
                 kappa(2)
                 cp([xr, "PU"], ["Z"], T.Z[:], XR[:, 0:W].indirect(T.PU[:]))
             elif t == 0:
@@ -556,27 +562,21 @@ def rank_program(g, core, T, topo):
                 cp(["X"], ["SN1"], T.SN1[:], T.X[:, 1:W:32])
                 send("S1", prv, T.SS1[:], T.SN1[:], ["SN1"], "SS1")
                 winners()
-                count()
                 far_write()
-                pairings()
+                pairings(0, "N0")
                 kappa(0)
-                tt(whole("FB") + ["TFREE"], ["NH1"], T.NH1[:], T.FB[:, 1:W:32], T.TFREE[:], A.is_gt)
+                ts(whole("FB"), ["NH1"], T.NH1[:], T.FB[:, 1:W:32], 0.0, A.is_ge)
                 kappa(1)
                 send("L1", prv, T.NL1[:], T.NH1[:], ["NH1"], "NL1")
                 kappa(2)
                 send("X1", prv, T.XR1[:, 0:W], T.X[:, 0:W], ["X"], "XR1")
-                fa_piece("p7")
-                fa_piece("p3")
-                fa_piece("p2")
-                fa_piece("p7")
             else:
+                pairings(k, "N2")
                 rec_write()
-                winners()
-                pairings()
                 dma("Y", "oX", [(T.yx[:], T.X[:, 0:W])], ["X"], ["yx"])
                 far_write()
                 dma("Y", "oA", [(T.ya[:], T.FA[0:128:16, 0:W])], whole("FA"), ["ya"])
 
-    tt(whole("FB") + ["NM1"], whole("FB"), T.FB[:, 1:W:32], T.FB[:, 1:W:32], T.NM1[:], A.add)
+    near("FB", TB * D - 1, "N2")
     dma("Y", "oB", [(T.yb[:], T.FB[0:128:16, 0:W])], whole("FB"), ["yb"])
     finish()

@@ -7,38 +7,40 @@ WX = W + L
 FULL = 16777216.0
 BIG = 8192.0
 LOW = 1.0e6
-SPLIT = (72, 72, 64)
+SPLIT = ((76, 72, 72), (72, 72, 72))
 MAGIC = 12582912.0
 
 F32, BF, F16, I32, U16 = "float32", "bfloat16", "float16", "int32", "uint16"
 SCRATCH = {}
 for _names, _cols, _dt in (
         ("X XR0 XR1", WX, BF), ("FA FB", WX, F32),
-        ("PA2 PB2", 256, I32), ("PA2H PB2H", 256, F16), ("FT", 2048, F16),
-        ("WTI", 1, I32), ("WI", 2, I32), ("WF", 2, F32), ("WM", 1024, BF),
+        ("PA2 PB2", 256, I32), ("PA2H PB2H", 256, F16), ("FT", 2048, BF),
+        ("WM", 512, F16),
         ("PI", 2, I32), ("PX", 5, I32), ("PF", 5, F32), ("PG", 8, F32),
         ("CI CGI CI8 ZS", 128, I32), ("SLI", 64, I32), ("SL9 RB", 72, I32), ("IOT", WX, F32), ("CMI", 144, I32),
-        ("IDF ONF CEX CY CIW CPL CPK ST0 ST1", 128, F32), ("IL", 256, F32), ("CP", 256, BF), ("M16", 144, F32),
+        ("IDF ONF CEX CY CIW CPL CPK ST0 ST1", 128, F32), ("IL", 256, BF), ("YR", 128, F16), ("CP", 256, BF), ("M16", 144, F32),
         ("BOB BOBIG IB NIB HI BIGI KM", 128, BF), ("K2K KQ", 192, BF), ("GM", 16, BF), ("K9", 72, BF),
-        ("BO16 I16", 128, F16), ("C0", 256, BF), ("SL", 272, F16), ("NS", 272, BF),
+        ("C0", 256, BF), ("SL NS", 272, BF),
         ("RSB", 72, F32), ("BJ0 BJ BJ2 KC", 4, F32), ("KB", 12, F32),
-        ("SN0 SN1 SS0 SS1 NH0 NH1 NL0 NL1 Z", 128, BF),
+        ("SN0 SS0 SS1 NH0 NH1 NL0 NL1 Z", 128, BF),
         ("ZR", 1024, BF), ("SQ", 256, F32), ("AI CC", 256, I32), ("CU", 256, U16),
         ("CFE", 528, F16), ("NQE", 528, BF), ("DD GS AB", W, BF),
         ("YE", 128, F16), ("PY", 136, F32), ("YU PU", 8, U16), ("EQ", 1024, BF),
-        ("TK XG", 128, BF), ("YRS PGR PS PP", 128, F32), ("SG0 SG1 SG2", 128, BF),
+        ("TK XG", 128, BF), ("PGR PS PP", 128, F32), ("SG0 SG1 SG2", 128, BF),
         ("CT KF", 1, F32), ("KJ", 2, I32),
-        ("MP NM", 8 * TB * D, U16), ("MU", 136, U16), ("UL", 136 * TB * (D - 1), U16)):
+        ("PM", 8, F32), ("MP NM", 24, U16), ("MU", 136, U16), ("UL", 136 * (TB * D - 1), U16)):
     for _n in _names.split():
         SCRATCH[_n] = ("sbuf", [128, _cols], _dt)
 SCRATCH["P8"] = ("sbuf", [8, W], I32)
+SCRATCH["WTI"] = ("sbuf", [1, 384], I32)
+SCRATCH["WR"] = ("sbuf", [1, 128], F16)
+SCRATCH["WS"] = ("sbuf", [1, 2], BF)
 SCRATCH["LV8"] = ("sbuf", [8, 128], BF)
 SCRATCH["E8"] = ("sbuf", [8, 128], BF)
 for _n in range(1, 9):
     SCRATCH["p%d" % _n] = ("psum", [128, 512], F32)
 
-REMOTE = ["S0", "X0", "L0", "S1", "X1", "L1", "N0", "N1", "N2"]
-REMOTE += ["U%d%d" % (t, d) for t in range(TB) for d in range(D - 1)]
+REMOTE = ["S0", "X0", "L0", "X1", "L1", "N0", "N1", "N2"] + ["U%d" % k for k in range(TB * D - 1)]
 LOCAL = ["dW", "dP8", "dX", "dPB", "dPA", "oX", "oA", "oB"]
 SEMAPHORES = ["qV", "qS", "qT", "qG"] + ["a" + n for n in REMOTE] + ["l" + n for n in REMOTE] + LOCAL
 
@@ -116,8 +118,8 @@ def machine(g, core, T, topo):
         snap[tok] = dict(know[q])
         book(q, tok, reads, writes)
 
-    def send(name, dst, out, src, reads, lands):
-        deps("G", reads, [])
+    def send(name, dst, out, src, reads, lands, behind=()):
+        deps("G", reads, list(behind))
         rid, pid = topo.addr(dst)[0], topo.addr(dst)[1]
         g.remote_dma(out_ap=out, in_ap=src, remote_sem=T.sem["a" + name], local_sem=T.sem["l" + name],
                      pid=pid, routing_id=rid, dma_engine_mask=topo.mask(core, dst))
@@ -177,10 +179,9 @@ def rank_program(g, core, T, topo):
         op("T", reads, [bank], *fns)
 
     dma("Y", "dP8", [(T.P8[:], T.pa[:])], [], ["P8"])
-    dma("Y", "dW", [(T.WTI[:], T.wt[:])], [], ["WTI"])
+    dma("Y", "dW", [(T.WTI[:, 0:128], T.wt[:])], [], ["WTI"])
     dma("Y", "dX", [(T.X[:, 0:W], T.x[:])], [], ["X"])
     dma("Y", "dPB", [(T.PB2[:], T.pb[:])], [], ["PB2"])
-    dma("Y", "dPA", [(T.PA2[:], T.pa[:])], [], ["PA2"])
 
     iota("PI", [[1, 2]], 0, 1)
     iota("CMI", [[0, 9], [1, 16]], 0, 0)
@@ -201,7 +202,6 @@ def rank_program(g, core, T, topo):
     fill(["KM"], T.KM[:], MAGIC)
     P_, PM, PGc, PJ, PL = [T.PF[:, k:k + 1] for k in range(5)]
     ts(["CMI", "PF"], ["M16"], T.M16[:], T.CMI[:], PM, A.is_equal)
-    ts(["CGI", "PF"], ["BO16"], T.BO16[:], T.CGI[:], PGc, A.is_equal)
     ts(["CGI", "PF"], ["E8"], T.E8[:], T.CGI[0:8, :], T.PF[0:8, 0:1], A.is_equal)
     ts(["CI", "PF"], ["IDF"], T.IDF[:], T.CI[:], P_, A.is_equal)
     ts(["CGI", "PF"], ["BOB"], T.BOB[:], T.CGI[:], PGc, A.is_equal)
@@ -210,8 +210,17 @@ def rank_program(g, core, T, topo):
     ts(["PF"], ["PG4"], T.PG[:, 4:5], PM, 15.0, A.is_lt, BIG, A.mult)
     ts(["P8"], ["LV8"], T.LV8[:], T.P8[:, 0:W:32], 0.0, A.is_ge)
     te(["E8", "LV8"], "p7", mm(T.p7[:, 0:128], T.E8[:], T.LV8[:], True, True))
+    ts(["WTI"], ["WI0"], T.WTI[:, 128:256], T.WTI[:, 0:128], 2047.0, A.add)
+    fill(["WSa"], T.WS[:, 0:1], 1.0 / W)
+    fill(["WSb"], T.WS[:, 1:2], -1.0 / W)
     cp(["p7"], ["NH0"], T.NH0[:], T.p7[:, 0:128])
     send("L0", nxt, T.NL0[:], T.NH0[:], ["NH0"], "NL0")
+    ts(["WI0"], ["WI1"], T.WTI[:, 256:384], T.WTI[:, 128:256], W - 1, A.bitwise_and)
+    for k in range(6):
+        ts(["BOB", "M16"], ["FT%d" % k], T.FT[:, 128 * k:128 * k + 128], T.BOB[:], T.M16[:, k:k + 1], A.mult)
+        if k == 3:
+            ts(["WI1"], ["WR"], T.WR[:], T.WTI[:, 256:384], -2047.0, A.add)
+            te(["WR", "WSa", "WSb"], "p8", mm(T.p8[:, 0:2], T.WR[:], T.WS[:], True, True))
     iota("BJ0", [[256, 4]], 16, 0, True)
     iota("SLI", [[-16, 8], [-1, 8]], 0, 1)
     iota("SL9", [[-16, 8], [-1, 9]], 1, 1)
@@ -223,10 +232,6 @@ def rank_program(g, core, T, topo):
     act(["M16"], ["C0b"], T.C0[:, 128:256], T.M16[:, 0:128], scale=-4 * BIG, bias=4 * BIG + 2048)
     act(["M16"], ["CY"], T.CY[:], T.M16[:, 0:128], scale=LOW, bias=-LOW)
     act(["BOB"], ["BOBIG"], T.BOBIG[:], T.BOB[:], scale=BIG)
-    act(["IDF", "PG3"], ["IL0"], T.IL[:, 0:128], T.IDF[:], scale=T.PG[:, 3:4])
-    act(["IDF", "PF"], ["IL1"], T.IL[:, 128:256], T.IDF[:], scale=PL)
-    for k in range(16):
-        ts(["BO16", "M16"], ["FT%d" % k], T.FT[:, 128 * k:128 * k + 128], T.BO16[:], T.M16[:, k:k + 1], A.mult)
 
     def table(name, c, bank, on):
         src = T["P" + name[1] + "2H"]
@@ -234,6 +239,8 @@ def rank_program(g, core, T, topo):
             mm(T[bank][:, 256 * e:256 * e + 256], T.FT[:, 128 * (2 * c + e):128 * (2 * c + e + 1)], src[:], True, True)
             for e in range(2)])
         out = T[name][:, 512 * c:512 * c + 512]
+        if on == "V later":
+            return lambda: ts([bank], [name + str(c)], out, T[bank][:, 0:512], 2047.0, A.add)
         if on == "later":
             return lambda: act([bank], [name + str(c)], out, T[bank][:, 0:512], bias=2047.0)
         if on == "S":
@@ -244,24 +251,16 @@ def rank_program(g, core, T, topo):
     def whole(name):
         return [name + str(c) for c in range(8)]
 
-    ts(["WTI"], ["WI0"], T.WI[:, 0:1], T.WTI[:], 4032, A.bitwise_and)
-    ts(["WTI"], ["WI1"], T.WI[:, 1:2], T.WTI[:], 63, A.bitwise_and)
     ts(["BJ0", "PG2"], ["BJ"], T.BJ[:], T.BJ0[:], T.PG[:, 2:3], A.add)
-    ts(["WI0", "WI1"], ["WF"], T.WF[:], T.WI[:], 1.0 / W, A.mult)
-    tt(["BJ"], ["BJ2"], T.BJ2[:], T.BJ[:], T.BJ[:], A.mult)
     for k in range(4):
-        ts(["CI8", "PG%d" % (k // 2), "WF"], ["WM%d" % k], T.WM[:, 128 * k:128 * k + 128], T.CI8[:],
-           T.PG[:, k // 2:k // 2 + 1], A.is_equal, T.WF[:, k % 2:k % 2 + 1], A.mult)
+        ts(["CI8", "PG%d" % (k % 2), "p8"], ["WM%d" % k], T.WM[:, 128 * k:128 * k + 128], T.CI8[:],
+           T.PG[:, k % 2:k % 2 + 1], A.is_equal, T.p8[:, k // 2:k // 2 + 1], A.mult)
+    tt(["BJ"], ["BJ2"], T.BJ2[:], T.BJ[:], T.BJ[:], A.mult)
+    cp(["NQE"], ["CFE"], T.CFE[:], T.NQE[:])
     for d in range(D):
         ts(["BJ2"], ["KB%d" % d], T.KB[:, 4 * d:4 * d + 4], T.BJ2[:], -1.0 / 32, A.mult, 97.0 * d - 0.4375, A.add)
-    ts(["WM%d" % k for k in range(4)], ["WMn"], T.WM[:, 512:1024], T.WM[:, 0:512], -1.0, A.mult)
-    cp(["NQE"], ["CFE"], T.CFE[:], T.NQE[:])
     ts(["CI", "PF"], ["GMa"], T.GM[:, 0:8], T.CI[:, 0:8], PGc, A.is_equal, float(W), A.mult)
     ts(["CI", "PF"], ["GMb"], T.GM[:, 8:16], T.CI[:, 0:8], PGc, A.is_equal, -float(W), A.mult)
-    for e in range(4):
-        src, c = ("SLI", slice(64 * e, 64 * e + 64)) if e < 2 else ("SL9", slice(72 * e - 16, 72 * e + 56))
-        ts([src], ["SL%d" % e], T.SL[:, c], T[src][:], 8.0 * (e % 2), A.is_equal)
-        ts([src], ["NS%d" % e], T.NS[:, c], T[src][:], 8.0 * (e % 2), A.is_equal, -FULL, A.mult)
 
     def const(writes, ap, c, reads=()):
         act(["IDF"] + list(reads), writes, ap, T.IDF[:, 0:ap.shape[1]], scale=0.0, bias=c)
@@ -270,39 +269,62 @@ def rank_program(g, core, T, topo):
     const(["KQa"], T.KQ[:, 0:128], -0.25)
     const(["PYc"], T.PY[:, 0:1], -1.0)
     const(["RSBc"], T.RSB[:], -5.0e7)
-    const(["ONF"], T.ONF[:], 1.0 / 16)
     const(["K9"], T.K9[:, 0:72:9], -2 * FULL, ["K9a"])
-    for n in ("X", "FB", "XR0", "XR1", "FA", "IOT"):
-        const([n + "spare"], T[n][:, W:WX], 0.0)
-    act(["M16"], ["CPA"], T.CP[:, 0:128], T.M16[:, 0:128], scale=4 * BIG)
-    act(["M16"], ["CPB"], T.CP[:, 128:256], T.M16[:, 15:143], scale=-BIG)
-    te(["IB", "CPA", "CPB"], "p6", mm(T.p6[:, 0:128], T.IB[:], T.CP[:, 0:128], True, False),
-       mm(T.p6[:, 0:128], T.IB[:], T.CP[:, 128:256], False, True))
     te(["IDF", "CY", "CIW"], "p1", mm(T.p1[:, 0:128], T.IDF[:], T.CY[:], True, False),
        mm(T.p1[:, 0:128], T.IDF[:], T.CIW[:], False, True))
-    act(["p6"], ["CPK"], T.CPK[:], T.p6[:, 0:128])
+    for k in range(6, 16):
+        act(["BOB", "M16"], ["FT%d" % k], T.FT[:, 128 * k:128 * k + 128], T.BOB[:], scale=T.M16[:, k:k + 1])
     act(["p1"], ["CPL"], T.CPL[:], T.p1[:, 0:128])
+    act(["IDF", "PG3"], ["IL0"], T.IL[:, 0:128], T.IDF[:], scale=T.PG[:, 3:4])
+    act(["IDF", "PF"], ["IL1"], T.IL[:, 128:256], T.IDF[:], scale=PL)
+
+    def late_constants():
+        for n in ("IOT", "FB", "X"):
+            const([n + "spare"], T[n][:, W:WX], 0.0)
+        const(["ONF"], T.ONF[:], 1.0 / 16)
+        act(["M16"], ["CPA"], T.CP[:, 0:128], T.M16[:, 0:128], scale=4 * BIG)
+        act(["M16"], ["CPB"], T.CP[:, 128:256], T.M16[:, 15:143], scale=-BIG)
+
+    def later_constants():
+        te(["IB", "CPA", "CPB"], "p4", mm(T.p4[:, 0:128], T.IB[:], T.CP[:, 0:128], True, False),
+           mm(T.p4[:, 0:128], T.IB[:], T.CP[:, 128:256], False, True))
+        const(["XR0spare"], T.XR0[:, W:WX], 0.0)
+        act(["p4"], ["CPK"], T.CPK[:], T.p4[:, 0:128])
+
+    def last_constants():
+        act(["SL%d" % e for e in range(4)], ["NS"], T.NS[:], T.SL[:], scale=-FULL)
+        for n in ("XR1", "FA"):
+            const([n + "spare"], T[n][:, W:WX], 0.0)
+
     cp(["X"], ["SN0"], T.SN0[:], T.X[:, 0:W:32])
     send("S0", nxt, T.SS0[:], T.SN0[:], ["SN0"], "SS0")
-    send("X0", nxt, T.XR0[:, 0:W], T.X[:, 0:W], ["X"], "XR0")
     iota("ST1", [[32, 128]], 1, 0, True)
-    op("G", [], ["IOT"], lambda: g.iota(T.IOT[:, 0:W], [[1, W]], 1, 0, allow_small_or_imprecise_dtypes=True))
+    for lo, hi in ((0, 512), (512, W)):
+        op("G", [], ["IOT"], lambda: g.iota(T.IOT[:, lo:hi], [[1, hi - lo]], lo + 1, 0,
+                                            allow_small_or_imprecise_dtypes=True))
+        if lo == 0:
+            send("X0", nxt, T.XR0[:, 0:W], T.X[:, 0:W], ["X"], "XR0", ["SN0"])
+            dma("Y", "dPA", [(T.PA2[:], T.pa[:])], [], ["PA2", "SN0"])
+    for e in range(4):
+        src, c = ("SLI", slice(64 * e, 64 * e + 64)) if e < 2 else ("SL9", slice(72 * e - 16, 72 * e + 56))
+        ts([src], ["SL%d" % e], T.SL[:, c], T[src][:], 8.0 * (e % 2), A.is_equal)
     fill(["ZSc"], T.ZS[:], 0)
-    cp(["IDF"], ["I16"], T.I16[:], T.IDF[:])
     ts(["PB2"], ["PB2H"], T.PB2H[:], T.PB2[:], -2047.0, A.add)
-    for c in range(5):
-        table("FB", c, ("p2", "p3", "p4", "p5", "p7")[c], "V" if c in (1, 3) else "S")
+    for c in range(3):
+        table("FB", c, ("p2", "p3", "p4")[c], "SV"[c % 2])
+    in_head = table("FB", 3, "p8", "later")
 
     zr_all = ["ZR%d" % m for m in range(8)]
-    pieces = [("FB", c) for c in range(5, 8)] + [("FA", c) for c in range(8)]
+    pieces = [("FB", c) for c in range(4, 8)] + [("FA", c) for c in range(8)]
 
     def piece(bank):
         if pieces:
             table(*pieces.pop(0), bank, "S")
 
-    def near(name, k, msg):
-        c = T[name][:, k // D:W:32]
-        tt(whole(name) + ["IOT", "IOTspare", msg], whole(name), c, T.IOT[:].indirect(T.NM[:, 8 * k:8 * k + 8]), c, A.add)
+    def near(name, e):
+        c = T[name][:, min(e, 1):W:32]
+        tt(whole(name) + ["IOT", "IOTspare", "N%d" % e], whole(name), c, T.IOT[:].indirect(T.NM[:, 8 * e:8 * e + 8]), c,
+           A.add)
 
     for t in range(TB):
         far = "FB" if t == 0 else "FA"
@@ -312,26 +334,30 @@ def rank_program(g, core, T, topo):
         to = nxt if t == 0 else prv
         home = prv if t == 0 else nxt
         for d in range(D):
-            zn = ss if d == 0 else "Z"
-            Z = T[zn]
             first = t == 0 and d == 0
+            zn, z0, zs = ("XR1", 1, 32) if (t, d) == (1, 0) else (ss if first else "Z", 0, 1)
+            Z = T[zn]
             kn, KN = ("KB0", T.KB) if first else ("KC", T.KC)
             stopped = [nl] + ["SG%d" % e for e in range(d)]
 
             pu = T.p1[:, 0:64]
 
             def weighted(sign):
-                return [mm(pu, T.WM[:, 128 * (4 * sign + k):128 * (4 * sign + k + 1)], Z[:, k // 2:128:2], False,
-                           sign == 0 and k == 3) for k in range(4)]
+                return [mm(pu, T.WM[:, 128 * (2 * sign + e):128 * (2 * sign + e + 1)],
+                           Z[:, z0 + zs * e:128 * zs:2 * zs], False, sign == 0 and e == 1) for e in range(2)]
 
             te(["IB", "KQ"], "p1", mm(pu, T.IB[:], T.KQ[:, 128:192], True, False))
-            te(["WMn", "IB", "NIB", "KM", zn] + ["WM%d" % k for k in range(4)], "p1", *(
+            te(["IB", "NIB", "KM", zn] + ["WM%d" % k for k in range(4)], "p1", *(
                 weighted(1) + [mm(pu, T.IB[:], T.KM[:, 0:64]), mm(pu, T.NIB[:], T.KM[:, 0:64])] + weighted(0)))
             for m in range(8):
-                cp([zn], ["ZR%d" % m], T.ZR[:, m:1024:8], Z[:])
+                cp([zn], ["ZR%d" % m], T.ZR[:, m:1024:8], Z[:, z0:128 * zs:zs])
+            if (t, d) == (1, 0):
+                cp([zn], [ss], T[ss][:], Z[:, z0:128 * zs:zs])
             for b in range(4):
                 act(["p1", "BJ"], ["SQ%d" % b], T.SQ[:, 64 * b:64 * b + 64], pu, AF.Square, scale=float(W),
                     bias=T.BJ[:, b:b + 1])
+            if first:
+                in_head()
 
             def whole_part(b):
                 c = slice(64 * b, 64 * b + 64)
@@ -366,10 +392,10 @@ def rank_program(g, core, T, topo):
                     mm(keys(b, lo, hi, j), T.DD[:, 1024 * b + 8 * lo + j:1024 * b + 8 * hi:8], T.GM[:, 8:16])
                     for j in range(8)])
 
-            def plus_abs(b, lo, hi, parts):
+            def plus_abs(b, lo, hi, parts, stop=False):
                 te(["AB%d_%d" % (b, e) for e in parts] + ["GMa"], kbank(b), *[
-                    mm(keys(b, lo, hi, j), T.AB[:, 1024 * b + 8 * lo + j:1024 * b + 8 * hi:8], T.GM[:, 0:8])
-                    for j in range(8)])
+                    mm(keys(b, lo, hi, j), T.AB[:, 1024 * b + 8 * lo + j:1024 * b + 8 * hi:8], T.GM[:, 0:8], False,
+                       stop and j == 7) for j in range(8)])
 
             def minus_z(bank, lo, hi):
                 te(["NIB"] + zr_all, bank, mm(T[bank][:, 0:8 * (hi - lo)], T.NIB[:], T.ZR[:, 8 * lo:8 * hi], True, False))
@@ -398,47 +424,49 @@ def rank_program(g, core, T, topo):
                 if d > 0:
                     tt(["CC%d" % b, "p6"], ["NQE%d" % b], T.NQE[:, 2 + 128 * b:130 + 128 * b:2],
                        T.CC[:, 64 * b:64 * b + 64], T.p6[:, 0:64], A.not_equal)
-                    spread(T.NQE, T.NS, ["NQE", "NQE%d" % b] + ["NS%d" % e for e in range(4)], b)
+                    spread(T.NQE, T.NS, ["NQE", "NQE%d" % b, "NS"], b)
 
             def places(b, stop):
                 spread(T.CFE, T.SL, ["CFE"] + ["SL%d" % e for e in range(4)], b, stop)
 
             te(["IB", "K2K"], "p4", mm(T.p4[:, 0:192], T.IB[:], T.K2K[:], True, False))
             te(["IB", "K9"], "p5", mm(T.p5[:, 0:72], T.IB[:], T.K9[:], True, False))
-            s0, s1, s2 = SPLIT
+            s0, s1, s2 = SPLIT[min(d, 1)]
             minus_z("p2", s0, 128)
             minus_z("p3", s1, 128)
             minus_z("p7", s2, 128)
             for b in range(4):
                 whole_part(b)
             modulo(0, 1)
-            modulo(1, 4)
+            modulo(1, 2)
+            modulo(2, 4)
             offsets(0, 1)
-            offsets(1, 4)
+            offsets(1, 2)
+            barred(0)
+            barred(1)
+            offsets(2, 4)
             gather_s(0, s0, 128)
             gather_v(0, 0, s0)
             te(["IB", "C0b"], "p1", mm(T.p1[:, 0:128], T.IB[:], T.C0[:, 128:256], True, False))
-            early = table(*pieces.pop(0), "p8", "later") if pieces else None
+            early = [table(*pieces.pop(0), bank, "later") for bank in (["p8", "p6"] if first else ["p8"]) if pieces]
             plus_x("p2", 0, s0, 128)
             gather_s(1, s1, 128)
             abs_s("p2", 0, s0, 128)
             minus_d(0, 0, s0)
-            for b in range(4):
-                barred(b)
-            relu_v(0, 0, s0)
             gather_v(1, 0, s1)
+            relu_v(0, 0, s0)
             plus_x("p3", 1, s1, 128)
             gather_s(2, s2, 128)
-            te(["IB", "C0a"], "p6", mm(T.p6[:, 0:128], T.IB[:], T.C0[:, 0:128], True, False))
             abs_s("p3", 1, s1, 128)
-            plus_abs(0, 0, 128, [0, s0])
-            minus_z("p2", 64, 96)
-            ts(["CU%d" % b for b in range(4)], ["CFE"], T.CFE[:, 2:514:2], T.CU[:], -2048.0, A.add)
             minus_d(1, 0, s1)
+            minus_z("p2", 64, 96)
+            plus_abs(0, 0, 128, [0, s0])
+            barred(2)
+            ts(["CU%d" % b for b in range(4)], ["CFE"], T.CFE[:, 2:514:2], T.CU[:], -2048.0, A.add)
             gather_v(2, 0, s2)
             relu_v(1, 0, s1)
-            plus_x("p7", 2, s2, 128)
             places(0, False)
+            plus_x("p7", 2, s2, 128)
             gather_s(3, 64, 96)
             minus_z("p3", 96, 128)
             gather_s(3, 96, 128)
@@ -453,54 +481,62 @@ def rank_program(g, core, T, topo):
             minus_d(3, 0, 32)
             plus_x("p3", 3, 96, 128)
             abs_s("p3", 3, 96, 128)
-            if early:
-                early()
+            for copy in early:
+                copy()
             gather_v(3, 32, 64)
             relu_v(3, 0, 32)
             plus_abs(2, 0, 128, [0, s2])
             places(2, True)
-            relu_v(3, 32, 64)
             minus_d(3, 32, 64)
-            plus_abs(3, 0, 128, [0, 32, 64, 96])
-            places(3, True)
+            barred(3)
+            relu_v(3, 32, 64)
+            if d == 0:
+                places(3, False)
+            plus_abs(3, 0, 128, [0, 32, 64, 96], d == 0)
+            if d > 0:
+                places(3, True)
             for e in range(8):
                 op("V", ["p4", "RSBc"], ["RSB%d" % e], lambda: V.tensor_reduce(
                     T.RSB[:, 9 * e + 1:9 * e + 2], T.p4[:, 24 * e:24 * e + 24], AxisListType.X, A.min))
             te(stopped + ["IB", "C0b", "BIGI"], "p7", mm(T.p7[:, 0:128], T.IB[:], T.C0[:, 128:256], True, False),
                *[mm(T.p7[:, 0:128], T.BIGI[:], T[n][:]) for n in stopped])
             te(stopped + ["BIGI"], "p1", *[mm(T.p1[:, 0:128], T.BIGI[:], T[n][:]) for n in stopped])
-            piece("p3")
             if first:
-                piece("p2")
-            late = {(1, 0): [("FA", e, "N0") for e in range(D)], (1, 2): [("FB", D + e, "N1") for e in range(D - 1)]}
-            late = late.get((t, d), [])
+                on_vector = table(*pieces.pop(0), "p4", "V later")
+            piece("p3")
+            te(["IB", "C0a"], "p6", mm(T.p6[:, 0:128], T.IB[:], T.C0[:, 0:128], True, False))
 
             scan(["p5", "RSBc"] + ["RSB%d" % e for e in range(8)], ["RB"], T.RB[:], T.RSB[:], T.p5[:, 0:72], 0.0, A.max, A.min)
             ts(["RB", "ZSc"], ["ZS"], T.ZS[:, 0:128:16], T.RB[:, 8:72:9], W - 1, A.bitwise_and)
             scan(["ZS", "ZSc", "CEX"], ["YE"], T.YE[:], T.CEX[:], T.ZS[:], 0.0, A.min, A.add)
             if first:
-                ts(["PA2"], ["PA2H"], T.PA2H[:], T.PA2[:], -2047.0, A.add)
-            for e in late[:2]:
-                near(*e)
+                on_vector()
+            if (t, d) == (1, 0):
+                near("FA", 0)
+            if (t, d) == (1, 2):
+                near("FB", 1)
             for bank, stop in (("p7", True), ("p6", True), ("p1", False)):
-                te(["YE", "I16"], bank, mm(T[bank][:, 0:128], T.YE[:], T.I16[:], False, stop))
+                te(["YE", "IB"], bank, mm(T[bank][:, 0:128], T.YE[:], T.IB[:], False, stop))
             te(["IB", "KQa", "HI", ss], "p2", mm(T.p2[:, 0:128], T.IB[:], T.KQ[:, 0:128], True, False),
                mm(T.p2[:, 0:128], T.HI[:], T[ss][:]))
             scan(["p7", "CPL", "PYc"], ["PY"], T.PY[:, 1:129], T.CPL[:], T.p7[:, 0:128], -1.0, A.max, A.min)
-            for e in late[2:]:
-                near(*e)
+            ts(["p6"], ["YR"], T.YR[:], T.p6[:, 0:128], -2048.0, A.add)
             ts(["PY"], ["YU"], T.YU[:], T.PY[:, 16:129:16], W - 1.0, A.min)
             act(whole(far) + ["YU"], ["TK"], T.TK[:], F[:, 0:W].indirect(T.YU[:]), AF.Relu, bias=1.0)
-            act(["X", "YU"], ["XG"], T.XG[:], T.X[:, 0:W].indirect(T.YU[:]))
+            if first:
+                late_constants()
             tt(["p6", "PY", "PYc"], ["EQ7"], T.EQ[:, 896:1024], T.p6[:, 0:128], T.PY[:, 0:128], A.is_equal)
             te(["EQ7", "BOBIG"], "p1", mm(T.p1[:, 0:128], T.BOBIG[:], T.EQ[:, 896:1024]))
             for h in range(7):
                 lo = 16 * h + 17
                 e = T.EQ[:, 128 * h + lo:128 * h + 128]
-                ts(["p6", "PY"], ["EQ%d" % h], e, T.p6[:, lo:128], T.PY[:, 16 * h + 16:16 * h + 17], A.is_equal)
-                if h == 5:
-                    te(["TK", "BIGI"], "p1", mm(T.p1[:, 0:128], T.BIGI[:], T.TK[:]))
-                te(["EQ%d" % h, "BOBIG"], "p1", mm(T.p1[:, lo:128], T.BOBIG[:], e, False, h == 6))
+                ts(["YR", "PY"], ["EQ%d" % h], e, T.YR[:, lo:128], 2048.0, A.add, T.PY[:, 16 * h + 16:16 * h + 17],
+                   A.is_equal)
+                te(["EQ%d" % h, "BOBIG"], "p1", mm(T.p1[:, lo:128], T.BOBIG[:], e))
+            cp(["X", "YU"], ["XG"], T.XG[:], T.X[:, 0:W].indirect(T.YU[:]))
+            if first:
+                ts(["PA2"], ["PA2H"], T.PA2H[:], T.PA2[:], -2047.0, A.add)
+            te(["TK", "BIGI"], "p1", mm(T.p1[:, 0:128], T.BIGI[:], T.TK[:], False, True))
             te(["XG", "HI", "IB", "KM"], "p2", mm(T.p2[:, 0:128], T.HI[:], T.XG[:]),
                mm(T.p2[:, 0:128], T.IB[:], T.KM[:], False, True))
             scan(["p1", "CPL"], ["PP"], T.PP[:], T.CPL[:], T.p1[:, 0:128], -1.0, A.max, A.min)
@@ -509,7 +545,6 @@ def rank_program(g, core, T, topo):
             mp, sg = "ML", "SG%d" % d
             sl = T.MU[:, 128:136]
             cp(["PP"], [mp], sl, T.PP[:, 15:128:16])
-            cp(["PP"], ["MP%d" % k], T.MP[:, 8 * k:8 * k + 8], T.PP[:, 15:128:16])
 
             def far_write():
                 cp([mp, st, far + "spare"], whole(far), F[:, 0:WX].indirect(sl), T[st][:])
@@ -521,9 +556,20 @@ def rank_program(g, core, T, topo):
                 act(["IOT", "IOTspare", mp], [sg, "CT"], T[sg][:], T.IOT[:].indirect(sl), AF.Sign, accum_out=T.CT[:])
                 te(["CT", "ONF"], "p5", mm(T.p5[:, 0:1], T.ONF[:], T.CT[:], True, True))
 
-            def pairings(lo, name):
-                c = slice(8 * lo, 8 * k + 8)
-                send(name, home, T.NM[:, c], T.MP[:, c], ["MP%d" % e for e in range(lo, k + 1)], name)
+            def update(k, dst):
+                send("U%d" % k, dst, T.UL[:, 136 * k:136 * k + 136], T.MU[:], ["NR", mp], "UL%d" % k)
+                return T.UL[:, 136 * k:136 * k + 128], T.UL[:, 136 * k + 128:136 * k + 136]
+
+            def paired():
+                if d == 0:
+                    cp(["PP"], ["PM"], T.PM[:], T.PP[:, 15:128:16])
+                else:
+                    tt(["PP", "PM"], ["PM"], T.PM[:], T.PP[:, 15:128:16], T.PM[:], A.min)
+
+            def pairings(e):
+                c = slice(8 * e, 8 * e + 8)
+                cp(["PM"], ["MP%d" % e], T.MP[:, c], T.PM[:])
+                send("N%d" % e, home, T.NM[:, c], T.MP[:, c], ["MP%d" % e], "N%d" % e)
 
             def kappa(step):
                 if step == 0:
@@ -536,47 +582,51 @@ def rank_program(g, core, T, topo):
                     act(["KF", "KB%d" % e], ["KC"], T.KC[:], T.KB[:, 4 * e:4 * e + 4], AF.Identity, bias=T.KF[:])
 
             if d < D - 1:
-                kk = (D - 1) * t + d
-                ur, up = T.UL[:, 136 * kk:136 * kk + 128], T.UL[:, 136 * kk + 128:136 * kk + 136]
-                send("U%d%d" % (t, d), to, T.UL[:, 136 * kk:136 * kk + 136], T.MU[:], ["NR", mp], "UL%d" % kk)
-                if t == 1 and d == 1:
-                    pairings(D, "N1")
-                act(["p6"], ["YRS"], T.YRS[:], T.p6[:, 0:128])
+                ur, up = update(k, to)
+                te(["YR", "IL0", "IL1", "IB", "K2K"], "p6", mm(T.p6[:, 0:64], T.IB[:], T.K2K[:, 0:64], True, False), *[
+                    mm(T.p6[:, 0:64], T.IL[:, 128 * e:128 * e + 128], T.YR[:, e:128:2], False, e == 1) for e in range(2)])
+                if first:
+                    later_constants()
                 winners()
                 far_write()
                 act(whole(far) + ["YU"], ["PGR"], T.PGR[:], F[:, 0:W].indirect(T.YU[:]))
-                te(["YRS", "IL0", "IL1"], "p6", *[
-                    mm(T.p6[:, 0:64], T.IL[:, 128 * e:128 * e + 128], T.YRS[:, e:128:2], e == 0, e == 1) for e in range(2)])
+                if first:
+                    last_constants()
                 rec_write()
+                if k == 1:
+                    send("X1", prv, T.XR1[:, 0:W], T.X[:, 0:W], ["X"], "XR1", ["NR"])
                 scan(["PGR", "CPK"], ["PS"], T.PS[:], T.CPK[:], T.PGR[:], -BIG, A.add, A.min)
                 kappa(0)
-                ts(["PS", "PG4"], ["PU"], T.PU[:], T.PS[:, 15:128:16], T.PG[:, 4:5], A.add)
-                kappa(1)
+                paired()
                 piece("p7")
                 piece("p3")
-                cp(["UL%d" % kk, xr + "spare"], [xr], XR[:, 0:WX].indirect(up), ur)
-                kappa(2)
+                cp(["UL%d" % k, xr + "spare"], [xr], XR[:, 0:WX].indirect(up), ur)
+                ts(["PS", "PG4"], ["PU"], T.PU[:], T.PS[:, 15:128:16], T.PG[:, 4:5], A.add)
+                kappa(1)
+                if k == 4:
+                    pairings(1)
                 cp([xr, "PU"], ["Z"], T.Z[:], XR[:, 0:W].indirect(T.PU[:]))
+                kappa(2)
             elif t == 0:
-                rec_write()
-                cp(["X"], ["SN1"], T.SN1[:], T.X[:, 1:W:32])
-                send("S1", prv, T.SS1[:], T.SN1[:], ["SN1"], "SS1")
+                ur, up = update(k, prv)
                 winners()
                 far_write()
-                pairings(0, "N0")
+                paired()
+                rec_write()
                 kappa(0)
+                pairings(0)
                 ts(whole("FB"), ["NH1"], T.NH1[:], T.FB[:, 1:W:32], 0.0, A.is_ge)
                 kappa(1)
                 send("L1", prv, T.NL1[:], T.NH1[:], ["NH1"], "NL1")
                 kappa(2)
-                send("X1", prv, T.XR1[:, 0:W], T.X[:, 0:W], ["X"], "XR1")
+                cp(["UL%d" % k, "XR1spare"], ["XR1"], T.XR1[:, 0:WX].indirect(up), ur)
             else:
-                pairings(k, "N2")
+                send("N2", home, T.NM[:, 16:24], sl, [mp], "N2")
                 rec_write()
                 dma("Y", "oX", [(T.yx[:], T.X[:, 0:W])], ["X"], ["yx"])
                 far_write()
                 dma("Y", "oA", [(T.ya[:], T.FA[0:128:16, 0:W])], whole("FA"), ["ya"])
 
-    near("FB", TB * D - 1, "N2")
+    near("FB", 2)
     dma("Y", "oB", [(T.yb[:], T.FB[0:128:16, 0:W])], whole("FB"), ["yb"])
     finish()

from concourse.mybir import dt, AluOpType, AxisListType, ActivationFunctionType

A = AluOpType
AF = ActivationFunctionType
W, L, TB, D = 4096, 128, 2, 3
WX = W + L
FULL = 16777216.0
BIG = 8192.0
LOW = 1.0e6
SPLIT = ((76, 72, 72), (72, 72, 72))
MAGIC = 12582912.0

F32, BF, F16, I32, U16 = "float32", "bfloat16", "float16", "int32", "uint16"
SCRATCH = {}
for _names, _cols, _dt in (
        ("X XR0 XR1", WX, BF), ("FA FB", WX, F32),
        ("PA2 PB2", 256, I32), ("PA2H PB2H", 256, F16), ("FT", 2048, BF),
        ("WM", 512, F16),
        ("PI", 2, I32), ("PX", 5, I32), ("PF", 5, F32), ("PG", 8, F32),
        ("CI CGI CI8 ZS", 128, I32), ("SLI", 64, I32), ("SL9 RB", 72, I32), ("IOT", WX, F32), ("CMI", 144, I32),
        ("IDF ONF CEX CY CIW CPL CPK ST0 ST1", 128, F32), ("IL", 256, BF), ("YR", 128, F16), ("CP", 256, BF), ("M16", 144, F32),
        ("BOB BOBIG IB NIB HI BIGI KM", 128, BF), ("K2K KQ", 192, BF), ("GM", 16, BF), ("K9", 72, BF),
        ("C0", 256, BF), ("SL NS", 272, BF),
        ("RSB", 72, F32), ("BJ0 BJ BJ2 KC", 4, F32), ("KB", 12, F32),
        ("SN0 SS0 SS1 NH0 NH1 NL0 NL1 Z", 128, BF),
        ("ZR", 1024, BF), ("SQ", 256, F32), ("AI CC", 256, I32), ("CU", 256, U16),
        ("CFE", 528, F16), ("NQE", 528, BF), ("DD GS AB", W, BF),
        ("YE", 128, F16), ("PY", 136, F32), ("YU PU", 8, U16), ("EQ", 1024, BF),
        ("TK XG", 128, BF), ("PGR PS PP", 128, F32), ("SG0 SG1 SG2", 128, BF),
        ("CT KF", 1, F32), ("KJ", 2, I32),
        ("PM", 8, F32), ("MP NM", 24, U16), ("MU", 136, U16), ("UL", 136 * (TB * D - 1), U16)):
    for _n in _names.split():
        SCRATCH[_n] = ("sbuf", [128, _cols], _dt)
SCRATCH["P8"] = ("sbuf", [8, W], I32)
SCRATCH["WTI"] = ("sbuf", [1, 384], I32)
SCRATCH["WR"] = ("sbuf", [1, 128], F16)
SCRATCH["WS"] = ("sbuf", [1, 2], BF)
SCRATCH["LV8"] = ("sbuf", [8, 128], BF)
SCRATCH["E8"] = ("sbuf", [8, 128], BF)
for _n in range(1, 9):
    SCRATCH["p%d" % _n] = ("psum", [128, 512], F32)

REMOTE = ["S0", "X0", "L0", "X1", "L1", "N0", "N1", "N2"] + ["U%d" % k for k in range(TB * D - 1)]
LOCAL = ["dW", "dP8", "dX", "dPB", "dPA", "oX", "oA", "oB"]
SEMAPHORES = ["qV", "qS", "qT", "qG"] + ["a" + n for n in REMOTE] + ["l" + n for n in REMOTE] + LOCAL


def machine(g, core, T, topo):
    Q = {"V": g.vector, "S": g.scalar, "T": g.tensor, "G": g, "Y": g.sync}
    sem = {"V": "qV", "S": "qS", "T": "qT", "G": "qG"}
    cnt = {}
    know = {q: {} for q in Q}
    snap = {}
    lastw = {}
    readers = {}

    def wait(q, toks):
        todo = []
        for t in toks:
            if t not in todo and know[q].get(t[0], 0) < t[1]:
                todo.append(t)
        keep = []
        for t in todo:
            covered = False
            for o in todo:
                if o != t and snap.get(o, {}).get(t[0], 0) >= t[1]:
                    covered = True
            if not covered:
                keep.append(t)
        for s, v in keep:
            if know[q].get(s, 0) >= v:
                continue
            Q[q].wait_ge(T.sem[s], v)
            know[q][s] = max(know[q].get(s, 0), v)
            for a, b in snap.get((s, v), {}).items():
                know[q][a] = max(know[q].get(a, 0), b)

    def deps(q, reads, writes):
        toks = []
        for r in reads:
            if r in lastw:
                toks.append(lastw[r][0])
            if r[0] == "p":
                toks.extend([t for t in readers.get(r, []) if t[0] != sem.get(q)])
        for w in writes:
            if w in lastw and not (q == "T" and lastw[w][1] == "T"):
                toks.append(lastw[w][0])
            toks.extend(readers.get(w, []))
        wait(q, toks)

    def book(q, tok, reads, writes):
        for r in reads:
            old = [t for t in readers.get(r, []) if t[0] != tok[0]]
            readers[r] = old + [tok]
        for w in writes:
            lastw[w] = (tok, q)
            readers[w] = []

    def op(q, reads, writes, *fns):
        deps(q, reads, writes)
        ins = None
        for f in fns:
            ins = f()
        cnt[sem[q]] = cnt.get(sem[q], 0) + 1
        ins.then_inc(T.sem[sem[q]], 1)
        tok = (sem[q], cnt[sem[q]])
        know_now = dict(know[q])
        know_now[sem[q]] = tok[1]
        snap[tok] = know_now
        book(q, tok, reads, writes)

    def dma(q, name, pairs, reads, writes):
        deps(q, reads, writes)
        for o, i in pairs:
            Q[q].dma_start(o, i).then_inc(T.sem[name], 16)
        cnt[name] = 16 * len(pairs)
        tok = (name, cnt[name])
        snap[tok] = dict(know[q])
        book(q, tok, reads, writes)

    def send(name, dst, out, src, reads, lands, behind=()):
        deps("G", reads, list(behind))
        rid, pid = topo.addr(dst)[0], topo.addr(dst)[1]
        g.remote_dma(out_ap=out, in_ap=src, remote_sem=T.sem["a" + name], local_sem=T.sem["l" + name],
                     pid=pid, routing_id=rid, dma_engine_mask=topo.mask(core, dst))
        n = len(topo.engines(core, dst))
        cnt["l" + name] = n
        cnt["a" + name] = n
        book("G", ("l" + name, n), reads, [])
        lastw[lands] = (("a" + name, n), "R")
        readers[lands] = []

    def finish():
        wait("G", [(s, n) for s, n in cnt.items()])

    return op, dma, send, finish


def rank_program(g, core, T, topo):
    rank = T.rank_of(core)
    if rank is None:
        return
    N = len(T.cores)
    nxt, prv = T.cores[(rank + 1) % N], T.cores[(rank - 1) % N]
    op, dma, send, finish = machine(g, core, T, topo)
    V, S, TE = g.vector, g.scalar, g.tensor

    def ts(reads, writes, out, in0, s1, o0, s2=None, o1=None):
        if o1 is None:
            op("V", reads, writes, lambda: V.tensor_scalar(out, in0, s1, None, o0))
        else:
            op("V", reads, writes, lambda: V.tensor_scalar(out, in0, s1, s2, o0, o1))

    def tt(reads, writes, out, in0, in1, o):
        op("V", reads, writes, lambda: V.tensor_tensor(out, in0, in1, o))

    def cp(reads, writes, out, in_):
        op("V", reads, writes, lambda: V.tensor_copy(out, in_))

    def scan(reads, writes, out, d0, d1, init, o0, o1):
        op("V", reads, writes, lambda: V.tensor_tensor_scan(out, d0, d1, init, o0, o1))

    def act(reads, writes, out, in_, func=AF.Copy, **kw):
        op("S", reads, writes, lambda: S.activation(out, in_, func, **kw))

    def fill(writes, ap, c):
        op("V", [], writes, lambda: V.memset(ap, c))

    def iota(name, pattern, base, cm, floats=False):
        if floats:
            op("G", [], [name], lambda: g.iota(T[name][:], pattern, base, cm, allow_small_or_imprecise_dtypes=True))
        else:
            op("G", [], [name], lambda: g.iota(T[name][:], pattern, base, cm))

    def mm(out, lhsT, rhs, start=False, stop=False):
        return lambda: TE.matmul(out, lhsT, rhs, start, stop)

    def te(reads, bank, *fns):
        op("T", reads, [bank], *fns)

    dma("Y", "dP8", [(T.P8[:], T.pa[:])], [], ["P8"])
    dma("Y", "dW", [(T.WTI[:, 0:128], T.wt[:])], [], ["WTI"])
    dma("Y", "dX", [(T.X[:, 0:W], T.x[:])], [], ["X"])
    dma("Y", "dPB", [(T.PB2[:], T.pb[:])], [], ["PB2"])

    iota("PI", [[1, 2]], 0, 1)
    iota("CMI", [[0, 9], [1, 16]], 0, 0)
    iota("CGI", [[1, 8], [0, 16]], 0, 0)
    iota("CI", [[1, 128]], 0, 0)
    iota("CI8", [[1, 16], [0, 8]], 0, 0)
    fill(["NQE"], T.NQE[:], 0.0)
    p = T.PI[:, 0:1]
    cp(["PI"], ["PX0"], T.PX[:, 0:1], p)
    ts(["PI"], ["PX1"], T.PX[:, 1:2], p, 15, A.bitwise_and)
    ts(["PI"], ["PX2"], T.PX[:, 2:3], p, 4, A.logical_shift_right)
    ts(["PI"], ["PX3"], T.PX[:, 3:4], p, 7, A.bitwise_and)
    ts(["PI"], ["PX4"], T.PX[:, 4:5], p, 3, A.logical_shift_right, 1, A.bitwise_and)
    fill(["K2K"], T.K2K[:], 2048.0)
    cp(["PX%d" % k for k in range(5)], ["PF"], T.PF[:], T.PX[:])
    fill(["C0a"], T.C0[:, 0:128], 2048.0)
    fill(["KQ"], T.KQ[:, 128:192], 0.5)
    fill(["KM"], T.KM[:], MAGIC)
    P_, PM, PGc, PJ, PL = [T.PF[:, k:k + 1] for k in range(5)]
    ts(["CMI", "PF"], ["M16"], T.M16[:], T.CMI[:], PM, A.is_equal)
    ts(["CGI", "PF"], ["E8"], T.E8[:], T.CGI[0:8, :], T.PF[0:8, 0:1], A.is_equal)
    ts(["CI", "PF"], ["IDF"], T.IDF[:], T.CI[:], P_, A.is_equal)
    ts(["CGI", "PF"], ["BOB"], T.BOB[:], T.CGI[:], PGc, A.is_equal)
    for k, (src, a, b) in enumerate(((PGc, 2.0, 0.0), (PGc, 2.0, 1.0), (PJ, 32.0, 0.0), (PL, -1.0, 1.0))):
        ts(["PF"], ["PG%d" % k], T.PG[:, k:k + 1], src, a, A.mult, b, A.add)
    ts(["PF"], ["PG4"], T.PG[:, 4:5], PM, 15.0, A.is_lt, BIG, A.mult)
    ts(["P8"], ["LV8"], T.LV8[:], T.P8[:, 0:W:32], 0.0, A.is_ge)
    te(["E8", "LV8"], "p7", mm(T.p7[:, 0:128], T.E8[:], T.LV8[:], True, True))
    ts(["WTI"], ["WI0"], T.WTI[:, 128:256], T.WTI[:, 0:128], 2047.0, A.add)
    fill(["WSa"], T.WS[:, 0:1], 1.0 / W)
    fill(["WSb"], T.WS[:, 1:2], -1.0 / W)
    cp(["p7"], ["NH0"], T.NH0[:], T.p7[:, 0:128])
    send("L0", nxt, T.NL0[:], T.NH0[:], ["NH0"], "NL0")
    ts(["WI0"], ["WI1"], T.WTI[:, 256:384], T.WTI[:, 128:256], W - 1, A.bitwise_and)
    for k in range(6):
        ts(["BOB", "M16"], ["FT%d" % k], T.FT[:, 128 * k:128 * k + 128], T.BOB[:], T.M16[:, k:k + 1], A.mult)
        if k == 3:
            ts(["WI1"], ["WR"], T.WR[:], T.WTI[:, 256:384], -2047.0, A.add)
            te(["WR", "WSa", "WSb"], "p8", mm(T.p8[:, 0:2], T.WR[:], T.WS[:], True, True))
    iota("BJ0", [[256, 4]], 16, 0, True)
    iota("SLI", [[-16, 8], [-1, 8]], 0, 1)
    iota("SL9", [[-16, 8], [-1, 9]], 1, 1)
    iota("CEX", [[0, 8], [30000, 16]], -2048, 0, True)
    iota("CIW", [[1, 128]], W, 0, True)
    iota("ST0", [[32, 128]], 0, 0, True)
    for name, scale in (("IB", 1.0), ("NIB", -1.0), ("HI", 0.5), ("BIGI", BIG)):
        act(["IDF"], [name], T[name][:], T.IDF[:], scale=scale)
    act(["M16"], ["C0b"], T.C0[:, 128:256], T.M16[:, 0:128], scale=-4 * BIG, bias=4 * BIG + 2048)
    act(["M16"], ["CY"], T.CY[:], T.M16[:, 0:128], scale=LOW, bias=-LOW)
    act(["BOB"], ["BOBIG"], T.BOBIG[:], T.BOB[:], scale=BIG)

    def table(name, c, bank, on):
        src = T["P" + name[1] + "2H"]
        te(["P" + name[1] + "2H", "FT%d" % (2 * c), "FT%d" % (2 * c + 1)], bank, *[
            mm(T[bank][:, 256 * e:256 * e + 256], T.FT[:, 128 * (2 * c + e):128 * (2 * c + e + 1)], src[:], True, True)
            for e in range(2)])
        out = T[name][:, 512 * c:512 * c + 512]
        if on == "V later":
            return lambda: ts([bank], [name + str(c)], out, T[bank][:, 0:512], 2047.0, A.add)
        if on == "later":
            return lambda: act([bank], [name + str(c)], out, T[bank][:, 0:512], bias=2047.0)
        if on == "S":
            act([bank], [name + str(c)], out, T[bank][:, 0:512], bias=2047.0)
        else:
            ts([bank], [name + str(c)], out, T[bank][:, 0:512], 2047.0, A.add)

    def whole(name):
        return [name + str(c) for c in range(8)]

    ts(["BJ0", "PG2"], ["BJ"], T.BJ[:], T.BJ0[:], T.PG[:, 2:3], A.add)
    for k in range(4):
        ts(["CI8", "PG%d" % (k % 2), "p8"], ["WM%d" % k], T.WM[:, 128 * k:128 * k + 128], T.CI8[:],
           T.PG[:, k % 2:k % 2 + 1], A.is_equal, T.p8[:, k // 2:k // 2 + 1], A.mult)
    tt(["BJ"], ["BJ2"], T.BJ2[:], T.BJ[:], T.BJ[:], A.mult)
    cp(["NQE"], ["CFE"], T.CFE[:], T.NQE[:])
    for d in range(D):
        ts(["BJ2"], ["KB%d" % d], T.KB[:, 4 * d:4 * d + 4], T.BJ2[:], -1.0 / 32, A.mult, 97.0 * d - 0.4375, A.add)
    ts(["CI", "PF"], ["GMa"], T.GM[:, 0:8], T.CI[:, 0:8], PGc, A.is_equal, float(W), A.mult)
    ts(["CI", "PF"], ["GMb"], T.GM[:, 8:16], T.CI[:, 0:8], PGc, A.is_equal, -float(W), A.mult)

    def const(writes, ap, c, reads=()):
        act(["IDF"] + list(reads), writes, ap, T.IDF[:, 0:ap.shape[1]], scale=0.0, bias=c)

    const(["K9a"], T.K9[:], 2048.0)
    const(["KQa"], T.KQ[:, 0:128], -0.25)
    const(["PYc"], T.PY[:, 0:1], -1.0)
    const(["RSBc"], T.RSB[:], -5.0e7)
    const(["K9"], T.K9[:, 0:72:9], -2 * FULL, ["K9a"])
    te(["IDF", "CY", "CIW"], "p1", mm(T.p1[:, 0:128], T.IDF[:], T.CY[:], True, False),
       mm(T.p1[:, 0:128], T.IDF[:], T.CIW[:], False, True))
    for k in range(6, 16):
        act(["BOB", "M16"], ["FT%d" % k], T.FT[:, 128 * k:128 * k + 128], T.BOB[:], scale=T.M16[:, k:k + 1])
    act(["p1"], ["CPL"], T.CPL[:], T.p1[:, 0:128])
    act(["IDF", "PG3"], ["IL0"], T.IL[:, 0:128], T.IDF[:], scale=T.PG[:, 3:4])
    act(["IDF", "PF"], ["IL1"], T.IL[:, 128:256], T.IDF[:], scale=PL)

    def late_constants():
        for n in ("IOT", "FB", "X"):
            const([n + "spare"], T[n][:, W:WX], 0.0)
        const(["ONF"], T.ONF[:], 1.0 / 16)
        act(["M16"], ["CPA"], T.CP[:, 0:128], T.M16[:, 0:128], scale=4 * BIG)
        act(["M16"], ["CPB"], T.CP[:, 128:256], T.M16[:, 15:143], scale=-BIG)

    def later_constants():
        te(["IB", "CPA", "CPB"], "p4", mm(T.p4[:, 0:128], T.IB[:], T.CP[:, 0:128], True, False),
           mm(T.p4[:, 0:128], T.IB[:], T.CP[:, 128:256], False, True))
        const(["XR0spare"], T.XR0[:, W:WX], 0.0)
        act(["p4"], ["CPK"], T.CPK[:], T.p4[:, 0:128])

    def last_constants():
        act(["SL%d" % e for e in range(4)], ["NS"], T.NS[:], T.SL[:], scale=-FULL)
        for n in ("XR1", "FA"):
            const([n + "spare"], T[n][:, W:WX], 0.0)

    cp(["X"], ["SN0"], T.SN0[:], T.X[:, 0:W:32])
    send("S0", nxt, T.SS0[:], T.SN0[:], ["SN0"], "SS0")
    iota("ST1", [[32, 128]], 1, 0, True)
    for lo, hi in ((0, 512), (512, W)):
        op("G", [], ["IOT"], lambda: g.iota(T.IOT[:, lo:hi], [[1, hi - lo]], lo + 1, 0,
                                            allow_small_or_imprecise_dtypes=True))
        if lo == 0:
            send("X0", nxt, T.XR0[:, 0:W], T.X[:, 0:W], ["X"], "XR0", ["SN0"])
            dma("Y", "dPA", [(T.PA2[:], T.pa[:])], [], ["PA2", "SN0"])
    for e in range(4):
        src, c = ("SLI", slice(64 * e, 64 * e + 64)) if e < 2 else ("SL9", slice(72 * e - 16, 72 * e + 56))
        ts([src], ["SL%d" % e], T.SL[:, c], T[src][:], 8.0 * (e % 2), A.is_equal)
    fill(["ZSc"], T.ZS[:], 0)
    ts(["PB2"], ["PB2H"], T.PB2H[:], T.PB2[:], -2047.0, A.add)
    for c in range(3):
        table("FB", c, ("p2", "p3", "p4")[c], "SV"[c % 2])
    in_head = table("FB", 3, "p8", "later")

    zr_all = ["ZR%d" % m for m in range(8)]
    pieces = [("FB", c) for c in range(4, 8)] + [("FA", c) for c in range(8)]

    def piece(bank):
        if pieces:
            table(*pieces.pop(0), bank, "S")

    def near(name, e):
        c = T[name][:, min(e, 1):W:32]
        tt(whole(name) + ["IOT", "IOTspare", "N%d" % e], whole(name), c, T.IOT[:].indirect(T.NM[:, 8 * e:8 * e + 8]), c,
           A.add)

    for t in range(TB):
        far = "FB" if t == 0 else "FA"
        F = T[far]
        xr, ss, nl, st = "XR%d" % t, "SS%d" % t, "NL%d" % t, "ST%d" % t
        XR = T[xr]
        to = nxt if t == 0 else prv
        home = prv if t == 0 else nxt
        for d in range(D):
            first = t == 0 and d == 0
            zn, z0, zs = ("XR1", 1, 32) if (t, d) == (1, 0) else (ss if first else "Z", 0, 1)
            Z = T[zn]
            kn, KN = ("KB0", T.KB) if first else ("KC", T.KC)
            stopped = [nl] + ["SG%d" % e for e in range(d)]

            pu = T.p1[:, 0:64]

            def weighted(sign):
                return [mm(pu, T.WM[:, 128 * (2 * sign + e):128 * (2 * sign + e + 1)],
                           Z[:, z0 + zs * e:128 * zs:2 * zs], False, sign == 0 and e == 1) for e in range(2)]

            te(["IB", "KQ"], "p1", mm(pu, T.IB[:], T.KQ[:, 128:192], True, False))
            te(["IB", "NIB", "KM", zn] + ["WM%d" % k for k in range(4)], "p1", *(
                weighted(1) + [mm(pu, T.IB[:], T.KM[:, 0:64]), mm(pu, T.NIB[:], T.KM[:, 0:64])] + weighted(0)))
            for m in range(8):
                cp([zn], ["ZR%d" % m], T.ZR[:, m:1024:8], Z[:, z0:128 * zs:zs])
            if (t, d) == (1, 0):
                cp([zn], [ss], T[ss][:], Z[:, z0:128 * zs:zs])
            for b in range(4):
                act(["p1", "BJ"], ["SQ%d" % b], T.SQ[:, 64 * b:64 * b + 64], pu, AF.Square, scale=float(W),
                    bias=T.BJ[:, b:b + 1])
            if first:
                in_head()

            def whole_part(b):
                c = slice(64 * b, 64 * b + 64)
                ts(["SQ%d" % b, kn], ["AI%d" % b], T.AI[:, c], T.SQ[:, c], 1.0 / 32, A.mult, KN[:, b:b + 1], A.add)

            def modulo(lo, hi):
                ts(["AI%d" % b for b in range(lo, hi)], ["CC%d" % b for b in range(lo, hi)], T.CC[:, 64 * lo:64 * hi],
                   T.AI[:, 64 * lo:64 * hi], W - 1, A.bitwise_and)

            def offsets(lo, hi):
                cp(["CC%d" % b for b in range(lo, hi)], ["CU%d" % b for b in range(lo, hi)], T.CU[:, 64 * lo:64 * hi],
                   T.CC[:, 64 * lo:64 * hi])

            def keys(b, lo, hi, j):
                if b < 3:
                    return T.p4[lo:hi, 3 * j + b:192:24]
                return T.p5[lo:hi, j + 1:72:9]

            def kbank(b):
                return "p4" if b < 3 else "p5"

            def gather_v(b, lo, hi):
                tt(["X", "CU%d" % b] + zr_all, ["DD%d_%d" % (b, lo)], T.DD[:, 1024 * b + 8 * lo:1024 * b + 8 * hi],
                   T.X[:, 0:W].indirect(T.CU[:, 64 * b + lo // 2:64 * b + hi // 2]), T.ZR[:, 8 * lo:8 * hi], A.subtract)

            def relu_v(b, lo, hi):
                ts(["DD%d_%d" % (b, lo)], ["AB%d_%d" % (b, lo)], T.AB[:, 1024 * b + 8 * lo:1024 * b + 8 * hi],
                   T.DD[:, 1024 * b + 8 * lo:1024 * b + 8 * hi], 0.0, A.max, 2.0, A.mult)

            def minus_d(b, lo, hi):
                te(["DD%d_%d" % (b, lo), "GMb"], kbank(b), *[
                    mm(keys(b, lo, hi, j), T.DD[:, 1024 * b + 8 * lo + j:1024 * b + 8 * hi:8], T.GM[:, 8:16])
                    for j in range(8)])

            def plus_abs(b, lo, hi, parts, stop=False):
                te(["AB%d_%d" % (b, e) for e in parts] + ["GMa"], kbank(b), *[
                    mm(keys(b, lo, hi, j), T.AB[:, 1024 * b + 8 * lo + j:1024 * b + 8 * hi:8], T.GM[:, 0:8], False,
                       stop and j == 7) for j in range(8)])

            def minus_z(bank, lo, hi):
                te(["NIB"] + zr_all, bank, mm(T[bank][:, 0:8 * (hi - lo)], T.NIB[:], T.ZR[:, 8 * lo:8 * hi], True, False))

            def gs(b, lo, hi):
                return T.GS[:, 1024 * b + 8 * lo:1024 * b + 8 * hi]

            def gather_s(b, lo, hi):
                act(["X", "CU%d" % b], ["GS%d_%d" % (b, lo)], gs(b, lo, hi),
                    T.X[:, 0:W].indirect(T.CU[:, 64 * b + lo // 2:64 * b + hi // 2]))

            def plus_x(bank, b, lo, hi):
                te(["GS%d_%d" % (b, lo), "IB"], bank, mm(T[bank][:, 0:8 * (hi - lo)], T.IB[:], gs(b, lo, hi), False, True))

            def abs_s(bank, b, lo, hi):
                act([bank], ["AB%d_%d" % (b, lo)], T.AB[:, 1024 * b + 8 * lo:1024 * b + 8 * hi],
                    T[bank][:, 0:8 * (hi - lo)], AF.Abs)

            def spread(src, sel, names, b, stop=False):
                out, o, n = (T.p4[:, b:192:3], 0, 64) if b < 3 else (T.p5[:, 0:72], 128, 72)
                te(names, kbank(b), *[
                    mm(out, src[:, 2 - e + 128 * b:130 - e + 128 * b], sel[:, o + n * e:o + n * e + n], False,
                       stop and e == 1) for e in range(2)])

            def barred(b):
                if d > 0:
                    tt(["CC%d" % b, "p6"], ["NQE%d" % b], T.NQE[:, 2 + 128 * b:130 + 128 * b:2],
                       T.CC[:, 64 * b:64 * b + 64], T.p6[:, 0:64], A.not_equal)
                    spread(T.NQE, T.NS, ["NQE", "NQE%d" % b, "NS"], b)

            def places(b, stop):
                spread(T.CFE, T.SL, ["CFE"] + ["SL%d" % e for e in range(4)], b, stop)

            te(["IB", "K2K"], "p4", mm(T.p4[:, 0:192], T.IB[:], T.K2K[:], True, False))
            te(["IB", "K9"], "p5", mm(T.p5[:, 0:72], T.IB[:], T.K9[:], True, False))
            s0, s1, s2 = SPLIT[min(d, 1)]
            minus_z("p2", s0, 128)
            minus_z("p3", s1, 128)
            minus_z("p7", s2, 128)
            for b in range(4):
                whole_part(b)
            modulo(0, 1)
            modulo(1, 2)
            modulo(2, 4)
            offsets(0, 1)
            offsets(1, 2)
            barred(0)
            barred(1)
            offsets(2, 4)
            gather_s(0, s0, 128)
            gather_v(0, 0, s0)
            te(["IB", "C0b"], "p1", mm(T.p1[:, 0:128], T.IB[:], T.C0[:, 128:256], True, False))
            early = [table(*pieces.pop(0), bank, "later") for bank in (["p8", "p6"] if first else ["p8"]) if pieces]
            plus_x("p2", 0, s0, 128)
            gather_s(1, s1, 128)
            abs_s("p2", 0, s0, 128)
            minus_d(0, 0, s0)
            gather_v(1, 0, s1)
            relu_v(0, 0, s0)
            plus_x("p3", 1, s1, 128)
            gather_s(2, s2, 128)
            abs_s("p3", 1, s1, 128)
            minus_d(1, 0, s1)
            minus_z("p2", 64, 96)
            plus_abs(0, 0, 128, [0, s0])
            barred(2)
            ts(["CU%d" % b for b in range(4)], ["CFE"], T.CFE[:, 2:514:2], T.CU[:], -2048.0, A.add)
            gather_v(2, 0, s2)
            relu_v(1, 0, s1)
            places(0, False)
            plus_x("p7", 2, s2, 128)
            gather_s(3, 64, 96)
            minus_z("p3", 96, 128)
            gather_s(3, 96, 128)
            abs_s("p7", 2, s2, 128)
            minus_d(2, 0, s2)
            plus_abs(1, 0, 128, [0, s1])
            places(1, False)
            gather_v(3, 0, 32)
            relu_v(2, 0, s2)
            plus_x("p2", 3, 64, 96)
            abs_s("p2", 3, 64, 96)
            minus_d(3, 0, 32)
            plus_x("p3", 3, 96, 128)
            abs_s("p3", 3, 96, 128)
            for copy in early:
                copy()
            gather_v(3, 32, 64)
            relu_v(3, 0, 32)
            plus_abs(2, 0, 128, [0, s2])
            places(2, True)
            minus_d(3, 32, 64)
            barred(3)
            relu_v(3, 32, 64)
            if d == 0:
                places(3, False)
            plus_abs(3, 0, 128, [0, 32, 64, 96], d == 0)
            if d > 0:
                places(3, True)
            for e in range(8):
                op("V", ["p4", "RSBc"], ["RSB%d" % e], lambda: V.tensor_reduce(
                    T.RSB[:, 9 * e + 1:9 * e + 2], T.p4[:, 24 * e:24 * e + 24], AxisListType.X, A.min))
            te(stopped + ["IB", "C0b", "BIGI"], "p7", mm(T.p7[:, 0:128], T.IB[:], T.C0[:, 128:256], True, False),
               *[mm(T.p7[:, 0:128], T.BIGI[:], T[n][:]) for n in stopped])
            te(stopped + ["BIGI"], "p1", *[mm(T.p1[:, 0:128], T.BIGI[:], T[n][:]) for n in stopped])
            if first:
                on_vector = table(*pieces.pop(0), "p4", "V later")
            piece("p3")
            te(["IB", "C0a"], "p6", mm(T.p6[:, 0:128], T.IB[:], T.C0[:, 0:128], True, False))

            scan(["p5", "RSBc"] + ["RSB%d" % e for e in range(8)], ["RB"], T.RB[:], T.RSB[:], T.p5[:, 0:72], 0.0, A.max, A.min)
            ts(["RB", "ZSc"], ["ZS"], T.ZS[:, 0:128:16], T.RB[:, 8:72:9], W - 1, A.bitwise_and)
            scan(["ZS", "ZSc", "CEX"], ["YE"], T.YE[:], T.CEX[:], T.ZS[:], 0.0, A.min, A.add)
            if first:
                on_vector()
            if (t, d) == (1, 0):
                near("FA", 0)
            if (t, d) == (1, 2):
                near("FB", 1)
            for bank, stop in (("p7", True), ("p6", True), ("p1", False)):
                te(["YE", "IB"], bank, mm(T[bank][:, 0:128], T.YE[:], T.IB[:], False, stop))
            te(["IB", "KQa", "HI", ss], "p2", mm(T.p2[:, 0:128], T.IB[:], T.KQ[:, 0:128], True, False),
               mm(T.p2[:, 0:128], T.HI[:], T[ss][:]))
            scan(["p7", "CPL", "PYc"], ["PY"], T.PY[:, 1:129], T.CPL[:], T.p7[:, 0:128], -1.0, A.max, A.min)
            ts(["p6"], ["YR"], T.YR[:], T.p6[:, 0:128], -2048.0, A.add)
            ts(["PY"], ["YU"], T.YU[:], T.PY[:, 16:129:16], W - 1.0, A.min)
            act(whole(far) + ["YU"], ["TK"], T.TK[:], F[:, 0:W].indirect(T.YU[:]), AF.Relu, bias=1.0)
            if first:
                late_constants()
            tt(["p6", "PY", "PYc"], ["EQ7"], T.EQ[:, 896:1024], T.p6[:, 0:128], T.PY[:, 0:128], A.is_equal)
            te(["EQ7", "BOBIG"], "p1", mm(T.p1[:, 0:128], T.BOBIG[:], T.EQ[:, 896:1024]))
            for h in range(7):
                lo = 16 * h + 17
                e = T.EQ[:, 128 * h + lo:128 * h + 128]
                ts(["YR", "PY"], ["EQ%d" % h], e, T.YR[:, lo:128], 2048.0, A.add, T.PY[:, 16 * h + 16:16 * h + 17],
                   A.is_equal)
                te(["EQ%d" % h, "BOBIG"], "p1", mm(T.p1[:, lo:128], T.BOBIG[:], e))
            cp(["X", "YU"], ["XG"], T.XG[:], T.X[:, 0:W].indirect(T.YU[:]))
            if first:
                ts(["PA2"], ["PA2H"], T.PA2H[:], T.PA2[:], -2047.0, A.add)
            te(["TK", "BIGI"], "p1", mm(T.p1[:, 0:128], T.BIGI[:], T.TK[:], False, True))
            te(["XG", "HI", "IB", "KM"], "p2", mm(T.p2[:, 0:128], T.HI[:], T.XG[:]),
               mm(T.p2[:, 0:128], T.IB[:], T.KM[:], False, True))
            scan(["p1", "CPL"], ["PP"], T.PP[:], T.CPL[:], T.p1[:, 0:128], -1.0, A.max, A.min)
            ts(["p2"], ["NR"], T.MU[:, 0:128], T.p2[:, 0:128], -MAGIC, A.add)
            k = D * t + d
            mp, sg = "ML", "SG%d" % d
            sl = T.MU[:, 128:136]
            cp(["PP"], [mp], sl, T.PP[:, 15:128:16])

            def far_write():
                cp([mp, st, far + "spare"], whole(far), F[:, 0:WX].indirect(sl), T[st][:])

            def rec_write():
                cp([mp, "NR", "Xspare"], ["X"], T.X[:, 0:WX].indirect(sl), T.MU[:, 0:128])

            def winners():
                act(["IOT", "IOTspare", mp], [sg, "CT"], T[sg][:], T.IOT[:].indirect(sl), AF.Sign, accum_out=T.CT[:])
                te(["CT", "ONF"], "p5", mm(T.p5[:, 0:1], T.ONF[:], T.CT[:], True, True))

            def update(k, dst):
                send("U%d" % k, dst, T.UL[:, 136 * k:136 * k + 136], T.MU[:], ["NR", mp], "UL%d" % k)
                return T.UL[:, 136 * k:136 * k + 128], T.UL[:, 136 * k + 128:136 * k + 136]

            def paired():
                if d == 0:
                    cp(["PP"], ["PM"], T.PM[:], T.PP[:, 15:128:16])
                else:
                    tt(["PP", "PM"], ["PM"], T.PM[:], T.PP[:, 15:128:16], T.PM[:], A.min)

            def pairings(e):
                c = slice(8 * e, 8 * e + 8)
                cp(["PM"], ["MP%d" % e], T.MP[:, c], T.PM[:])
                send("N%d" % e, home, T.NM[:, c], T.MP[:, c], ["MP%d" % e], "N%d" % e)

            def kappa(step):
                if step == 0:
                    cp(["p5"], ["KJ0"], T.KJ[:, 0:1], T.p5[:, 0:1])
                elif step == 1:
                    ts(["KJ0"], ["KJ1"], T.KJ[:, 1:2], T.KJ[:, 0:1], 31, A.bitwise_and)
                else:
                    cp(["KJ1"], ["KF"], T.KF[:], T.KJ[:, 1:2])
                    e = (d + 1) % D
                    act(["KF", "KB%d" % e], ["KC"], T.KC[:], T.KB[:, 4 * e:4 * e + 4], AF.Identity, bias=T.KF[:])

            if d < D - 1:
                ur, up = update(k, to)
                te(["YR", "IL0", "IL1", "IB", "K2K"], "p6", mm(T.p6[:, 0:64], T.IB[:], T.K2K[:, 0:64], True, False), *[
                    mm(T.p6[:, 0:64], T.IL[:, 128 * e:128 * e + 128], T.YR[:, e:128:2], False, e == 1) for e in range(2)])
                if first:
                    later_constants()
                winners()
                far_write()
                act(whole(far) + ["YU"], ["PGR"], T.PGR[:], F[:, 0:W].indirect(T.YU[:]))
                if first:
                    last_constants()
                rec_write()
                if k == 1:
                    send("X1", prv, T.XR1[:, 0:W], T.X[:, 0:W], ["X"], "XR1", ["NR"])
                scan(["PGR", "CPK"], ["PS"], T.PS[:], T.CPK[:], T.PGR[:], -BIG, A.add, A.min)
                kappa(0)
                paired()
                piece("p7")
                piece("p3")
                cp(["UL%d" % k, xr + "spare"], [xr], XR[:, 0:WX].indirect(up), ur)
                ts(["PS", "PG4"], ["PU"], T.PU[:], T.PS[:, 15:128:16], T.PG[:, 4:5], A.add)
                kappa(1)
                if k == 4:
                    pairings(1)
                cp([xr, "PU"], ["Z"], T.Z[:], XR[:, 0:W].indirect(T.PU[:]))
                kappa(2)
            elif t == 0:
                ur, up = update(k, prv)
                winners()
                far_write()
                paired()
                rec_write()
                kappa(0)
                pairings(0)
                ts(whole("FB"), ["NH1"], T.NH1[:], T.FB[:, 1:W:32], 0.0, A.is_ge)
                kappa(1)
                send("L1", prv, T.NL1[:], T.NH1[:], ["NH1"], "NL1")
                kappa(2)
                cp(["UL%d" % k, "XR1spare"], ["XR1"], T.XR1[:, 0:WX].indirect(up), ur)
            else:
                send("N2", home, T.NM[:, 16:24], sl, [mp], "N2")
                rec_write()
                dma("Y", "oX", [(T.yx[:], T.X[:, 0:W])], ["X"], ["yx"])
                far_write()
                dma("Y", "oA", [(T.ya[:], T.FA[0:128:16, 0:W])], whole("FA"), ["ya"])

    near("FB", 2)
    dma("Y", "oB", [(T.yb[:], T.FB[0:128:16, 0:W])], whole("FB"), ["yb"])
    finish()
